import numpy as np, ml_dtypes
CORES = [6,15,38,47]
N = 4
BF = ml_dtypes.bfloat16
def gentries(a):
    return np.ascontiguousarray(a.reshape(8, 16, -1).transpose(0, 2, 1)).reshape(8, -1)
def gtable(e):
    e = np.asarray(e); return np.ascontiguousarray(e.reshape(8, -1, 16).transpose(0, 2, 1)).reshape(128, -1).astype(np.int32)
P, L, S, F, RO = 4096, 4096, 4, 256, 2
H = P - F
def depths(rng, up, top):
    s = np.where(rng.random((N, 8, P)) < up, 1, 1 - rng.geometric(0.5, (N, 8, P))); d = np.zeros((N, 8, P), np.int64); now = np.zeros((N, 8), np.int64)
    for v in range(1, P):
        now = np.minimum(np.maximum(now + s[:, :, v], 0), top); d[:, :, v] = now
    return d
def closed(d):
    e = np.zeros(d.shape, np.int64); last = np.full(d.shape[:-1] + (1,), P, np.int64)
    for k in range(int(np.max(d)) + 1):
        m = np.minimum.accumulate(np.where(d <= k, np.arange(P), P)[..., ::-1], axis=-1)[..., ::-1]
        e = np.where(d == k, np.concatenate([m[..., 1:], last], axis=-1), e)
    return e
def parts(rng):
    up = rng.choice(np.array([0.4, 0.5, 0.6]), (N, 8, 1)); top = rng.integers(3, 13, (N, 8))
    full = np.arange(P) < (P * rng.choice(np.array([8, 12, 14, 16]), (N, 8, 1))) // 16
    d = np.where(full, depths(rng, up, top), 0)
    x = np.where(rng.random((N, 8, 16, P)) < 0.25, rng.integers(0, 4, (N, 8, 16, P)), rng.integers(0, 256, (N, 8, 16, P))) * full[:, :, None, :]
    return x, d, rng.integers(0, 256, (N, 8, 16, L)), rng.integers(0, P, (N, 8, RO, L))
def pack(x, e, w, st):
    return {"x": np.ascontiguousarray(x.reshape(N, 128, P)).astype(np.float32).astype(BF), "w": np.ascontiguousarray(w.reshape(N, 128, L)).astype(np.float32).astype(BF),
            "ends": np.ascontiguousarray(e).astype(np.int32), "start": np.stack([gtable(a.reshape(8, -1)) for a in st])}
def setup_inputs(rng):
    x, d, w, st = parts(rng)
    return pack(x, closed(d), w, st)
def setup_inputs_room(rng):
    x, d, w, st = parts(rng); x = rng.integers(0, 256, x.shape); Q = P // 16; z = F // 4
    at = ((H - z, H), (H - z + 1, H + 1), (H, H + z), (H - 1, H - 1 + z), (P - z, P), (P - z + 1, P + 1), (P - 1, P - 1 + z), (H - z, -1))
    for q in range(N):
        for g in range(8):
            n = int(rng.integers(Q // 2, Q + 1)); a, b = at[(g + q) % 8]; a = a - n; b = P if b < 0 else b - n; D = d[q, g].copy()
            d[q, g] = np.concatenate([np.tile(np.arange(3), Q), D[:a - 3 * Q], np.zeros(1, np.int64), 1 + D[:b - a - 1], D[:P - b]])
            hot = 3 * rng.permutation(Q)[:n]
            st[q, g, 0] = rng.permutation(np.concatenate([hot, rng.choice(hot, L - n)]))
    return pack(x, closed(d), w, st)
def setup_inputs_ties(rng):
    x, d, w, st = parts(rng); lo = rng.choice(np.array([0, 100, 252]), (N, 8, 1, 1))
    x = lo + rng.integers(0, 4, x.shape); x[:, 1::2] = (lo + 2 * rng.integers(0, 2, (N, 8, 1, P)))[:, 1::2]
    return pack(x, closed(d), np.minimum(lo + rng.integers(0, 5, w.shape), 255), st)
def setup_inputs_alike(rng):
    x, d, w, st = parts(rng); x = rng.integers(0, 256, x.shape); e = closed(d); at = np.arange(P)
    names = rng.integers(0, P, (N, 8, RO, 6)); names[..., 0] = 0; names[..., 1] = P - 1
    st = np.take_along_axis(names, rng.integers(0, 6, st.shape), 3)
    for q in range(N):
        g = (np.arange(4) + q) % 8
        e[q, g[0]] = P; st[q, g[0], 0] = rng.choice(np.array([0, P - 1, P - 2, P - 3, P - 1 - S, P - 2 - S]), L)
        e[q, g[1]] = at + 1; e[q, g[1], :2] = P; st[q, g[1], 0] = 0
        e[q, g[2]] = at + 1
        e[q, g[3]] = np.where(at % 2 == 0, P, at + 1); st[q, g[3], 0] = rng.integers(0, P, L)
    return pack(x, e, w, st)
def setup_inputs_far(rng):
    x, d, w, st = parts(rng); x = rng.integers(0, 256, x.shape); w = rng.integers(1, 256, w.shape); g = rng.permutation(8); odd = np.arange(N) % 2 == 1; i4 = np.arange(16)[:, None] % 4
    kid = np.where(odd, rng.integers(3 * P // 4 + 2, P - 1, N), P - 1); low = np.where(odd, rng.integers(3 * P // 4, H, N), P - 1)
    left = np.where(odd, rng.integers(15 * P // 32, P // 2 - 4, N), rng.integers(7 * P // 16 + 1, 15 * P // 32, N)); T = min(P // 7, L // 4)
    st[:, g[:4]] = P - 1
    for q in range(N):
        D = d[q].copy(); b = int(kid[q]); z = int(low[q]); s = int(left[q]); m = D[g[0]]
        d[q, g[0]] = np.concatenate([np.array([0, 1, 2, 3]), 3 + m[:b - 4], np.array([2]), m[:P - b - 1]])
        x[q, g[0], :, b] = 0; st[q, g[0], 0] = 0
        d[q, g[1]] = np.concatenate([np.zeros(z + 1, np.int64), D[g[1]][:P - z - 1]])
        v = rng.choice(np.array([0, z - 2]), L); v[0] = 0; v[1] = z - 2; st[q, g[1], 0] = v
        m = D[g[2]]; d[q, g[2]] = np.concatenate([np.arange(3), 2 + m[:s - 1], m[:P - s - 2]]); st[q, g[2], 0] = 0
        m = D[g[3]]; a = H - 4 + q % 2
        d[q, g[3]] = np.concatenate([m[:H - 4], np.array([0, 0, 1, 2, 3]) if q % 2 else np.array([0, 1, 2, 3, 3]), m[:P - H - 1]])
        v = np.where(rng.random(L) < 0.5, a, rng.integers(H, P, L)); v[0] = a; st[q, g[3], 1] = v
        d[q, g[4]] = np.concatenate([np.tile(np.array([0, 1, 2, 2, 1, 2, 2]), T), D[g[4]][:P - 7 * T]])
        few = np.array([4, 0, 2, 3, 1, 2, 3])[np.arange(P) % 7]
        x[q, g[4]] = np.where(i4 == few, rng.integers(0, 61, (16, P)), rng.integers(200, 256, (16, P)))
        j = rng.permutation(np.concatenate([np.arange(4 * T), rng.integers(0, 4 * T, L - 4 * T)])); st[q, g[4], 0] = 7 * (j // 4)
        w[q, g[4]] = np.where((i4 == (j % 4) // 2) | (i4 == 2 + j % 2), rng.integers(100, 201, (16, L)), 0)
    x[:, g[0], :, 2] = 255; x[:, g[0], :, 3] = 0; x[:, g[0], :, 4] = 255; x[:, g[3], :, H - 1] = 255; x[:, g[3], :, H] = 0
    for k in (1, 2):
        x[:, g[k], :, 2] = 0; x[:, g[k], :, 3] = 255
    e = closed(d)
    for q in range(N):
        z = int(low[q]); e[q, g[1], :z + 1] = z + 1; e[q, g[1], 2] = 3
    return pack(x, e, w, st)
def setup_inputs_spread(rng):
    x, d, w, st = parts(rng)
    d = depths(rng, 0.35 + 0.35 * rng.random((N, 8, 1)), np.exp2(1 + 5 * rng.random((N, 8))).astype(np.int64) + 1)
    x = np.minimum((np.exp2(8 * rng.random((N, 8, 1, P))) * rng.random((N, 8, 16, P))).astype(np.int64), 255)
    w = np.minimum((np.exp2(8 * rng.random((N, 8, 1, L))) * rng.random((N, 8, 16, L))).astype(np.int64), 255)
    st = np.minimum((P * rng.random((N, 8, RO, L)) ** rng.choice(np.array([1, 2, 4]), (N, 8, 1, 1))).astype(np.int64), P - 1)
    return pack(x, closed(d), w, st)
def check_inputs(d):
    bad = []
    for k in ("x", "w"):
        v = d[k].astype(np.float32)
        if not np.all((v >= 0) & (v <= 255) & (v == np.floor(v))): bad.append("whole numbers from 0 to 255 in " + k)
    e = d["ends"].astype(np.int64); n = e - np.arange(P)
    if np.min(n) < 1 or np.max(e) > P: bad.append("range of ends")
    else:
        big = e; most = np.zeros(e.shape, np.int64); k = 1
        while k <= P:
            sel = (n >= k) & (n < 2 * k)
            most = np.where(sel, np.maximum(big, np.take_along_axis(big, np.where(sel, e - k, 0), 2)), most)
            big = np.concatenate([np.maximum(big[..., :P - k], big[..., k:]), big[..., P - k:]], axis=2); k = 2 * k
        if np.any(most > e): bad.append("runs that cross")
    if np.min(d["start"]) < 0 or np.max(d["start"]) > P - 1: bad.append("range of start")
    return bad
def grow(x, e, w, v):
    G = np.arange(8)[:, None]; at = np.arange(P); n = np.zeros((8, L), np.int64); par = v
    for i in range(S):
        ev = e[G, v]; a = np.minimum(v + 1, P - 1); b = e[G, a]; kids = ev > v + 1; two = kids & (b < ev); b = np.minimum(b, P - 1)
        ra = np.add.reduce(np.maximum(w - x[G, a], 0), axis=2); rb = np.add.reduce(np.maximum(w - x[G, b], 0), axis=2)
        par = np.where(kids, v, par); n = n + kids; v = np.where(kids, np.where(two & (rb > ra), b, a), v)
    hit = (n >= 2) & (e[G, v] == v + 1); gi = np.broadcast_to(G, v.shape)[hit]
    head = np.zeros((8, P), bool); head[gi, v[hit]] = True; mark = np.zeros((8, P), bool); mark[gi, par[hit]] = True
    zero = np.zeros((8, 1), np.int64); reach = np.maximum.accumulate(np.where(mark, e, 0), axis=1)
    top = mark & (np.concatenate([zero, reach[:, :-1]], axis=1) <= at); inside = reach > at; keep = ~head
    first = np.maximum.accumulate(np.where(top, at, 0), axis=1)
    K = np.concatenate([zero, np.add.accumulate(keep.astype(np.int64), axis=1)], axis=1)
    M = np.concatenate([zero, np.add.accumulate(keep * (1 + 2 * inside), axis=1)], axis=1)
    size = np.where(inside, K[G, e] - K[:, :P], M[G, e] - M[:, :P]); s = K[G, e[G, first]] - K[G, first]
    nx = np.zeros((8, P, 16), np.int64); ne = np.zeros((8, P), np.int64) + at + 1
    for c in range(3):
        q = np.where(inside, M[G, first] + c * s + K[:, :P] - K[G, first], M[:, :P])
        gk, vk = np.nonzero(keep & (inside | (c == 0)) & (q < P)); qk = q[gk, vk]
        nx[gk, qk] = np.maximum(x[gk, vk] - c, 0); ne[gk, qk] = qk + size[gk, vk]
    return nx, ne
def reference(x, w, ends, start):
    X = np.ascontiguousarray(x.astype(np.float32).astype(np.int64).reshape(N, 8, 16, P).transpose(0, 1, 3, 2)); E = ends.astype(np.int64)
    W = np.ascontiguousarray(w.astype(np.float32).astype(np.int64).reshape(N, 8, 16, L).transpose(0, 1, 3, 2))
    st = np.stack([gentries(a) for a in start]).astype(np.int64).reshape(N, 8, RO, L)
    for t in range(RO):
        both = [grow(X[r], E[r], W[r], st[r, :, t]) for r in range(N)]
        gx = np.stack([a for a, b in both]); ge = np.stack([b for a, b in both])
        X = np.concatenate([gx[:, :, :H], np.roll(gx[:, :, H:], 1, axis=0)], axis=2)
        E = np.concatenate([np.minimum(ge[:, :, :H], H), np.roll(np.minimum(ge[:, :, H:], P), 1, axis=0)], axis=2)
    return {"y": np.ascontiguousarray(X.transpose(0, 1, 3, 2)).reshape(N, 128, P).astype(np.float32).astype(BF), "ye": E.astype(np.float32)}

@@ -1,0 +1,586 @@
+from concourse.mybir import dt, AluOpType, AxisListType, ActivationFunctionType
+
+OP = AluOpType
+AF = ActivationFunctionType
+F32, BF, I32, U16 = "float32", "bfloat16", "int32", "uint16"
+NDMA = 110
+SCRATCH = {
+    "XW0": ("sbuf", [128, 12304], BF), "XW1": ("sbuf", [128, 12304], BF),
+    "XB": ("sbuf", [128, 4096], BF), "W": ("sbuf", [128, 4096], BF), "KT": ("sbuf", [128, 4096], BF),
+    "WB": ("sbuf", [128, 16416], BF), "WF": ("sbuf", [128, 16384], F32),
+    "VT0": ("sbuf", [128, 4096], BF), "VT2": ("sbuf", [128, 4096], BF), "ST1": ("sbuf", [128, 4096], F32),
+    "ST2": ("sbuf", [128, 1024], F32),
+    "ZB": ("sbuf", [128, 264], BF), "CR": ("sbuf", [128, 132], BF),
+    "IDF": ("sbuf", [128, 128], F32), "SHU": ("sbuf", [128, 128], F32),
+    "SHD": ("sbuf", [128, 128], F32), "TRI": ("sbuf", [128, 128], F32), "DF": ("sbuf", [128, 64], F32),
+    "MROW": ("sbuf", [128, 128], F32), "ONE": ("sbuf", [128, 2], F32), "PI": ("sbuf", [128, 8], I32),
+    "PC": ("sbuf", [128, 16], F32), "SEL": ("sbuf", [128, 128], BF),
+    "AT1": ("sbuf", [128, 256], F32), "ATK": ("sbuf", [128, 256], F32), "QT": ("sbuf", [128, 256], F32),
+    "EB": ("sbuf", [128, 258], F32),
+    "NHB": ("sbuf", [128, 256], BF), "DHI": ("sbuf", [128, 256], BF), "DLO": ("sbuf", [128, 256], BF),
+    "HMB": ("sbuf", [128, 256], BF), "HM": ("sbuf", [128, 528], BF),
+    "BLB": ("sbuf", [128, 256], U16), "ELB": ("sbuf", [128, 256], U16), "BLW": ("sbuf", [128, 256], U16),
+    "VL": ("sbuf", [128, 256], U16), "QL0": ("sbuf", [128, 256], U16), "QL1": ("sbuf", [128, 256], U16),
+    "QL2": ("sbuf", [128, 256], U16),
+    "TA": ("sbuf", [128, 256], F32), "TB": ("sbuf", [128, 256], F32), "TC": ("sbuf", [128, 256], F32),
+    "TD": ("sbuf", [128, 256], F32), "TE": ("sbuf", [128, 256], F32),
+    "VI": ("sbuf", [128, 256], I32), "HI": ("sbuf", [128, 256], I32),
+    "S1": ("sbuf", [128, 256], BF), "S2": ("sbuf", [128, 256], BF), "FL": ("sbuf", [64, 528], BF),
+    "HB": ("sbuf", [128, 256], BF), "HB1": ("sbuf", [128, 256], BF),
+    "KEEP": ("sbuf", [128, 256], BF), "KEX": ("sbuf", [128, 256], F32), "R": ("sbuf", [128, 256], F32),
+    "INS": ("sbuf", [128, 256], BF), "KI": ("sbuf", [128, 256], BF), "IEX": ("sbuf", [128, 256], F32),
+    "IH": ("sbuf", [128, 256], F32), "TOP": ("sbuf", [128, 256], BF),
+    "PHI": ("sbuf", [128, 256], BF), "PLO": ("sbuf", [128, 256], BF),
+    "CROW": ("sbuf", [128, 128], F32), "TX": ("sbuf", [128, 256], BF),
+    "LX0": ("sbuf", [128, 256], BF), "LX1": ("sbuf", [128, 256], BF),
+    "ES0": ("sbuf", [128, 16], F32), "ES1": ("sbuf", [128, 16], F32),
+    "RE0": ("sbuf", [128, 16], F32), "RE1": ("sbuf", [128, 16], F32),
+}
+for _k in range(8):
+    SCRATCH["P%d" % _k] = ("psum", [128, 512], F32)
+SEMAPHORES = ["qv", "qs", "qt", "qg"] + ["d%d" % k for k in range(NDMA)]
+SEMAPHORES += ["%s%d" % (a, k) for a in ("xs", "xr", "es", "er") for k in range(2)]
+
+ALIAS = {"SC": (4096, 528, 65), "D1": (4640, 528, 65), "HIT": (5200, 256, 128), "KEY": (5456, 256, 128),
+         "Q0M": (5712, 256, 128)}
+S_P, S_M, S_A, S_D, S_N, S_B, S_0, S_01, S_K, S_I = 0, 8, 16, 24, 32, 40, 48, 56, 64, 72
+BIG = float(2 ** 24)
+KM, GB = 4112, 8208
+
+
+def rank_program(g, core, T, topo):
+    rank = T.rank_of(core)
+    if rank is None:
+        return
+    n = len(T.cores)
+    nxt, prv = T.cores[(rank + 1) % n], T.cores[(rank - 1) % n]
+    eng = {"v": g.vector, "s": g.scalar, "t": g.tensor, "g": g, "y": g.sync}
+    hist, known, cnt, total = {}, {q: {} for q in eng}, {q: 0 for q in eng}, {}
+    nd, serial = [0], [0]
+
+    def over(a, b):
+        if a[0] >= b[1] or b[0] >= a[1] or a[3] >= b[4] or b[3] >= a[4]:
+            return False
+        return not (a[2] == 16 and b[2] == 16 and a[0] % 16 != b[0] % 16)
+
+    def inside(a, b):
+        if not (b[0] <= a[0] and a[1] <= b[1] and b[3] <= a[3] and a[4] <= b[4]):
+            return False
+        return b[2] == 1 or (a[2] == 16 and a[0] % 16 == b[0] % 16)
+
+    def is_psum(name):
+        return name[0] == "P" and name[1:].isdigit()
+
+    def op(q, call, R, W, dma=False, remote=None):
+        deps = []
+        for name, reg in R:
+            ps = is_psum(name)
+            for r in hist.get(name, []):
+                if over(r["reg"], reg) and (r["w"] or (ps and r["q"] != q)):
+                    deps.append(r)
+        for name, reg in W:
+            for r in hist.get(name, []):
+                if over(r["reg"], reg) and not (q == "t" and r["q"] == "t"):
+                    deps.append(r)
+        deps.sort(key=lambda r: -r["n"])
+        kn = known[q]
+        for r in deps:
+            if kn.get(r["sem"], 0) >= r["val"]:
+                continue
+            eng[q].wait_ge(T.sem[r["sem"]], r["val"])
+            for k, v in r["vc"].items():
+                if kn.get(k, 0) < v:
+                    kn[k] = v
+            kn[r["sem"]] = r["val"]
+        ins = call()
+        serial[0] += 1
+        if remote is not None:
+            sem, val = remote
+        elif dma:
+            sem, val = "d%d" % nd[0], 16
+            nd[0] += 1
+            ins.then_inc(T.sem[sem], 16)
+        else:
+            cnt[q] += 1
+            sem, val = "q" + q, cnt[q]
+            ins.then_inc(T.sem[sem], 1)
+        total[sem] = val
+        vc = dict(kn)
+        for w, lst in ((False, R), (True, W)):
+            for name, reg in lst:
+                h = hist.setdefault(name, [])
+                if w or is_psum(name):
+                    h[:] = [r for r in h if not inside(r["reg"], reg)]
+                elif not dma and remote is None:
+                    h[:] = [r for r in h if r["w"] or r["dma"] or r["q"] != q or not inside(r["reg"], reg)]
+                h.append({"reg": reg, "w": w, "q": q, "sem": sem, "val": val, "vc": vc, "n": serial[0],
+                          "dma": dma or remote is not None})
+
+    def A(name, c0=0, c1=None, cs=1, p0=0, p1=None, ps=1):
+        if name in ALIAS:
+            o, k, r = ALIAS[name]
+            return A("WF", o + c0, o + (k if c1 is None else c1), cs, p0, r if p1 is None else p1, ps)
+        shape = T[name].shape
+        c1 = shape[1] if c1 is None else c1
+        p1 = shape[0] if p1 is None else p1
+        sc = slice(c0, c1) if cs == 1 else slice(c0, c1, cs)
+        sp = slice(p0, p1) if ps == 1 else slice(p0, p1, ps)
+        reg = (0, 128, 1, 0, 512) if is_psum(name) else (p0, p1, ps, c0, c1)
+        return T[name][sp, sc], [(name, reg)]
+
+    def IND(name, c0, c1, lst, l0, l1):
+        return (T[name][:, c0:c1].indirect(T[lst][:, l0:l1]),
+                [(name, (0, 128, 1, c0, c1)), (lst, (0, 128, 1, l0, l1))])
+
+    def outs(o):
+        return o[1][:1], o[1][1:]
+
+    def tt(o, a, b, f):
+        op("v", lambda: g.vector.tensor_tensor(o[0], a[0], b[0], f), a[1] + b[1], o[1])
+
+    def ts(o, a, s1, s2, f1, f2=None):
+        r = list(a[1])
+        x = [s1, s2]
+        for k in range(2):
+            if isinstance(x[k], tuple):
+                r += x[k][1]
+                x[k] = x[k][0]
+        if f2 is None:
+            op("v", lambda: g.vector.tensor_scalar(o[0], a[0], x[0], None, f1), r, o[1])
+        else:
+            op("v", lambda: g.vector.tensor_scalar(o[0], a[0], x[0], x[1], f1, f2), r, o[1])
+
+    def cp(o, a):
+        w, r = outs(o)
+        op("v", lambda: g.vector.tensor_copy(o[0], a[0]), a[1] + r, w)
+
+    def fill(o, val):
+        op("v", lambda: g.vector.memset(o[0], val), [], o[1])
+
+    def scan(o, a, b, f1, f2):
+        op("v", lambda: g.vector.tensor_tensor_scan(o[0], a[0], b[0], 0.0, f1, f2), a[1] + b[1], o[1])
+
+    def act(o, a, f=AF.Copy, bias=None, scale=1.0):
+        w, r = outs(o)
+        if bias is None:
+            op("s", lambda: g.scalar.activation(o[0], a[0], f), a[1] + r, w)
+        else:
+            op("s", lambda: g.scalar.activation(o[0], a[0], f, bias=bias[0], scale=scale), a[1] + r + bias[1], w)
+
+    def mm(o, l, r, start=True, stop=True):
+        op("t", lambda: g.tensor.matmul(o[0], l[0], r[0], start, stop), l[1] + r[1], o[1])
+
+    def dma(o, a, q="y"):
+        op(q, lambda: eng[q].dma_start(o[0], a[0]), a[1], o[1], dma=True)
+
+    def iota(o, pattern, base, mul, loose=True):
+        if loose:
+            op("g", lambda: g.iota(o[0], pattern, base, mul, allow_small_or_imprecise_dtypes=True), [], o[1])
+        else:
+            op("g", lambda: g.iota(o[0], pattern, base, mul), [], o[1])
+
+    def IO(name, *idx):
+        return (T[name][idx] if idx else T[name][:]), []
+
+    def sel(c, k=8):
+        return A("SEL", c, c + k)
+
+    def tr(o, a):
+        mm(o, a, A("IDF"))
+
+    def rows(name, off, r, src, q="y"):
+        dma(A(name, off, off + 4096, 1, r, 128, 16), src, q)
+
+    dma(A("VI"), IO("ends"), "y")
+    dma(A("HI"), IO("start", slice(0, 128), slice(0, 256)), "s")
+    fill(A("XW0", 0, 16), 0.0)
+    fill(A("XW0", 4104, 4112), 0.0)
+    dma(A("XW0", 15, 4111), IO("x"), "y")
+    dma(A("W"), IO("w"), "s")
+
+    def pick(o, pattern, f, v, base, mul):
+        op("g", lambda: g.affine_select(o[0], o[0], pattern, f, v, base, mul), o[1], o[1])
+
+    def selector(c, lo, hi):
+        pick(sel(c), [[-16, 8]], OP.is_ge, 0.0, -lo, 1)
+        pick(sel(c), [[16, 8]], OP.is_ge, 0.0, hi, -1)
+
+    def one_group(nm):
+        pick(A(nm), [[-16, 8], [0, 16]], OP.is_ge, 0.0, 0, 1)
+        pick(A(nm), [[16, 8], [0, 16]], OP.is_ge, 0.0, 15, -1)
+
+    for nm, v in (("SHU", 0.0), ("SEL", 1.0), ("IDF", 0.0), ("SHD", 0.0), ("TRI", 1.0), ("DF", 0.0)):
+        fill(A(nm), v)
+    fill(sel(S_M), -1.0)
+    fill(A("ZB"), 0.0)
+    fill(A("ONE"), 1.0)
+    fill(A("KT"), 0.0)
+    iota(A("PI", 0, 1), [[0, 1]], 0, 1, False)
+    iota(A("TA"), [[1, 256]], 0, 0)
+    iota(A("TB"), [[0, 2], [1, 128]], 0, 0)
+    iota(A("TC"), [[128, 2], [0, 128]], 0, 0)
+    pick(A("SHU"), [[-1, 128]], OP.not_equal, 1.0, -1, 1)
+    for c, lo, hi in ((S_B, 0, 4), (S_P, 0, 15), (S_M, 0, 15), (S_A, 0, 2), (S_D, 3, 4), (S_N, 2, 2)):
+        selector(c, lo, hi)
+    pick(sel(S_B), [[-16, 8]], OP.not_equal, 0.0, -2, 1)
+    pick(A("IDF"), [[-1, 128]], OP.not_equal, 1.0, 0, 1)
+    iota(A("CR", 0, 65), [[1, 65]], -65, 0)
+    iota(A("CR", 65, 131), [[1, 66]], 0, 0)
+    iota(A("QT"), [[128, 2], [0, 8], [256, 16]], 0, 1)
+    iota(A("MROW", 0, 128), [[0, 8], [1, 16]], 0, 0)
+    iota(A("KEX"), [[0, 16], [256, 16]], 0, 0)
+    iota(A("IEX"), [[1, 16], [0, 16]], 0, 0)
+    pi = lambda k: A("PI", k, k + 1)
+    pc = lambda k: A("PC", k, k + 1)
+    ts(pi(1), pi(0), 15, None, OP.bitwise_and)
+    ts(pi(3), pi(0), 7, None, OP.bitwise_and)
+    cp(pc(0), pi(1))
+    ts(pc(1), pc(0), 256.0, None, OP.mult)
+    ts(A("AT1"), A("TA"), pc(1), 1.0, OP.add, OP.add)
+    cp(A("PLO"), A("TB"))
+    ts(A("PHI"), A("TC"), pc(1), None, OP.add)
+    rows("KT", 0, 0, A("PLO"), "y")
+    rows("KT", 0, 1, A("PHI"), "s")
+    ts(pc(5), pc(0), 15.0, 8192.0, OP.is_equal, OP.mult)
+
+    def late_constants():
+        for c, lo, hi in ((S_0, 0, 0), (S_01, 0, 1), (S_K, 0, 1), (S_I, 2, 3)):
+            selector(c, lo, hi)
+        pick(A("SHD"), [[-1, 128]], OP.not_equal, 1.0, 1, 1)
+        one_group("SHD")
+        pick(A("TRI"), [[1, 128]], OP.is_ge, 0.0, -1, -1)
+        one_group("TRI")
+        for k, v in ((0, 1.0), (1, -2.0), (2, 1.0)):
+            pick(A("DF"), [[-1, 64]], OP.not_equal, v, -k, 1)
+        fill(pc(10), -1.0)
+        fill(pc(11), -2.0)
+        ts(A("MROW", 0, 128), A("MROW", 0, 128), 1.0, None, OP.min)
+        ts(A("ATK"), A("AT1"), -1.0, 1.0, OP.add, OP.max)
+        ts(A("ATK"), A("ATK"), 4096.0, None, OP.mult)
+        fill(A("HM"), 0.0)
+        fill(A("WB", 16384, 16416), 0.0)
+        cp(pc(3), pi(3))
+        ts(pc(4), pc(3), 16.0, None, OP.mult)
+        tt(pc(7), pc(0), pc(3), OP.subtract)
+        ts(pc(7), pc(7), 16.0, None, OP.mult)
+        for name in ("VT0", "ST1", "VT2"):
+            iota(A(name), [[0, 4096]], 0, 0)
+        for name, la, ha, lt, ht in (("VT0", 0, 0, "PLO", "PHI"), ("ST1", 65, 4032, "R", "IH"),
+                                     ("VT2", 1, 8192, "HB", "HB1")):
+            ts(A(lt), A("IEX"), pc(4), float(la), OP.add, OP.add)
+            ts(A(ht), A("KEX"), pc(7), float(ha), OP.add, OP.add)
+            rows(name, 0, 0, A(lt))
+            rows(name, 0, 1, A(ht))
+
+    def st2():
+        ts(pc(6), pc(0), 0.0, 64.0, OP.is_equal, OP.mult)
+        ts(pc(8), pc(0), 1.0, 64.0, OP.is_equal, OP.mult)
+        tt(pc(6), pc(6), pc(8), OP.subtract)
+        ts(A("ST2"), A("VT2", 3072, 4096), pc(6), None, OP.add)
+
+    zb = lambda k: A("ZB", 0, k)
+    half = lambda nm, h: A(nm, 128 * h, 128 * h + 128)
+
+    def exts(buf, off, h, out, s, k=8, start=True, stop=True):
+        for i in range(16):
+            mm(A(out, i, i + (k - 1) * 16 + 1, 16), A(buf, off + 2048 * h + i, off + 2048 * h + 2048, 16), sel(s, k),
+               start, stop if stop is True else (stop == "last" and i == 15))
+
+    def maxcarry(col):
+        mm(A("P4", 0, 128, 1, 0, 1), col, A("SHD"))
+        scan(A("CROW", 0, 128, 1, 0, 1), A("MROW", 0, 128, 1, 0, 1), A("P4", 0, 128, 1, 0, 1), OP.mult, OP.max)
+        mm(A("P5", 0, 1), A("CROW", 0, 128, 1, 0, 1), A("ONE", 0, 1, 1, 0, 1))
+        return A("P5", 0, 1)
+
+    def sumcarry(col):
+        mm(A("P5", 8, 9), A("TRI"), col)
+        return A("P5", 8, 9)
+
+    def split(hi, lo, src):
+        cp(hi, src)
+        tt(lo, src, hi, OP.subtract)
+
+    for t in range(2):
+        X, XO = "XW%d" % t, "XW%d" % (1 - t)
+        if t == 0:
+            cp(A("EB", 0, 256), A("VI"))
+        mm(A("P4", 0, 1), A("SHU"), A("EB", 0, 1))
+        tt(A("NHB"), A("EB", 0, 256), A("AT1"), OP.is_gt)
+        rows("KT", 0, 2, A("NHB"), "y")
+        ts(A("EB", 256, 257), A("P4", 0, 1), pc(5), None, OP.add)
+        tt(A("TC"), A("EB", 1, 257), A("EB", 0, 256), OP.is_lt)
+        tt(A("TD"), A("EB", 1, 257), A("AT1"), OP.subtract)
+        tt(A("TD"), A("TD"), A("TC"), OP.mult)
+        cp(A("DHI"), A("TD"))
+        rows("KT", 0, 3, A("DHI"), "s")
+        tt(A("DLO"), A("TD"), A("DHI"), OP.subtract)
+        rows("KT", 0, 4, A("DLO"), "y")
+        for h in range(2):
+            cp(half("VL", h), half("HI", h))
+        tt(A("TC"), A("TD"), A("AT1"), OP.add)
+        ts(A("BLB"), A("TC"), 15.0, None, OP.add)
+        ts(A("ELB"), A("EB", 0, 256), -1.0, None, OP.add)
+        if t == 0:
+            late_constants()
+
+        def xa(h):
+            tt(A("WB", 4096 + 2048 * h, 6144 + 2048 * h), IND(X, 16, 4112, "VL", 128 * h, 128 * h + 128),
+               A("W", 2048 * h, 2048 * h + 2048), OP.min)
+            mm(A("P%d" % h, 0, 128), zb(128), zb(128), True, False)
+            exts("WB", 4096, h, "P%d" % h, S_P, 8, False, False)
+
+        def xb(h):
+            tt(A("WB", 8192 + 2048 * h, 10240 + 2048 * h), IND("XB", 0, 4096, "VL", 128 * h, 128 * h + 128),
+               A("W", 2048 * h, 2048 * h + 2048), OP.min)
+            exts("WB", 8192, h, "P%d" % h, S_M, 8, False, "last")
+
+        def kid(h):
+            act(A("WB", 12288 + 2048 * h, 14336 + 2048 * h), IND("KT", 0, 4096, "VL", 128 * h, 128 * h + 128))
+            exts("WB", 12288, h, "P%d" % (2 + h), S_A, 24)
+
+        def small(h, last):
+            ts(half("TA", h), A("P%d" % h, 0, 128), 0.0, None, OP.is_gt)
+            tt(half("TB", h), A("P%d" % (2 + h), 128, 256), half("TA", h), OP.mult)
+            tt(half("VI" if last else "TC", h), A("P%d" % (2 + h), 0, 128), half("TB", h), OP.add)
+            if not last:
+                tr(A("P%d" % (4 + h), 0, 128), half("TC", h))
+
+        def relist(h):
+            cp(half("VL", h), A("P%d" % (4 + h), 0, 128))
+
+        for h in range(2):
+            exts("KT", 0, h, "P%d" % (4 + h), S_B)
+        kid(0)
+        xa(0)
+        xa(1)
+        for h in range(2):
+            ts(half("TD", h), A("P%d" % (4 + h), 0, 128), 16.0, None, OP.add)
+            tr(A("P%d" % (6 + h), 0, 128), half("TD", h))
+        ts(A("KEY"), A("EB", 0, 256), 4096.0, None, OP.mult)
+        tt(A("KEY"), A("KEY"), A("AT1"), OP.subtract)
+        for h in (1, 0):
+            cp(half("BLW", h), A("P%d" % (6 + h), 0, 128))
+        act(A("XB", 2048, 4096), IND(X, 0, 4112, "BLW", 128, 256))
+        kid(1)
+        cp(A("XB", 0, 2048), IND(X, 0, 4112, "BLW", 0, 128))
+        xb(0)
+        xb(1)
+        small(0, False)
+        tt(A("KEY"), A("KEY"), A("NHB"), OP.mult)
+        ts(A("HMB"), A("NHB"), -BIG, BIG, OP.mult, OP.add)
+        for q in range(8):
+            dma(A("HM", 66 * q, 66 * q + 64, 1, 0, 64), A("HMB", 0, 256, 1, 16 * q, 16 * q + 16))
+        iota(A("WB", 0, 4096), [[0, 4096]], 0, 0)
+        iota(A("WF", 0, 4096), [[0, 4096]], 0, 0)
+        relist(0)
+        for s in range(1, 4):
+            xa(0)
+            kid(0)
+            small(1, False)
+            xb(0)
+            relist(1)
+            xa(1)
+            kid(1)
+            if s == 1:
+                act(half("HIT", 0), A("P2", 256, 384))
+                act(half("HIT", 1), A("P3", 256, 384))
+            small(0, s == 3)
+            xb(1)
+            if s < 3:
+                relist(0)
+                o = 4112 if s == 1 else 8208
+                act(A(X, o, o + 4096), A(X, 15, 4111), AF.Relu, pc(9 + s))
+
+        for b in range(4, 8):
+            mm(A("P%d" % b, 0, 264, 1, 0, 65), zb(65), zb(264), True, False)
+        slot, slot2 = 0, 0
+        for h in range(2):
+            if h == 1:
+                small(1, True)
+            ts(half("HI", h), half("VI", h), 6, None, OP.arith_shift_right)
+            ts(half("TA", h), half("HI", h), -64.0, None, OP.add)
+            ts(half("HI", h), half("VI", h), 63, None, OP.bitwise_and)
+            ts(half("S2", h), half("HI", h), 1.0, None, OP.add)
+            tt(half("S1", h), half("TA", h), half("HIT", h), OP.mult)
+            for q in range(8):
+                for i in range(16):
+                    c = 128 * h + 16 * q + i
+                    if i % 4 == 3:
+                        o, b, last = 7860 + 131 * (slot2 % 30), 4, 15
+                        slot2 += 1
+                        act(A(XO, o, o + 65), A("CR", 0, 65), AF.Relu, A("S1", c, c + 1), -1.0)
+                        act(A(XO, o + 65, o + 131), A("CR", 65, 131), AF.Relu, A("S2", c, c + 1), -1.0)
+                    else:
+                        o, b, last = 131 * (slot % 60), 6, 14
+                        slot += 1
+                        ts(A(XO, o, o + 131), A("CR", 0, 131), A("S1", c, c + 1), A("S2", c, c + 1), OP.max, OP.min)
+                    mm(A("P%d" % (b + q // 4), 66 * (q % 4), 66 * (q % 4) + 66, 1, 0, 65), A(XO, o, o + 65),
+                       A(XO, o + 65, o + 131), False, h == 1 and i == last and q % 4 == 3)
+        if t == 0:
+            dma(A("HI"), IO("start", slice(0, 128), slice(256, 512)), "y")
+        act(A("SC", 0, 264), A("P6", 0, 264, 1, 0, 65))
+        cp(A("SC", 264, 528), A("P7", 0, 264, 1, 0, 65))
+        tt(A("SC", 264, 528), A("SC", 264, 528), A("P5", 0, 264, 1, 0, 65), OP.subtract)
+        tt(A("SC", 0, 264), A("SC", 0, 264), A("P4", 0, 264, 1, 0, 65), OP.subtract)
+        tt(A("D1", 0, 527), A("SC", 1, 528), A("SC", 0, 527), OP.subtract)
+        tt(A("SC", 0, 526), A("D1", 0, 526), A("D1", 1, 527), OP.subtract)
+        for b, (c0, c1) in enumerate(((0, 264), (264, 526))):
+            mm(A("P%d" % (6 + b), 0, c1 - c0, 1, 0, 64), A("DF", 0, 64, 1, 0, 65), A("SC", c0, c1))
+            tt(A("FL", c0, c1), A("P%d" % (6 + b), 0, c1 - c0, 1, 0, 64), A("HM", c0, c1, 1, 0, 64), OP.mult)
+        for q in range(8):
+            dma(A(XO, 15, 4111, 1, 16 * q, 16 * q + 1), A("FL", 66 * q, 66 * q + 64), "y" if q % 2 else "s")
+        dma(A("HB"), A(XO, 15, 4111, 1, 0, 128, 16), "y")
+        dma(A("HB1"), A(XO, 16, 4112, 1, 0, 128, 16), "y")
+
+        act(A(XO, GB, GB + 2048), IND(XO, 0, 4112, "BLB", 0, 128))
+        cp(A(XO, GB + 2048, GB + 4096), IND(XO, 0, 4112, "BLB", 128, 256))
+        for h in range(2):
+            exts(XO, GB, h, "P%d" % h, S_0)
+        if t == 0:
+            st2()
+        ts(A("KEEP"), A("HB"), 0.0, None, OP.is_le)
+        fill(A("TE"), 0.0)
+        scan(A("TA"), A("KEEP"), A("TE"), OP.add, OP.add)
+        k0 = sumcarry(A("TA", 255, 256))
+        for h in range(2):
+            ts(half("TB", h), A("P%d" % h, 0, 128), 0.0, BIG, OP.is_gt, OP.mult)
+            tr(A("P2", 128 * h, 128 * h + 128), half("TB", h))
+        ts(A("TA"), A("TA"), k0, None, OP.add)
+        split(A("PHI"), A("PLO"), A("TA"))
+        rows(XO, KM, 0, A("PHI"), "y")
+        rows(XO, KM, 1, A("PLO"), "y")
+        tt(A("KEX"), A("TA"), A("KEEP"), OP.subtract)
+        tt(A("TC"), A("P2", 0, 256), A("HB1"), OP.add)
+        tt(A("TC"), A("TC"), A("KEY"), OP.min)
+        scan(A("R"), A("TC"), A("TC"), OP.max, OP.max)
+        c = maxcarry(A("R", 255, 256))
+        ts(A("R"), A("R"), c, None, OP.max)
+        tt(A("INS"), A("R"), A("ATK"), OP.is_ge)
+        tt(A("KI"), A("KEEP"), A("INS"), OP.mult)
+        scan(A("TA"), A("KI"), A("TE"), OP.add, OP.add)
+        c = sumcarry(A("TA", 255, 256))
+        tt(A("TOP"), A("R"), A("TC"), OP.is_equal)
+        tt(A("TOP"), A("TOP"), A("INS"), OP.mult)
+        ts(A("TA"), A("TA"), c, None, OP.add)
+        split(A("DHI"), A("DLO"), A("TA"))
+        rows(XO, KM, 2, A("DHI"), "y")
+        rows(XO, KM, 3, A("DLO"), "y")
+        for h in range(2):
+            act(A(XO, GB + 2048 * h, GB + 2048 * h + 2048), IND(XO, KM, KM + 4096, "ELB", 128 * h, 128 * h + 128))
+        tt(A("IEX"), A("TA"), A("KI"), OP.subtract)
+        tt(A("TB"), A("TOP"), A("IEX"), OP.mult)
+        scan(A("IH"), A("TB"), A("TB"), OP.max, OP.max)
+        c = maxcarry(A("IH", 255, 256))
+        ts(A("IH"), A("IH"), c, None, OP.max)
+        tt(A("TB"), A("IH"), A("IEX"), OP.subtract)
+        tt(A("TB"), A("TB"), A("INS"), OP.mult)
+        tt(A("TB"), A("TB"), A("IEX"), OP.add)
+        ts(A("TB"), A("TB"), 2.0, None, OP.mult)
+        tt(A("TB"), A("TB"), A("KEX"), OP.add)
+        ts(A("TD"), A("AT1"), 12287.0, None, OP.add)
+        tt(A("TB"), A("TB"), A("TD"), OP.subtract)
+        tt(A("TC"), A("TB"), A("KEEP"), OP.mult)
+        tt(A("TC"), A("TC"), A("TD"), OP.add)
+        cp(A("QL0"), A("TC"))
+        sc0 = lambda k: cp(IND("WB", 0, 16384, "QL0", 64 * k, 64 * k + 64), A("VT0", 1024 * k, 1024 * k + 1024))
+        sc2 = lambda k: cp(IND("WB", 0, 16384, "QL2", 64 * k, 64 * k + 64), A("VT2", 1024 * k, 1024 * k + 1024))
+        sc0(0)
+        tt(A("TB"), A("TB"), A("KI"), OP.mult)
+        tt(A("Q0M"), A("TB"), A("TD"), OP.add)
+        ts(A("TE"), A("INS"), -2.0, 2.0, OP.mult, OP.add)
+        for h in range(2):
+            exts(XO, GB, h, "P%d" % h, S_K, 16)
+        for h in range(2):
+            cp(half("TA", h), A("P%d" % h, 128, 256))
+            tr(A("P2", 128 * h, 128 * h + 128), half("TA", h))
+        for h in range(2):
+            cp(half("TB", h), A("P%d" % h, 0, 128))
+            tr(A("P3", 128 * h, 128 * h + 128), half("TB", h))
+        tt(A("TC"), A("P2", 0, 256), A("TOP"), OP.mult)
+        scan(A("R"), A("TC"), A("TC"), OP.max, OP.max)
+        c = maxcarry(A("R", 255, 256))
+        tt(A("TD"), A("P2", 0, 256), A("IEX"), OP.subtract)
+        tt(A("TD"), A("TD"), A("TE"), OP.mult)
+        ts(A("R"), A("R"), c, None, OP.max)
+        tt(A("R"), A("R"), A("IH"), OP.subtract)
+        tt(A("R"), A("R"), A("KI"), OP.mult)
+        tt(A("TC"), A("Q0M"), A("R"), OP.add)
+        cp(A("QL1"), A("TC"))
+        for k in range(4):
+            act(IND("WF", 0, 16384, "QL1", 64 * k, 64 * k + 64), A("ST1", 1024 * k, 1024 * k + 1024), AF.Silu)
+        tt(A("TC"), A("TC"), A("R"), OP.add)
+        cp(A("QL2"), A("TC"))
+        tt(A("TA"), A("P3", 0, 256), A("KEX"), OP.subtract)
+        tt(A("TA"), A("TA"), A("TD"), OP.add)
+        split(A("PHI"), A("PLO"), A("TA"))
+        act(IND("WF", 0, 16384, "QL2", 192, 256), A("ST2"), AF.Silu)
+        for k in range(1, 4):
+            sc0(k)
+        for k in range(3):
+            sc2(k)
+        for k in range(3):
+            o = 4096 + (15, 4112, 8208)[k]
+            rows("WB", o, 0, A("PHI"), "y")
+            rows("WB", o, 1, A("PLO"), "y")
+        act(A("XB", 2048, 4096), A("WF", 2048, 4096))
+        act(A("XB", 0, 2048), A("WF", 0, 2048))
+        for h in (1, 0):
+            mm(A("P%d" % h, 0, 128), zb(128), zb(128), True, False)
+            exts("XB", 0, h, "P%d" % h, S_01, 8, False, False)
+        for h in (1, 0):
+            exts("WB", 0, h, "P%d" % h, S_01, 8, False, "last")
+        for h in (1, 0):
+            ts(half("TB", h), A("P%d" % h, 0, 128), 15.0, None, OP.add)
+            tr(A("P%d" % (2 + h), 0, 128), half("TB", h))
+            cp(half("VL", h), A("P%d" % (2 + h), 0, 128))
+        LX, ES, RE = ["%s%d" % (nm, t) for nm in ("LX", "ES", "RE")]
+        dx = 15 if t == 0 else 0
+        SZ = lambda a, b: IND("WB", 4096, 16400, "VL", a, b)
+        XI = lambda a, b: IND(X, 0, 12304, "VL", a, b)
+        cp(A("TX"), XI(240, 256))
+        act(A(XO, GB + 3840, GB + 4096), SZ(240, 256))
+        for h in range(2):
+            mm(A("P4", 8 * h, 8 * h + 8), A(XO, GB + 3840 + 128 * h, GB + 3968 + 128 * h), sel(S_01))
+        tt(A(ES), A("P4", 0, 16), A("QT", 15, 256, 16), OP.add)
+        ts(A(ES), A(ES), 4096.0, None, OP.min)
+        rid, pid, _se = topo.addr(nxt)
+        m = topo.mask(core, nxt)
+        ne, nb = len(topo.engines(core, nxt)), len(topo.engines(prv, core))
+
+        def send(src, dst, ss, rs):
+            sa, da = A(src), T[dst][:]
+            op("g", lambda: g.remote_dma(da, sa[0], T.sem[rs], T.sem[ss], pid, rid, m), sa[1], [], remote=(ss, ne))
+            total[rs] = nb
+            hist[dst] = [{"reg": (0, 128, 1, 0, 256), "w": True, "q": "remote", "sem": rs, "val": nb, "vc": {}, "n": 0,
+                          "dma": True}]
+        send("TX", LX, "xs%d" % t, "xr%d" % t)
+        send(ES, RE, "es%d" % t, "er%d" % t)
+        cp(A(XO, dx + 2048, dx + 3840), XI(128, 240))
+        act(A(XO, GB + 2048, GB + 3840), SZ(128, 240))
+        if t == 1:
+            dma(IO("y", slice(0, 128), slice(2048, 3840)), A(XO, dx + 2048, dx + 3840))
+        cp(A(XO, dx, dx + 2048), XI(0, 128))
+        act(A(XO, GB, GB + 2048), SZ(0, 128))
+        for i in list(range(8, 15)) + list(range(8)):
+            for h in range(2):
+                mm(A("P5", 128 * h + i, 128 * h + 113 + i, 16),
+                   A(XO, GB + 256 * i + 128 * h, GB + 256 * i + 128 * h + 128), sel(S_01))
+        for h in range(2):
+            mm(A("P5", 128 * h + 15, 128 * h + 128, 16), zb(128), zb(8))
+        if t == 0:
+            cp(A(XO, 3855, 4111), A(LX))
+        else:
+            dma(IO("y", slice(0, 128), slice(0, 2048)), A(XO, dx, dx + 2048))
+            dma(IO("y", slice(0, 128), slice(3840, 4096)), A(LX))
+        tt(A("TA"), A("P5", 0, 256), A("QT"), OP.add)
+        ts(A("TA"), A("TA"), 3840.0, None, OP.min)
+        cp(A("TA", 15, 256, 16), A(RE))
+        for h in range(2):
+            tr(A("P6", 128 * h, 128 * h + 128), half("TA", h))
+        cp(A("EB", 0, 256), A("P6", 0, 256))
+        if t == 1:
+            dma(IO("ye"), A("EB", 0, 256))
+
+    for s in sorted(total):
+        if known["g"].get(s, 0) < total[s]:
+            g.wait_ge(T.sem[s], total[s])

@@ -4,34 +4,35 @@ OP = AluOpType
 AF = ActivationFunctionType
 F32, BF, I32, U16 = "float32", "bfloat16", "int32", "uint16"
 NDMA = 110
+ZC = 4128
 SCRATCH = {
-    "XW0": ("sbuf", [128, 12304], BF), "XW1": ("sbuf", [128, 12304], BF),
-    "XB": ("sbuf", [128, 4096], BF), "W": ("sbuf", [128, 4096], BF), "KT": ("sbuf", [128, 4096], BF),
-    "WB": ("sbuf", [128, 16416], BF), "WF": ("sbuf", [128, 16384], F32),
-    "VT0": ("sbuf", [128, 4096], BF), "VT2": ("sbuf", [128, 4096], BF), "ST1": ("sbuf", [128, 4096], F32),
-    "ST2": ("sbuf", [128, 1024], F32),
-    "ZB": ("sbuf", [128, 264], BF), "CR": ("sbuf", [128, 132], BF),
-    "IDF": ("sbuf", [128, 128], F32), "SHU": ("sbuf", [128, 128], F32),
-    "SHD": ("sbuf", [128, 128], F32), "TRI": ("sbuf", [128, 128], F32), "DF": ("sbuf", [128, 64], F32),
-    "MROW": ("sbuf", [128, 128], F32), "ONE": ("sbuf", [128, 2], F32), "PI": ("sbuf", [128, 8], I32),
-    "PC": ("sbuf", [128, 16], F32), "SEL": ("sbuf", [128, 128], BF),
-    "AT1": ("sbuf", [128, 256], F32), "ATK": ("sbuf", [128, 256], F32), "QT": ("sbuf", [128, 256], F32),
-    "EB": ("sbuf", [128, 258], F32),
-    "NHB": ("sbuf", [128, 256], BF), "DHI": ("sbuf", [128, 256], BF), "DLO": ("sbuf", [128, 256], BF),
-    "HMB": ("sbuf", [128, 256], BF), "HM": ("sbuf", [128, 528], BF),
-    "BLB": ("sbuf", [128, 256], U16), "ELB": ("sbuf", [128, 256], U16), "BLW": ("sbuf", [128, 256], U16),
-    "VL": ("sbuf", [128, 256], U16), "QL0": ("sbuf", [128, 256], U16), "QL1": ("sbuf", [128, 256], U16),
-    "QL2": ("sbuf", [128, 256], U16),
-    "TA": ("sbuf", [128, 256], F32), "TB": ("sbuf", [128, 256], F32), "TC": ("sbuf", [128, 256], F32),
-    "TD": ("sbuf", [128, 256], F32), "TE": ("sbuf", [128, 256], F32),
-    "VI": ("sbuf", [128, 256], I32), "HI": ("sbuf", [128, 256], I32),
-    "S1": ("sbuf", [128, 256], BF), "S2": ("sbuf", [128, 256], BF), "FL": ("sbuf", [64, 528], BF),
-    "HB": ("sbuf", [128, 256], BF), "HB1": ("sbuf", [128, 256], BF),
-    "KEEP": ("sbuf", [128, 256], BF), "KEX": ("sbuf", [128, 256], F32), "R": ("sbuf", [128, 256], F32),
-    "INS": ("sbuf", [128, 256], BF), "KI": ("sbuf", [128, 256], BF), "IEX": ("sbuf", [128, 256], F32),
-    "IH": ("sbuf", [128, 256], F32), "TOP": ("sbuf", [128, 256], BF),
+    "XW0": ("sbuf", [128, 3 * ZC], BF), "XW1": ("sbuf", [128, 3 * ZC], BF),
+    "XB": ("sbuf", [128, 4096], BF), "W": ("sbuf", [128, 4096], BF), "KT": ("sbuf", [128, 4112], BF),
+    "WB": ("sbuf", [128, 16384], BF), "WF": ("sbuf", [128, 16384], F32),
+    "VT": ("sbuf", [128, 4096], BF), "ST": ("sbuf", [128, 4096], F32),
+    "ZB": ("sbuf", [128, 264], BF), "CR": ("sbuf", [128, 194], BF), "CM": ("sbuf", [128, 11 * 128], BF),
+    "IDF": ("sbuf", [128, 128], F32), "SHU": ("sbuf", [128, 128], F32), "TRI": ("sbuf", [128, 128], F32),
+    "IHF": ("sbuf", [128, 128], F32), "DFV": ("sbuf", [128, 128], F32), "DFS": ("sbuf", [128, 128], F32),
+    "MSK": ("sbuf", [128, 16], F32), "DEC": ("sbuf", [128, 32], F32), "S15": ("sbuf", [128, 8], F32),
+    "PI": ("sbuf", [128, 8], I32), "PC": ("sbuf", [128, 16], F32), "SEL": ("sbuf", [128, 88], BF),
+    "ROW": ("sbuf", [2, 896], BF), "NG": ("sbuf", [128, 768], BF),
+    "AT1": ("sbuf", [128, 256], F32), "Q2": ("sbuf", [128, 256], F32),
+    "AM": ("sbuf", [128, 256], F32), "EB": ("sbuf", [128, 256], F32),
+    "DHI": ("sbuf", [128, 256], BF), "DLO": ("sbuf", [128, 256], BF),
     "PHI": ("sbuf", [128, 256], BF), "PLO": ("sbuf", [128, 256], BF),
-    "CROW": ("sbuf", [128, 128], F32), "TX": ("sbuf", [128, 256], BF),
+    "NB": ("sbuf", [128, 256], BF), "HM": ("sbuf", [128, 264], BF), "FL": ("sbuf", [128, 264], BF),
+    "BLB": ("sbuf", [128, 256], U16), "ELB": ("sbuf", [128, 256], U16), "VL": ("sbuf", [128, 256], U16),
+    "VB": ("sbuf", [128, 256], U16), "QL": ("sbuf", [128, 256], U16), "L15": ("sbuf", [128, 32], U16),
+    "TA": ("sbuf", [128, 256], F32), "TB": ("sbuf", [128, 256], F32), "TC": ("sbuf", [128, 256], F32),
+    "TD": ("sbuf", [128, 256], F32), "TE": ("sbuf", [128, 512], F32), "LEN": ("sbuf", [128, 256], F32),
+    "FS": ("sbuf", [128, 512], F32), "VI": ("sbuf", [128, 256], I32), "HI": ("sbuf", [128, 256], I32),
+    "AQ": ("sbuf", [128, 256], BF), "NOH": ("sbuf", [128, 256], BF), "S12": ("sbuf", [128, 512], BF),
+    "HB": ("sbuf", [128, 256], BF), "KP2": ("sbuf", [128, 256], BF), "KP4": ("sbuf", [128, 256], BF),
+    "KI": ("sbuf", [128, 256], BF), "INS": ("sbuf", [128, 256], BF), "TOP": ("sbuf", [128, 256], BF),
+    "K2": ("sbuf", [128, 260], F32), "I4": ("sbuf", [128, 260], F32), "CC": ("sbuf", [128, 16], F32),
+    "RH": ("sbuf", [128, 32], F32), "FA": ("sbuf", [128, 512], BF), "FB": ("sbuf", [128, 512], BF),
+    "M1": ("sbuf", [128, 256], BF), "M2": ("sbuf", [128, 256], BF), "C2": ("sbuf", [128, 256], BF),
+    "CS": ("sbuf", [128, 256], F32), "TX": ("sbuf", [128, 256], BF), "TZ": ("sbuf", [128, 256], BF),
     "LX0": ("sbuf", [128, 256], BF), "LX1": ("sbuf", [128, 256], BF),
     "ES0": ("sbuf", [128, 16], F32), "ES1": ("sbuf", [128, 16], F32),
     "RE0": ("sbuf", [128, 16], F32), "RE1": ("sbuf", [128, 16], F32),
@@ -41,11 +42,14 @@ for _k in range(8):
 SEMAPHORES = ["qv", "qs", "qt", "qg"] + ["d%d" % k for k in range(NDMA)]
 SEMAPHORES += ["%s%d" % (a, k) for a in ("xs", "xr", "es", "er") for k in range(2)]
 
-ALIAS = {"SC": (4096, 528, 65), "D1": (4640, 528, 65), "HIT": (5200, 256, 128), "KEY": (5456, 256, 128),
-         "Q0M": (5712, 256, 128)}
-S_P, S_M, S_A, S_D, S_N, S_B, S_0, S_01, S_K, S_I = 0, 8, 16, 24, 32, 40, 48, 56, 64, 72
-BIG = float(2 ** 24)
-KM, GB = 4112, 8208
+ALIAS = {"SCV": (8192, 264), "SCS": (8456, 264), "Z2": (8720, 264), "D1": (8984, 264)}
+S_P, S_M, S_K, S_0, S_J, S_E, S_C = 0, 8, 16, 40, 48, 64, 72
+CMS = (1.0, -64.0, 64.0, 32768.0, 32768.0, 128.0, 2.0, float(ZC), 4096.0, 256.0, 16.0)
+IB, N64, P64, BI, BSU, I128, I2, IZ, I4K, I256, I16 = range(11)
+BIG, TOPB = 32768.0, 8192.0
+KM = 4112
+VS = 128
+SCOL = (3, 7, 11, 15)
 
 
 def rank_program(g, core, T, topo):
@@ -61,27 +65,27 @@ def rank_program(g, core, T, topo):
     def over(a, b):
         if a[0] >= b[1] or b[0] >= a[1] or a[3] >= b[4] or b[3] >= a[4]:
             return False
-        return not (a[2] == 16 and b[2] == 16 and a[0] % 16 != b[0] % 16)
+        m = min(a[2], b[2])
+        return a[0] % m == b[0] % m
 
     def inside(a, b):
-        if not (b[0] <= a[0] and a[1] <= b[1] and b[3] <= a[3] and a[4] <= b[4]):
+        if not (b[0] <= a[0] and a[1] <= b[1] and b[3] <= a[3] and a[4] <= b[4] and b[5] == 1):
             return False
-        return b[2] == 1 or (a[2] == 16 and a[0] % 16 == b[0] % 16)
+        return a[2] % b[2] == 0 and a[0] % b[2] == b[0] % b[2]
 
     def is_psum(name):
         return name[0] == "P" and name[1:].isdigit()
 
     def op(q, call, R, W, dma=False, remote=None):
         deps = []
-        for name, reg in R:
-            ps = is_psum(name)
-            for r in hist.get(name, []):
-                if over(r["reg"], reg) and (r["w"] or (ps and r["q"] != q)):
-                    deps.append(r)
-        for name, reg in W:
-            for r in hist.get(name, []):
-                if over(r["reg"], reg) and not (q == "t" and r["q"] == "t"):
-                    deps.append(r)
+        for w, lst in ((False, R), (True, W)):
+            for name, reg in lst:
+                ps = is_psum(name)
+                for r in hist.get(name, []):
+                    if ps and r["q"] != q:
+                        deps.append(r)
+                    elif over(r["reg"], reg) and (w or r["w"]) and not (ps and q == "t"):
+                        deps.append(r)
         deps.sort(key=lambda r: -r["n"])
         kn = known[q]
         for r in deps:
@@ -109,7 +113,9 @@ def rank_program(g, core, T, topo):
         for w, lst in ((False, R), (True, W)):
             for name, reg in lst:
                 h = hist.setdefault(name, [])
-                if w or is_psum(name):
+                if is_psum(name):
+                    h[:] = [r for r in h if r["q"] == q and q != "t" and not (inside(r["reg"], reg) and (w or not r["w"]))]
+                elif w:
                     h[:] = [r for r in h if not inside(r["reg"], reg)]
                 elif not dma and remote is None:
                     h[:] = [r for r in h if r["w"] or r["dma"] or r["q"] != q or not inside(r["reg"], reg)]
@@ -118,37 +124,35 @@ def rank_program(g, core, T, topo):
 
     def A(name, c0=0, c1=None, cs=1, p0=0, p1=None, ps=1):
         if name in ALIAS:
-            o, k, r = ALIAS[name]
-            return A("WF", o + c0, o + (k if c1 is None else c1), cs, p0, r if p1 is None else p1, ps)
+            o, k = ALIAS[name]
+            return A("WF", o + c0, o + (k if c1 is None else c1), cs, p0, p1, ps)
         shape = T[name].shape
         c1 = shape[1] if c1 is None else c1
         p1 = shape[0] if p1 is None else p1
         sc = slice(c0, c1) if cs == 1 else slice(c0, c1, cs)
         sp = slice(p0, p1) if ps == 1 else slice(p0, p1, ps)
-        reg = (0, 128, 1, 0, 512) if is_psum(name) else (p0, p1, ps, c0, c1)
-        return T[name][sp, sc], [(name, reg)]
+        return T[name][sp, sc], [(name, (p0, p1, ps, c0, c1, cs))]
 
     def IND(name, c0, c1, lst, l0, l1):
         return (T[name][:, c0:c1].indirect(T[lst][:, l0:l1]),
-                [(name, (0, 128, 1, c0, c1)), (lst, (0, 128, 1, l0, l1))])
+                [(name, (0, 128, 1, c0, c1, 1)), (lst, (0, 128, 1, l0, l1, 1))])
 
     def outs(o):
         return o[1][:1], o[1][1:]
+
+    def num(x):
+        return x if isinstance(x, tuple) else (x, [])
 
     def tt(o, a, b, f):
         op("v", lambda: g.vector.tensor_tensor(o[0], a[0], b[0], f), a[1] + b[1], o[1])
 
     def ts(o, a, s1, s2, f1, f2=None):
-        r = list(a[1])
-        x = [s1, s2]
-        for k in range(2):
-            if isinstance(x[k], tuple):
-                r += x[k][1]
-                x[k] = x[k][0]
+        s1, s2 = num(s1), num(s2)
+        r = a[1] + s1[1] + s2[1]
         if f2 is None:
-            op("v", lambda: g.vector.tensor_scalar(o[0], a[0], x[0], None, f1), r, o[1])
+            op("v", lambda: g.vector.tensor_scalar(o[0], a[0], s1[0], None, f1), r, o[1])
         else:
-            op("v", lambda: g.vector.tensor_scalar(o[0], a[0], x[0], x[1], f1, f2), r, o[1])
+            op("v", lambda: g.vector.tensor_scalar(o[0], a[0], s1[0], s2[0], f1, f2), r, o[1])
 
     def cp(o, a):
         w, r = outs(o)
@@ -157,18 +161,28 @@ def rank_program(g, core, T, topo):
     def fill(o, val):
         op("v", lambda: g.vector.memset(o[0], val), [], o[1])
 
-    def scan(o, a, b, f1, f2):
-        op("v", lambda: g.vector.tensor_tensor_scan(o[0], a[0], b[0], 0.0, f1, f2), a[1] + b[1], o[1])
+    def scan(o, a, b, f1, f2, first=0.0):
+        first = num(first)
+        op("v", lambda: g.vector.tensor_tensor_scan(o[0], a[0], b[0], first[0], f1, f2), a[1] + b[1] + first[1], o[1])
+
+    def most(o, a):
+        op("v", lambda: g.vector.tensor_reduce(o[0], a[0], AxisListType.X, OP.max), a[1], o[1])
 
     def act(o, a, f=AF.Copy, bias=None, scale=1.0):
         w, r = outs(o)
-        if bias is None:
+        if bias is None and scale == 1.0:
             op("s", lambda: g.scalar.activation(o[0], a[0], f), a[1] + r, w)
+        elif bias is None:
+            op("s", lambda: g.scalar.activation(o[0], a[0], f, scale=scale), a[1] + r, w)
         else:
             op("s", lambda: g.scalar.activation(o[0], a[0], f, bias=bias[0], scale=scale), a[1] + r + bias[1], w)
 
     def mm(o, l, r, start=True, stop=True):
         op("t", lambda: g.tensor.matmul(o[0], l[0], r[0], start, stop), l[1] + r[1], o[1])
+
+    def mms(*terms):
+        for k, (o, l, r) in enumerate(terms):
+            mm(o, l, r, k == 0, k == len(terms) - 1)
 
     def dma(o, a, q="y"):
         op(q, lambda: eng[q].dma_start(o[0], a[0]), a[1], o[1], dma=True)
@@ -182,404 +196,467 @@ def rank_program(g, core, T, topo):
     def IO(name, *idx):
         return (T[name][idx] if idx else T[name][:]), []
 
-    def sel(c, k=8):
-        return A("SEL", c, c + k)
-
-    def tr(o, a):
-        mm(o, a, A("IDF"))
+    sel = lambda c, k=8: A("SEL", c, c + k)
+    cm = lambda k: A("CM", 128 * k, 128 * k + 128)
+    zb = lambda k: A("ZB", 0, k)
+    pi = lambda k: A("PI", k, k + 1)
+    pc = lambda k: A("PC", k, k + 1)
+    cc = lambda k: A("CC", k, k + 1)
+    half = lambda nm, h, o=0: A(nm, o + 128 * h, o + 128 * h + 128)
+    P = lambda b, c0=0, c1=256, cs=1, p0=0, p1=128: A("P%d" % b, c0, c1, cs, p0, p1)
+    IDF = A("IDF")
 
     def rows(name, off, r, src, q="y"):
         dma(A(name, off, off + 4096, 1, r, 128, 16), src, q)
 
     dma(A("VI"), IO("ends"), "y")
     dma(A("HI"), IO("start", slice(0, 128), slice(0, 256)), "s")
-    fill(A("XW0", 0, 16), 0.0)
-    fill(A("XW0", 4104, 4112), 0.0)
-    dma(A("XW0", 15, 4111), IO("x"), "y")
-    dma(A("W"), IO("w"), "s")
+    dma(A("XW0", 0, 4096), IO("x"), "y")
+    dma(A("W", 0, 2048), IO("w", slice(0, 128), slice(0, 2048)), "s")
 
     def pick(o, pattern, f, v, base, mul):
         op("g", lambda: g.affine_select(o[0], o[0], pattern, f, v, base, mul), o[1], o[1])
 
-    def selector(c, lo, hi):
-        pick(sel(c), [[-16, 8]], OP.is_ge, 0.0, -lo, 1)
-        pick(sel(c), [[16, 8]], OP.is_ge, 0.0, hi, -1)
+    def selector(o, terms):
+        for r, v in terms:
+            pick(o, [[-16, 8]], OP.not_equal, float(v), -r, 1)
 
-    def one_group(nm):
-        pick(A(nm), [[-16, 8], [0, 16]], OP.is_ge, 0.0, 0, 1)
-        pick(A(nm), [[16, 8], [0, 16]], OP.is_ge, 0.0, 15, -1)
+    def blocks(nm, k):
+        pick(A(nm), [[-k, 128 // k], [0, k]], OP.is_ge, 0.0, 0, 1)
+        pick(A(nm), [[k, 128 // k], [0, k]], OP.is_ge, 0.0, k - 1, -1)
 
-    for nm, v in (("SHU", 0.0), ("SEL", 1.0), ("IDF", 0.0), ("SHD", 0.0), ("TRI", 1.0), ("DF", 0.0)):
-        fill(A(nm), v)
-    fill(sel(S_M), -1.0)
-    fill(A("ZB"), 0.0)
-    fill(A("ONE"), 1.0)
-    fill(A("KT"), 0.0)
     iota(A("PI", 0, 1), [[0, 1]], 0, 1, False)
     iota(A("TA"), [[1, 256]], 0, 0)
-    iota(A("TB"), [[0, 2], [1, 128]], 0, 0)
+    iota(A("TB"), [[0, 2], [1, 128]], 1, 0)
     iota(A("TC"), [[128, 2], [0, 128]], 0, 0)
-    pick(A("SHU"), [[-1, 128]], OP.not_equal, 1.0, -1, 1)
-    for c, lo, hi in ((S_B, 0, 4), (S_P, 0, 15), (S_M, 0, 15), (S_A, 0, 2), (S_D, 3, 4), (S_N, 2, 2)):
-        selector(c, lo, hi)
-    pick(sel(S_B), [[-16, 8]], OP.not_equal, 0.0, -2, 1)
-    pick(A("IDF"), [[-1, 128]], OP.not_equal, 1.0, 0, 1)
-    iota(A("CR", 0, 65), [[1, 65]], -65, 0)
-    iota(A("CR", 65, 131), [[1, 66]], 0, 0)
-    iota(A("QT"), [[128, 2], [0, 8], [256, 16]], 0, 1)
-    iota(A("MROW", 0, 128), [[0, 8], [1, 16]], 0, 0)
-    iota(A("KEX"), [[0, 16], [256, 16]], 0, 0)
-    iota(A("IEX"), [[1, 16], [0, 16]], 0, 0)
-    pi = lambda k: A("PI", k, k + 1)
-    pc = lambda k: A("PC", k, k + 1)
+    fill(A("KT"), 0.0)
+    for nm, v in (("SHU", 0.0), ("SEL", 0.0), ("IDF", 0.0), ("TRI", 1.0), ("DFV", 0.0), ("DFS", 0.0), ("ZB", 0.0),
+                  ("S15", 0.0), ("HM", 0.0)):
+        fill(A(nm), v)
+    for c in range(3):
+        fill(A("XW0", c * ZC + 4096, c * ZC + ZC), 0.0)
+    fill(sel(S_P), 4096.0)
+    fill(sel(S_M), -4096.0)
     ts(pi(1), pi(0), 15, None, OP.bitwise_and)
-    ts(pi(3), pi(0), 7, None, OP.bitwise_and)
     cp(pc(0), pi(1))
     ts(pc(1), pc(0), 256.0, None, OP.mult)
     ts(A("AT1"), A("TA"), pc(1), 1.0, OP.add, OP.add)
     cp(A("PLO"), A("TB"))
     ts(A("PHI"), A("TC"), pc(1), None, OP.add)
-    rows("KT", 0, 0, A("PLO"), "y")
-    rows("KT", 0, 1, A("PHI"), "s")
+    rows("KT", 1, 0, A("PLO"), "y")
+    rows("KT", 1, 1, A("PHI"), "s")
     ts(pc(5), pc(0), 15.0, 8192.0, OP.is_equal, OP.mult)
+    fill(pc(6), 1.0)
+    pick(A("SHU"), [[-1, 128]], OP.not_equal, 1.0, -1, 1)
+    pick(A("IDF"), [[-1, 128]], OP.not_equal, 1.0, 0, 1)
+    for k, rs in enumerate(((0, 1, 3, 4), (0, 1), (3, 4))):
+        selector(sel(S_K + 8 * k), [(r, 1) for r in rs])
+    for c in (S_P, S_M):
+        pick(sel(c), [[-16, 8]], OP.is_ge, 0.0, 0, 1)
+        pick(sel(c), [[16, 8]], OP.is_ge, 0.0, 15, -1)
+
+    dma(A("W", 2048, 4096), IO("w", slice(0, 128), slice(2048, 4096)), "g")
 
     def late_constants():
-        for c, lo, hi in ((S_0, 0, 0), (S_01, 0, 1), (S_K, 0, 1), (S_I, 2, 3)):
-            selector(c, lo, hi)
-        pick(A("SHD"), [[-1, 128]], OP.not_equal, 1.0, 1, 1)
-        one_group("SHD")
+        iota(A("CR", 0, 130), [[1, 130]], -64, 0)
+        iota(A("CR", 130, 194), [[1, 64]], -65, 0)
+        iota(A("ROW", 0, 128), [[0, 128]], 1, 0)
+        iota(A("ROW", 128, 256), [[0, 128]], -112, 0)
+        iota(A("ROW", 256, 384), [[0, 128]], 10240, -10239)
+        iota(A("ROW", 384, 896), [[-1, 2], [0, 256]], 0, 0)
+        selector(sel(S_0), [(0, 1)])
+        selector(sel(S_J), [(0, 1), (1, 1), (12, -1), (13, -1)])
+        selector(sel(S_J + 8), [(4, 16), (5, 16), (8, 1), (9, 1), (12, -17), (13, -17)])
+        selector(sel(S_E), [(0, 0.5), (1, 0.5)])
+        selector(sel(S_C), [(15, 0.5)])
+        selector(A("S15"), [(15, 0.5)])
         pick(A("TRI"), [[1, 128]], OP.is_ge, 0.0, -1, -1)
-        one_group("TRI")
-        for k, v in ((0, 1.0), (1, -2.0), (2, 1.0)):
-            pick(A("DF"), [[-1, 64]], OP.not_equal, v, -k, 1)
-        fill(pc(10), -1.0)
-        fill(pc(11), -2.0)
-        ts(A("MROW", 0, 128), A("MROW", 0, 128), 1.0, None, OP.min)
-        ts(A("ATK"), A("AT1"), -1.0, 1.0, OP.add, OP.max)
-        ts(A("ATK"), A("ATK"), 4096.0, None, OP.mult)
-        fill(A("HM"), 0.0)
-        fill(A("WB", 16384, 16416), 0.0)
-        cp(pc(3), pi(3))
-        ts(pc(4), pc(3), 16.0, None, OP.mult)
-        tt(pc(7), pc(0), pc(3), OP.subtract)
-        ts(pc(7), pc(7), 16.0, None, OP.mult)
-        for name in ("VT0", "ST1", "VT2"):
-            iota(A(name), [[0, 4096]], 0, 0)
-        for name, la, ha, lt, ht in (("VT0", 0, 0, "PLO", "PHI"), ("ST1", 65, 4032, "R", "IH"),
-                                     ("VT2", 1, 8192, "HB", "HB1")):
-            ts(A(lt), A("IEX"), pc(4), float(la), OP.add, OP.add)
-            ts(A(ht), A("KEX"), pc(7), float(ha), OP.add, OP.add)
-            rows(name, 0, 0, A(lt))
-            rows(name, 0, 1, A(ht))
+        blocks("TRI", 16)
+        for nm, terms in (("DFV", ((-1, -1.0), (0, 2.0), (1, -1.0))), ("DFS", ((0, 1.0), (1, -2.0), (2, 1.0)))):
+            for k, v in terms:
+                pick(A(nm), [[-1, 128]], OP.not_equal, v, -k, 1)
+            blocks(nm, 64)
+        pick(A("DFV"), [[-64, 2], [-200, 64]], OP.not_equal, 1.0, 0, 1)
+        iota(A("MSK"), [[1, 16]], 0, 0)
+        iota(A("NG", 0, 768), [[-3, 2], [0, 384]], -1, 0)
+        iota(A("NG", 256, 257), [[0, 1]], -16384, 0)
+        iota(A("NG", 384, 512), [[0, 128]], -1, 0)
 
-    def st2():
-        ts(pc(6), pc(0), 0.0, 64.0, OP.is_equal, OP.mult)
-        ts(pc(8), pc(0), 1.0, 64.0, OP.is_equal, OP.mult)
-        tt(pc(6), pc(6), pc(8), OP.subtract)
-        ts(A("ST2"), A("VT2", 3072, 4096), pc(6), None, OP.add)
+    def late_constants_v():
+        for k, v in enumerate(CMS):
+            ts(cm(k), A("SHU") if k == BSU else IDF, v, None, OP.mult)
+        ts(pc(2), pc(0), 15.0, 0.5, OP.not_equal, OP.mult)
+        ts(A("IHF"), IDF, pc(2), None, OP.mult)
+        ts(pc(3), pc(0), 15.0, 256.0, OP.is_equal, OP.mult)
+        ts(pc(3), pc(3), 3840.0, None, OP.add)
+        ts(pc(4), pc(0), -1.0, 1.0, OP.mult, OP.add)
+        ts(A("DEC", 0, 16), A("MSK"), pc(4), 0.0, OP.add, OP.min)
+        ts(A("DEC", 16, 32), A("DEC", 0, 16), 1024.0, None, OP.mult)
+        ts(A("DEC", 0, 16), A("DEC", 0, 16), 256.0, None, OP.mult)
+        ts(A("MSK"), A("MSK"), pc(0), None, OP.is_equal)
+        ts(A("Q2"), A("AT1"), -1.0, 2.0, OP.add, OP.mult)
+        ts(A("AM"), A("AT1"), 8191.0, None, OP.add)
+        for k, v in ((9, TOPB), (10, 2 * TOPB - 3)):
+            fill(pc(k), v)
+        fill(A("XW1", 11952, 3 * ZC), 0.0)
+        fill(A("K2", 0, 1), 0.0)
+        fill(A("I4", 0, 1), 0.0)
 
-    zb = lambda k: A("ZB", 0, k)
-    half = lambda nm, h: A(nm, 128 * h, 128 * h + 128)
+    def scatter_data():
+        for nm, tile in (("VT", "M1"), ("ST", "CS")):
+            iota(A(nm), [[0, 4096]], 0, 0)
+            for r, pattern, k in ((0, [[0, 16], [1, 16]], 0), (8, [[1, 16], [0, 16]], 1), (12, [[0, 256]], 2)):
+                src = A(("M1", "M2", "C2")[k]) if nm == "VT" else A(("CS", "TE", "TE")[k], 256 * (k // 2), 256 * (k // 2) + 256)
+                iota(src, pattern, 64, 0)
+                rows(nm, 0, r, src)
+        ts(A("KI"), A("ZB", 0, 256), pc(0), 64.0, OP.add, OP.add)
+        rows("VT", 0, 4, A("KI"))
+        ts(A("K2", 4, 260), A("ZB", 0, 256), pc(0), 64.0, OP.add, OP.add)
+        rows("ST", 0, 4, A("K2", 4, 260))
 
-    def exts(buf, off, h, out, s, k=8, start=True, stop=True):
+    def exts(buf, off, h, b, c0, s, k=8, start=True, stop=True):
         for i in range(16):
-            mm(A(out, i, i + (k - 1) * 16 + 1, 16), A(buf, off + 2048 * h + i, off + 2048 * h + 2048, 16), sel(s, k),
-               start, stop if stop is True else (stop == "last" and i == 15))
+            mm(P(b, c0 + i, c0 + i + (k - 1) * 16 + 1, 16), A(buf, off + 2048 * h + i, off + 2048 * h + 2048, 16),
+               sel(s, k), start, stop if stop is True else (stop == "last" and i == 15))
 
-    def maxcarry(col):
-        mm(A("P4", 0, 128, 1, 0, 1), col, A("SHD"))
-        scan(A("CROW", 0, 128, 1, 0, 1), A("MROW", 0, 128, 1, 0, 1), A("P4", 0, 128, 1, 0, 1), OP.mult, OP.max)
-        mm(A("P5", 0, 1), A("CROW", 0, 128, 1, 0, 1), A("ONE", 0, 1, 1, 0, 1))
-        return A("P5", 0, 1)
+    def carry(outs_, cols, dec=None):
+        k = len(cols)
+        for j, col in enumerate(cols):
+            ts(A("RH", 16 * j, 16 * j + 16), A("MSK"), col, None, OP.mult)
+        terms = [(P(4, 0, 16 * k), A("TRI"), A("RH", 0, 16 * k))]
+        if dec is not None:
+            terms += [(P(4, 16 * j, 16 * j + 16), IDF, A("DEC", dec, dec + 16)) for j in range(k)]
+        mms(*terms)
+        for j, o in enumerate(outs_):
+            most(o, P(4, 16 * j, 16 * j + 16))
 
-    def sumcarry(col):
-        mm(A("P5", 8, 9), A("TRI"), col)
-        return A("P5", 8, 9)
+    rid, pid, _se = topo.addr(nxt)
+    mask = topo.mask(core, nxt)
+    ne, nb = len(topo.engines(core, nxt)), len(topo.engines(prv, core))
 
-    def split(hi, lo, src):
-        cp(hi, src)
-        tt(lo, src, hi, OP.subtract)
+    def send(src, dst, ss, rs):
+        sa, da = A(src), T[dst][:]
+        op("g", lambda: g.remote_dma(da, sa[0], T.sem[rs], T.sem[ss], pid, rid, mask), sa[1], [], remote=(ss, ne))
+        total[rs] = nb
+        hist[dst] = [{"reg": (0, 128, 1, 0, 256, 1), "w": True, "q": "remote", "sem": rs, "val": nb, "vc": {}, "n": 0,
+                      "dma": True}]
+
+    def tables():
+        mm(P(4, 0, 1), A("SHU"), A("EB", 0, 1))
+        tt(P(7), P(6), A("AT1"), OP.subtract)
+        ts(P(6, 256, 257), P(4, 0, 1), pc(5), None, OP.add)
+        tt(A("TD"), P(6, 1, 257), A("AT1"), OP.subtract)
+        tt(P(5), P(7), A("TD"), OP.is_gt)
+        act(A("TC"), P(7), AF.Relu, pc(6), -1.0)
+        tt(P(5, 256, 512), P(5), A("TD"), OP.mult)
+        act(A("NB"), P(7), AF.Copy, None, BIG)
+        tt(P(5), P(5, 256, 512), A("TC"), OP.subtract)
+        cp(A("DHI"), P(5))
+        rows("KT", 1, 3, A("DHI"), "s")
+        tt(A("DLO"), P(5), A("DHI"), OP.subtract)
+        rows("KT", 1, 4, A("DLO"), "y")
+
+    def tables2():
+        tt(A("TC"), P(5), A("AT1"), OP.add)
+        cp(A("BLB"), A("TC"))
+        ts(P(7, 256, 512), P(7), 4.0, 4.0, OP.mult, OP.add)
+        tt(A("LEN"), P(7, 256, 512), A("NB"), OP.min)
+        for k in range(4):
+            dma(A("HM", 66 * k, 66 * k + 64), A("NB", 0, 256, 1, 32 * k, 32 * k + 32))
+
+    cp(P(6), A("VI"))
+    cp(A("EB"), A("VI"))
+    tables()
+    late_constants()
 
     for t in range(2):
         X, XO = "XW%d" % t, "XW%d" % (1 - t)
-        if t == 0:
-            cp(A("EB", 0, 256), A("VI"))
-        mm(A("P4", 0, 1), A("SHU"), A("EB", 0, 1))
-        tt(A("NHB"), A("EB", 0, 256), A("AT1"), OP.is_gt)
-        rows("KT", 0, 2, A("NHB"), "y")
-        ts(A("EB", 256, 257), A("P4", 0, 1), pc(5), None, OP.add)
-        tt(A("TC"), A("EB", 1, 257), A("EB", 0, 256), OP.is_lt)
-        tt(A("TD"), A("EB", 1, 257), A("AT1"), OP.subtract)
-        tt(A("TD"), A("TD"), A("TC"), OP.mult)
-        cp(A("DHI"), A("TD"))
-        rows("KT", 0, 3, A("DHI"), "s")
-        tt(A("DLO"), A("TD"), A("DHI"), OP.subtract)
-        rows("KT", 0, 4, A("DLO"), "y")
-        for h in range(2):
-            cp(half("VL", h), half("HI", h))
-        tt(A("TC"), A("TD"), A("AT1"), OP.add)
-        ts(A("BLB"), A("TC"), 15.0, None, OP.add)
-        ts(A("ELB"), A("EB", 0, 256), -1.0, None, OP.add)
-        if t == 0:
-            late_constants()
 
-        def xa(h):
-            tt(A("WB", 4096 + 2048 * h, 6144 + 2048 * h), IND(X, 16, 4112, "VL", 128 * h, 128 * h + 128),
-               A("W", 2048 * h, 2048 * h + 2048), OP.min)
-            mm(A("P%d" % h, 0, 128), zb(128), zb(128), True, False)
-            exts("WB", 4096, h, "P%d" % h, S_P, 8, False, False)
+        def xg(lst, off, h, a, b):
+            tt(A("WB", off + 2048 * h + 16 * a, off + 2048 * h + 16 * b), IND(X, 0, 4112, lst, 128 * h + a, 128 * h + b),
+               A("W", 2048 * h + 16 * a, 2048 * h + 16 * b), OP.min)
 
-        def xb(h):
-            tt(A("WB", 8192 + 2048 * h, 10240 + 2048 * h), IND("XB", 0, 4096, "VL", 128 * h, 128 * h + 128),
-               A("W", 2048 * h, 2048 * h + 2048), OP.min)
-            exts("WB", 8192, h, "P%d" % h, S_M, 8, False, "last")
+        def xa(h, a=0, b=128):
+            xg("VL", 8192, h, a, b)
+            if b == 128:
+                mm(P(h, 0, 128), zb(128), zb(128), True, False)
+                exts("WB", 8192, h, h, 0, S_P, 8, False, False)
+
+        def xb(h, a=0, b=128):
+            xg("VB", 12288, h, a, b)
+            if b == 128:
+                exts("WB", 12288, h, h, 0, S_M, 8, False, "last")
 
         def kid(h):
-            act(A("WB", 12288 + 2048 * h, 14336 + 2048 * h), IND("KT", 0, 4096, "VL", 128 * h, 128 * h + 128))
-            exts("WB", 12288, h, "P%d" % (2 + h), S_A, 24)
+            act(A("XB", 2048 * h, 2048 * h + 2048), IND("KT", 0, 4112, "VL", 128 * h, 128 * h + 128))
 
-        def small(h, last):
-            ts(half("TA", h), A("P%d" % h, 0, 128), 0.0, None, OP.is_gt)
-            tt(half("TB", h), A("P%d" % (2 + h), 128, 256), half("TA", h), OP.mult)
-            tt(half("VI" if last else "TC", h), A("P%d" % (2 + h), 0, 128), half("TB", h), OP.add)
-            if not last:
-                tr(A("P%d" % (4 + h), 0, 128), half("TC", h))
-
-        def relist(h):
-            cp(half("VL", h), A("P%d" % (4 + h), 0, 128))
-
-        for h in range(2):
-            exts("KT", 0, h, "P%d" % (4 + h), S_B)
-        kid(0)
-        xa(0)
-        xa(1)
-        for h in range(2):
-            ts(half("TD", h), A("P%d" % (4 + h), 0, 128), 16.0, None, OP.add)
-            tr(A("P%d" % (6 + h), 0, 128), half("TD", h))
-        ts(A("KEY"), A("EB", 0, 256), 4096.0, None, OP.mult)
-        tt(A("KEY"), A("KEY"), A("AT1"), OP.subtract)
-        for h in (1, 0):
-            cp(half("BLW", h), A("P%d" % (6 + h), 0, 128))
-        act(A("XB", 2048, 4096), IND(X, 0, 4112, "BLW", 128, 256))
-        kid(1)
-        cp(A("XB", 0, 2048), IND(X, 0, 4112, "BLW", 0, 128))
-        xb(0)
-        xb(1)
-        small(0, False)
-        tt(A("KEY"), A("KEY"), A("NHB"), OP.mult)
-        ts(A("HMB"), A("NHB"), -BIG, BIG, OP.mult, OP.add)
-        for q in range(8):
-            dma(A("HM", 66 * q, 66 * q + 64, 1, 0, 64), A("HMB", 0, 256, 1, 16 * q, 16 * q + 16))
-        iota(A("WB", 0, 4096), [[0, 4096]], 0, 0)
-        iota(A("WF", 0, 4096), [[0, 4096]], 0, 0)
-        relist(0)
-        for s in range(1, 4):
-            xa(0)
-            kid(0)
-            small(1, False)
-            xb(0)
-            relist(1)
-            xa(1)
-            kid(1)
-            if s == 1:
-                act(half("HIT", 0), A("P2", 256, 384))
-                act(half("HIT", 1), A("P3", 256, 384))
-            small(0, s == 3)
-            xb(1)
+        def kids(h, s):
+            exts("XB", 0, h, 2 + h, 0, S_K, 24)
+            act(A("FS", 256 * h, 256 * h + 256), P(2 + h))
+            mm(P(6 + h, 0, 128), A("FS", 256 * h, 256 * h + 128), IDF)
             if s < 3:
-                relist(0)
-                o = 4112 if s == 1 else 8208
-                act(A(X, o, o + 4096), A(X, 15, 4111), AF.Relu, pc(9 + s))
+                mm(P(4 + h, 0, 128), A("FS", 256 * h + 128, 256 * h + 256), IDF, True, False)
+            else:
+                mm(P(4 + h, 0, 128), IDF, A("FS", 256 * h + 128, 256 * h + 256), True, False)
+            if s == 1:
+                act(half("NOH", h), P(2 + h, 256, 384), AF.Relu, None, -1.0)
 
-        for b in range(4, 8):
-            mm(A("P%d" % b, 0, 264, 1, 0, 65), zb(65), zb(264), True, False)
-        slot, slot2 = 0, 0
+        def relu(h):
+            act(half("TA", h), P(h, 0, 128), AF.Relu)
+
+        def choose(h, s):
+            tt(half("TB", h), P(2 + h, 256, 384), half("TA", h), OP.min)
+            if s < 3:
+                mm(P(4 + h, 0, 128), half("TB", h), IDF, False, True)
+            else:
+                mm(P(4 + h, 0, 128), IDF, half("TB", h), False, True)
+
+        vl = lambda h: ts(half("VL", h), P(4 + h, 0, 128), 1.0, None, OP.add)
+        vb = lambda h: cp(half("VB", h), P(6 + h, 0, 128))
+
+        def digits(h):
+            ts(half("AQ", h), P(4 + h, 0, 128), 1.0 / 64, 160 - 31.5 / 64, OP.mult, OP.add)
+            f3 = A("FS", 256 * h + 128, 256 * h + 256)
+            mms((P(6 + h), A("ROW", 0, 128), A("ROW", 128, 384)),
+                (P(6 + h, 128, 256), IDF, f3), (P(6 + h, 128, 256), IDF, half("TB", h)),
+                (P(6 + h, 128, 256), cm(P64), half("NOH", h)),
+                (P(6 + h, 0, 128), cm(IB), half("AQ", h)), (P(6 + h, 128, 256), cm(N64), half("AQ", h)))
+            for b in (h, 2 + h):
+                mm(P(b, 0, 264), zb(128), zb(264), True, False)
+
+        slots = [0, 0]
+
+        def column(h, q, i):
+            c = 256 * h + 16 * q + i
+            s1, s2 = A("S12", c, c + 1), A("S12", c + 128, c + 129)
+            if i in SCOL:
+                o, b, last = 7800 + 130 * (slots[1] % 32), 2 + h, SCOL[-1]
+                slots[1] += 1
+                act(A(XO, o, o + 64), A("CR", 130, 194), AF.Relu, s1, -1.0)
+                act(A(XO, o + 64, o + 130), A("CR", 64, 130), AF.Relu, s2, -1.0)
+            else:
+                o, b, last = 130 * (slots[0] % 60), h, max(k for k in range(16) if k not in SCOL)
+                slots[0] += 1
+                ts(A(XO, o, o + 130), A("CR", 0, 130), s1, s2, OP.max, OP.min)
+            mm(P(b, 66 * (q // 2), 66 * (q // 2) + 66, 1, 64 * (q % 2), 64 * (q % 2) + 64), A(XO, o, o + 64),
+               A(XO, o + 64, o + 130), False, i == last and q >= 6)
+
+        def differences(h):
+            mm(P(4, 0, 264), A("DFV"), A("SCV"), h == 0, False)
+            mm(P(4, 0, 264), A("DFS"), A("SCS"), False, h == 1)
+
         for h in range(2):
-            if h == 1:
-                small(1, True)
-            ts(half("HI", h), half("VI", h), 6, None, OP.arith_shift_right)
-            ts(half("TA", h), half("HI", h), -64.0, None, OP.add)
-            ts(half("HI", h), half("VI", h), 63, None, OP.bitwise_and)
-            ts(half("S2", h), half("HI", h), 1.0, None, OP.add)
-            tt(half("S1", h), half("TA", h), half("HIT", h), OP.mult)
+            ts(half("VL", h), half("HI", h), 1.0, None, OP.add)
+        for s in range(4):
+            if s == 0:
+                kid(0)
+                xa(0)
+                kids(0, s)
+                kid(1)
+                xa(1)
+                tables2()
+            else:
+                relu(1)
+                kid(0)
+                xa(0, 0, 96)
+                choose(1, s - 1)
+                xa(0, 96, 128)
+                vl(1)
+                kids(0, s)
+                kid(1)
+                xa(1)
+            vb(0)
+            kids(1, s)
+            xb(0)
+            vb(1)
+            relu(0)
+            xb(1, 0, 96)
+            choose(0, s)
+            if s == 3:
+                digits(0)
+                act(A("S12", 0, 256), P(6))
+            xb(1, 96, 128)
+            if s < 3:
+                vl(0)
+            if s == 0:
+                if t == 0:
+                    late_constants_v()
+                    scatter_data()
+                iota(A("WB", 0, 8192), [[0, 8192]], 0, 0)
+                iota(A("WF", 0, 8192), [[0, 8192]], 0, 0)
+        relu(1)
+        for h in range(2):
             for q in range(8):
                 for i in range(16):
-                    c = 128 * h + 16 * q + i
-                    if i % 4 == 3:
-                        o, b, last = 7860 + 131 * (slot2 % 30), 4, 15
-                        slot2 += 1
-                        act(A(XO, o, o + 65), A("CR", 0, 65), AF.Relu, A("S1", c, c + 1), -1.0)
-                        act(A(XO, o + 65, o + 131), A("CR", 65, 131), AF.Relu, A("S2", c, c + 1), -1.0)
-                    else:
-                        o, b, last = 131 * (slot % 60), 6, 14
-                        slot += 1
-                        ts(A(XO, o, o + 131), A("CR", 0, 131), A("S1", c, c + 1), A("S2", c, c + 1), OP.max, OP.min)
-                    mm(A("P%d" % (b + q // 4), 66 * (q % 4), 66 * (q % 4) + 66, 1, 0, 65), A(XO, o, o + 65),
-                       A(XO, o + 65, o + 131), False, h == 1 and i == last and q % 4 == 3)
+                    column(h, q, i)
+                if h == 0 and q == 0:
+                    choose(1, 3)
+                if h == 0 and q == 1:
+                    digits(1)
+                if h == 0 and q == 3:
+                    cp(A("S12", 256, 512), P(7))
+                if h == 1 and q == 1:
+                    act(A("SCS"), P(2, 0, 264))
+                    cp(A("SCV"), P(0, 0, 264))
+                if h == 1 and q == 2:
+                    differences(0)
         if t == 0:
             dma(A("HI"), IO("start", slice(0, 128), slice(256, 512)), "y")
-        act(A("SC", 0, 264), A("P6", 0, 264, 1, 0, 65))
-        cp(A("SC", 264, 528), A("P7", 0, 264, 1, 0, 65))
-        tt(A("SC", 264, 528), A("SC", 264, 528), A("P5", 0, 264, 1, 0, 65), OP.subtract)
-        tt(A("SC", 0, 264), A("SC", 0, 264), A("P4", 0, 264, 1, 0, 65), OP.subtract)
-        tt(A("D1", 0, 527), A("SC", 1, 528), A("SC", 0, 527), OP.subtract)
-        tt(A("SC", 0, 526), A("D1", 0, 526), A("D1", 1, 527), OP.subtract)
-        for b, (c0, c1) in enumerate(((0, 264), (264, 526))):
-            mm(A("P%d" % (6 + b), 0, c1 - c0, 1, 0, 64), A("DF", 0, 64, 1, 0, 65), A("SC", c0, c1))
-            tt(A("FL", c0, c1), A("P%d" % (6 + b), 0, c1 - c0, 1, 0, 64), A("HM", c0, c1, 1, 0, 64), OP.mult)
-        for q in range(8):
-            dma(A(XO, 15, 4111, 1, 16 * q, 16 * q + 1), A("FL", 66 * q, 66 * q + 64), "y" if q % 2 else "s")
-        dma(A("HB"), A(XO, 15, 4111, 1, 0, 128, 16), "y")
-        dma(A("HB1"), A(XO, 16, 4112, 1, 0, 128, 16), "y")
+        act(A("SCS"), P(3, 0, 264))
+        cp(A("SCV"), P(1, 0, 264))
+        differences(1)
+        act(A("Z2"), P(4, 0, 264), AF.Copy, None, 2.0)
+        tt(A("D1", 0, 262), P(4, 0, 262), A("Z2", 1, 263), OP.subtract)
+        tt(P(5, 0, 262), P(4, 2, 264), A("D1", 0, 262), OP.add)
+        tt(A("FL", 0, 262), P(5, 0, 262), A("HM", 0, 262), OP.is_gt)
+        for k in range(4):
+            dma(A(XO, 0, 4096, 1, 32 * k, 32 * k + 32, 16), A("FL", 66 * k, 66 * k + 64), "ys"[k % 2])
+        for k in range(4):
+            dma(A("HB", 0, 256, 1, 32 * k, 32 * k + 32), A("FL", 66 * k, 66 * k + 64), "ys"[k % 2])
+        copy = lambda c: ts(A(X, c * ZC, c * ZC + 4096), A(X, 0, 4096), -float(c), 0.0, OP.add, OP.max)
+        copy(1)
 
-        act(A(XO, GB, GB + 2048), IND(XO, 0, 4112, "BLB", 0, 128))
-        cp(A(XO, GB + 2048, GB + 4096), IND(XO, 0, 4112, "BLB", 128, 256))
-        for h in range(2):
-            exts(XO, GB, h, "P%d" % h, S_0)
-        if t == 0:
-            st2()
-        ts(A("KEEP"), A("HB"), 0.0, None, OP.is_le)
-        fill(A("TE"), 0.0)
-        scan(A("TA"), A("KEEP"), A("TE"), OP.add, OP.add)
-        k0 = sumcarry(A("TA", 255, 256))
-        for h in range(2):
-            ts(half("TB", h), A("P%d" % h, 0, 128), 0.0, BIG, OP.is_gt, OP.mult)
-            tr(A("P2", 128 * h, 128 * h + 128), half("TB", h))
-        ts(A("TA"), A("TA"), k0, None, OP.add)
-        split(A("PHI"), A("PLO"), A("TA"))
+        act(A("XB", 2048, 4096), IND(XO, 0, 4096, "BLB", 128, 256))
+        cp(A("XB", 0, 2048), IND(XO, 0, 4096, "BLB", 0, 128))
+        for h in (1, 0):
+            exts("XB", 0, h, h, 0, S_0)
+        ts(A("KP2"), A("HB"), -2.0, 2.0, OP.mult, OP.add)
+        scan(A("K2", 1, 257), A("KP2"), zb(256), OP.add, OP.add)
+        ts(A("KP4"), A("HB"), -4.0, 4.0, OP.mult, OP.add)
+        act(half("M1", 1), P(1, 0, 128))
+        cp(half("M1", 0), P(0, 0, 128))
+        mms((P(2), zb(128), zb(256)), (P(2, 0, 255), cm(BI), A("HB", 1, 256)), (P(2, 255, 256), cm(BSU), A("HB", 0, 1)),
+            (P(2, 128, 256), half("M1", 1), cm(BI)), (P(2, 0, 128), half("M1", 0), cm(BI)))
+        tt(A("TC"), P(2), A("LEN"), OP.min)
+        ng4 = A("NG", 512, 768)
+        scan(A("TA"), ng4, A("TC"), OP.add, OP.max)
+        carry([P(3, 0, 1)], [A("TA", 255, 256)], 16)
+        mms((P(7), IDF, A("AM")), (P(7), cm(I4K), A("HB")))
+        scan(P(3, 1, 257), ng4, A("TC"), OP.add, OP.max, P(3, 0, 1))
+        tt(A("KI"), P(3, 1, 257), A("KP4"), OP.min)
+        ts(P(5), P(3), 4.0, BIG, OP.is_gt, OP.mult)
+        act(A("INS"), P(3, 1, 257), AF.Sign)
+        scan(A("I4", 1, 257), A("KI"), zb(256), OP.add, OP.add)
+        mms((P(4, 32, 33), A("TRI"), A("I4", 256, 257)), (P(4, 32, 33), A("TRI"), A("K2", 256, 257)))
+        mm(P(4, 33, 34), A("TRI"), A("K2", 256, 257))
+        tt(A("TA"), P(5), A("I4", 0, 256), OP.subtract)
+        scan(A("TB"), A("TA"), A("TA"), OP.min, OP.min, BIG)
+        cp(A("CC", 0, 2), P(4, 32, 34))
+        ts(cc(2), A("TB", 255, 256), -1.0, cc(0), OP.mult, OP.add)
+        ts(cc(2), cc(2), cc(1), None, OP.subtract)
+        ts(A("RH", 0, 16), A("MSK"), cc(2), None, OP.mult)
+        mm(P(4, 0, 16), A("TRI"), A("RH", 0, 16))
+        tt(A("TOP"), P(5), A("TC"), OP.is_lt)
+        mms((P(6), IDF, A("K2", 0, 256)), (P(6), cm(BI), A("HB")), (P(6), cm(IB), A("TOP")))
+        mms((P(2), IDF, A("EB")), (P(2), cm(I4K), A("INS")))
+        most(cc(3), P(4, 0, 16))
+        ts(cc(3), cc(3), -1.0, cc(1), OP.mult, OP.subtract)
+        ts(A("TD"), A("TB"), cc(0), cc(3), OP.subtract, OP.min)
+        tt(A("TA"), P(6), A("TD"), OP.subtract)
+        tt(A("TA"), P(7), A("TA"), OP.min)
+        cp(A("QL"), A("TA"))
+        act(IND("WF", 0, 16384, "QL", VS, 256), A("ST", 16 * VS, 4096), AF.Silu)
+        ts(A("ELB"), P(2), -1.0, None, OP.add)
+        tt(P(5), A("K2", 1, 257), A("TD"), OP.subtract)
+        tt(P(3), A("K2", 1, 257), A("I4", 1, 257), OP.add)
+        cp(A("DHI"), P(5))
+        tt(A("DLO"), P(5), A("DHI"), OP.subtract)
+        rows(XO, KM + 4096, 0, A("DHI"), "y")
+        rows(XO, KM + 4096, 1, A("DLO"), "y")
+        ts(P(3), P(3), cc(0), None, OP.add)
+        cp(A("PHI"), P(3))
+        tt(A("PLO"), P(3), A("PHI"), OP.subtract)
         rows(XO, KM, 0, A("PHI"), "y")
         rows(XO, KM, 1, A("PLO"), "y")
-        tt(A("KEX"), A("TA"), A("KEEP"), OP.subtract)
-        tt(A("TC"), A("P2", 0, 256), A("HB1"), OP.add)
-        tt(A("TC"), A("TC"), A("KEY"), OP.min)
-        scan(A("R"), A("TC"), A("TC"), OP.max, OP.max)
-        c = maxcarry(A("R", 255, 256))
-        ts(A("R"), A("R"), c, None, OP.max)
-        tt(A("INS"), A("R"), A("ATK"), OP.is_ge)
-        tt(A("KI"), A("KEEP"), A("INS"), OP.mult)
-        scan(A("TA"), A("KI"), A("TE"), OP.add, OP.add)
-        c = sumcarry(A("TA", 255, 256))
-        tt(A("TOP"), A("R"), A("TC"), OP.is_equal)
-        tt(A("TOP"), A("TOP"), A("INS"), OP.mult)
-        ts(A("TA"), A("TA"), c, None, OP.add)
-        split(A("DHI"), A("DLO"), A("TA"))
-        rows(XO, KM, 2, A("DHI"), "y")
-        rows(XO, KM, 3, A("DLO"), "y")
-        for h in range(2):
-            act(A(XO, GB + 2048 * h, GB + 2048 * h + 2048), IND(XO, KM, KM + 4096, "ELB", 128 * h, 128 * h + 128))
-        tt(A("IEX"), A("TA"), A("KI"), OP.subtract)
-        tt(A("TB"), A("TOP"), A("IEX"), OP.mult)
-        scan(A("IH"), A("TB"), A("TB"), OP.max, OP.max)
-        c = maxcarry(A("IH", 255, 256))
-        ts(A("IH"), A("IH"), c, None, OP.max)
-        tt(A("TB"), A("IH"), A("IEX"), OP.subtract)
-        tt(A("TB"), A("TB"), A("INS"), OP.mult)
-        tt(A("TB"), A("TB"), A("IEX"), OP.add)
-        ts(A("TB"), A("TB"), 2.0, None, OP.mult)
-        tt(A("TB"), A("TB"), A("KEX"), OP.add)
-        ts(A("TD"), A("AT1"), 12287.0, None, OP.add)
-        tt(A("TB"), A("TB"), A("TD"), OP.subtract)
-        tt(A("TC"), A("TB"), A("KEEP"), OP.mult)
-        tt(A("TC"), A("TC"), A("TD"), OP.add)
-        cp(A("QL0"), A("TC"))
-        sc0 = lambda k: cp(IND("WB", 0, 16384, "QL0", 64 * k, 64 * k + 64), A("VT0", 1024 * k, 1024 * k + 1024))
-        sc2 = lambda k: cp(IND("WB", 0, 16384, "QL2", 64 * k, 64 * k + 64), A("VT2", 1024 * k, 1024 * k + 1024))
-        sc0(0)
-        tt(A("TB"), A("TB"), A("KI"), OP.mult)
-        tt(A("Q0M"), A("TB"), A("TD"), OP.add)
-        ts(A("TE"), A("INS"), -2.0, 2.0, OP.mult, OP.add)
-        for h in range(2):
-            exts(XO, GB, h, "P%d" % h, S_K, 16)
-        for h in range(2):
-            cp(half("TA", h), A("P%d" % h, 128, 256))
-            tr(A("P2", 128 * h, 128 * h + 128), half("TA", h))
-        for h in range(2):
-            cp(half("TB", h), A("P%d" % h, 0, 128))
-            tr(A("P3", 128 * h, 128 * h + 128), half("TB", h))
-        tt(A("TC"), A("P2", 0, 256), A("TOP"), OP.mult)
-        scan(A("R"), A("TC"), A("TC"), OP.max, OP.max)
-        c = maxcarry(A("R", 255, 256))
-        tt(A("TD"), A("P2", 0, 256), A("IEX"), OP.subtract)
-        tt(A("TD"), A("TD"), A("TE"), OP.mult)
-        ts(A("R"), A("R"), c, None, OP.max)
-        tt(A("R"), A("R"), A("IH"), OP.subtract)
-        tt(A("R"), A("R"), A("KI"), OP.mult)
-        tt(A("TC"), A("Q0M"), A("R"), OP.add)
-        cp(A("QL1"), A("TC"))
-        for k in range(4):
-            act(IND("WF", 0, 16384, "QL1", 64 * k, 64 * k + 64), A("ST1", 1024 * k, 1024 * k + 1024), AF.Silu)
-        tt(A("TC"), A("TC"), A("R"), OP.add)
-        cp(A("QL2"), A("TC"))
-        tt(A("TA"), A("P3", 0, 256), A("KEX"), OP.subtract)
-        tt(A("TA"), A("TA"), A("TD"), OP.add)
-        split(A("PHI"), A("PLO"), A("TA"))
-        act(IND("WF", 0, 16384, "QL2", 192, 256), A("ST2"), AF.Silu)
-        for k in range(1, 4):
-            sc0(k)
-        for k in range(3):
-            sc2(k)
-        for k in range(3):
-            o = 4096 + (15, 4112, 8208)[k]
-            rows("WB", o, 0, A("PHI"), "y")
-            rows("WB", o, 1, A("PLO"), "y")
-        act(A("XB", 2048, 4096), A("WF", 2048, 4096))
-        act(A("XB", 0, 2048), A("WF", 0, 2048))
-        for h in (1, 0):
-            mm(A("P%d" % h, 0, 128), zb(128), zb(128), True, False)
-            exts("XB", 0, h, "P%d" % h, S_01, 8, False, False)
-        for h in (1, 0):
-            exts("WB", 0, h, "P%d" % h, S_01, 8, False, "last")
-        for h in (1, 0):
-            ts(half("TB", h), A("P%d" % h, 0, 128), 15.0, None, OP.add)
-            tr(A("P%d" % (2 + h), 0, 128), half("TB", h))
-            cp(half("VL", h), A("P%d" % (2 + h), 0, 128))
-        LX, ES, RE = ["%s%d" % (nm, t) for nm in ("LX", "ES", "RE")]
-        dx = 15 if t == 0 else 0
-        SZ = lambda a, b: IND("WB", 4096, 16400, "VL", a, b)
-        XI = lambda a, b: IND(X, 0, 12304, "VL", a, b)
-        cp(A("TX"), XI(240, 256))
-        act(A(XO, GB + 3840, GB + 4096), SZ(240, 256))
-        for h in range(2):
-            mm(A("P4", 8 * h, 8 * h + 8), A(XO, GB + 3840 + 128 * h, GB + 3968 + 128 * h), sel(S_01))
-        tt(A(ES), A("P4", 0, 16), A("QT", 15, 256, 16), OP.add)
-        ts(A(ES), A(ES), 4096.0, None, OP.min)
-        rid, pid, _se = topo.addr(nxt)
-        m = topo.mask(core, nxt)
-        ne, nb = len(topo.engines(core, nxt)), len(topo.engines(prv, core))
+        cp(IND("WB", 0, 16384, "QL", 0, VS), A("VT", 0, 16 * VS))
+        dma(A("FB"), A("WF", 0, 8192, 1, 12, 128, 16), "g")
+        dma(A("FA"), A("WB", 0, 8192, 1, 12, 128, 16), "y")
+        src = A("WF", 0, 8192, 1, 0, 128, 4)
+        dma(A("WB", 0, 8192, 1, 1, 128, 4), (src[0], src[1] + A("FA")[1]), "g")
+        act(A("XB"), IND(XO, KM, KM + 8192, "ELB", 0, 256))
+        copy(2)
 
-        def send(src, dst, ss, rs):
-            sa, da = A(src), T[dst][:]
-            op("g", lambda: g.remote_dma(da, sa[0], T.sem[rs], T.sem[ss], pid, rid, m), sa[1], [], remote=(ss, ne))
-            total[rs] = nb
-            hist[dst] = [{"reg": (0, 128, 1, 0, 256), "w": True, "q": "remote", "sem": rs, "val": nb, "vc": {}, "n": 0,
-                          "dma": True}]
-        send("TX", LX, "xs%d" % t, "xr%d" % t)
+        mms((P(0, 0, 512), A("ROW", 0, 128, 1, 0, 1), A("ROW", 384, 896, 1, 0, 1)),
+            *[(P(0, 256 * k, 256 * k + 256), cm(I128), A(nm, o, 512, 2))
+              for nm in ("FA", "FB") for k, o in ((0, 0), (0, 1), (1, 1))])
+        scan(A("TE"), A("NG", 0, 512), P(0, 0, 512), OP.add, OP.max)
+        carry([cc(4), cc(5)], [A("TE", 255, 256), A("TE", 511, 512)], 0)
+        ng1 = A("NG", 0, 256)
+        scan(P(1), ng1, P(0), OP.add, OP.max, cc(4))
+        scan(A("TB"), ng1, P(0, 256, 512), OP.add, OP.max, cc(5))
+        tt(A("TA"), P(1), A("TB"), OP.subtract)
+        act(P(3), A("TB"), AF.Identity, pc(10), -2.0)
+        tt(A("TC"), P(1), A("TA"), OP.add)
+        act(A("M1"), P(1), AF.Sign, pc(9), -1.0)
+        ts(A("M2"), A("TC"), TOPB, None, OP.is_lt)
+        mms((P(2), cm(I2), A("M2")), (P(2), cm(I2), A("M1")))
+        tt(A("CS"), P(2), A("TA"), OP.mult)
+        act(A("C2"), P(2))
+        tt(P(1), P(3), A("CS"), OP.min)
+        tt(A("TC"), A("Q2"), P(1), OP.subtract)
+        cp(A("QL"), A("TC"))
+        act(A("WB", 10240, 12288), IND("WB", 0, 8192, "QL", 128, 256))
+        cp(A("WB", 8192, 10240), IND("WB", 0, 8192, "QL", 0, 128))
+        for r in range(16):
+            mm(P(7, 256 + r, 384, 16, 0, 16), A("C2", r, 256, 16), sel(S_C))
+        mm(P(0, 0, 512), zb(128), A("NG", 0, 512), True, False)
+        mm(P(0), cm(IZ), A("M1"), False, False)
+        mm(P(0), cm(IZ), A("M2"), False, False)
+        mm(P(4, 0, 32), zb(128), zb(32), True, False)
+        for h in (1, 0):
+            exts("WB", 8192, h, 5 + h, 0, S_J, 16)
+        act(A("FA", 256, 512), P(6))
+        cp(A("FA", 0, 256), P(5))
+        weights = ((1, 0, IB), (1, 1, I16), (0, 0, I256), (0, 1, IB), (0, 2, IZ))
+        for h in (1, 0):
+            for k, (l, d, wt) in enumerate(weights[:4]):
+                mm(P(0, 256 * l + 128 * h, 256 * l + 128 * h + 128), A("FA", 256 * h + 128 * d, 256 * h + 128 * d + 128),
+                   cm(wt), False, h == 0 and k == 3)
+            for r in range(8 - 8 * h, 16 - 8 * h):
+                mm(P(7, r, 256, 16, 0, 16), A("WB", 8192 + 16 * r + 15, 12288, 256), sel(S_J, 16))
+        cp(A("VB"), P(0, 256, 512))
+        act(A("FB", 0, 384, 1, 0, 16), P(7, 0, 384, 1, 0, 16))
+        for k, (l, d, wt) in enumerate(weights):
+            mm(P(4, 16 * l, 16 * l + 16), A("FB", 128 * d, 128 * d + 128, 1, 0, 16),
+               A("CM", 128 * wt, 128 * wt + 16, 1, 0, 16), False, k == 4)
+        cp(A("VL"), P(0))
+        LX, ES, RE = ["%s%d" % (nm, t) for nm in ("LX", "ES", "RE")]
+        SZ = lambda lst, a, b: IND("XB", 0, 4096, lst, a, b)
+        XI = lambda lst, a, b: IND(X, 0, 3 * ZC, lst, a, b)
+        act(A("WB", 14336, 16384), SZ("VB", 128, 256))
+        cp(A("L15"), P(4, 0, 32))
+        cp(A("TZ"), SZ("L15", 16, 32))
+        mms((P(4, 0, 16), zb(128), zb(16)),
+            *[(P(4, 8 * h, 8 * h + 8), half("CS", h), A("S15")) for h in range(2)],
+            *[(P(4, 8 * h, 8 * h + 8), half("TZ", h), sel(S_E)) for h in range(2)])
+        cp(A("TX"), XI("L15", 0, 16))
+        ts(A(ES), P(4, 0, 16), 4096.0, None, OP.min)
         send(ES, RE, "es%d" % t, "er%d" % t)
-        cp(A(XO, dx + 2048, dx + 3840), XI(128, 240))
-        act(A(XO, GB + 2048, GB + 3840), SZ(128, 240))
-        if t == 1:
-            dma(IO("y", slice(0, 128), slice(2048, 3840)), A(XO, dx + 2048, dx + 3840))
-        cp(A(XO, dx, dx + 2048), XI(0, 128))
-        act(A(XO, GB, GB + 2048), SZ(0, 128))
-        for i in list(range(8, 15)) + list(range(8)):
-            for h in range(2):
-                mm(A("P5", 128 * h + i, 128 * h + 113 + i, 16),
-                   A(XO, GB + 256 * i + 128 * h, GB + 256 * i + 128 * h + 128), sel(S_01))
-        for h in range(2):
-            mm(A("P5", 128 * h + 15, 128 * h + 128, 16), zb(128), zb(8))
+        send("TX", LX, "xs%d" % t, "xr%d" % t)
+        cp(A("WB", 12288, 14336), SZ("VB", 0, 128))
+        for h in (1, 0):
+            exts("WB", 12288, h, 5, 128 * h, S_E)
+        act(A(XO, KM + 2048, KM + 4096), XI("VL", 128, 256))
+        cp(A(XO, KM, KM + 2048), XI("VL", 0, 128))
+        act(A("TA"), P(5))
+        for i in range(15):
+            (act if i % 3 == 2 else cp)(A(XO, 256 * i, 256 * i + 256), A(XO, KM + i, KM + 4096, 16))
+            if t == 1 and i in (7, 14):
+                a = 0 if i == 7 else 2048
+                dma(IO("y", slice(0, 128), slice(a, 256 * i + 256)), A(XO, a, 256 * i + 256), "ys"[i % 2])
+            if i == 3:
+                cp(A("TA", 15, 256, 16), A(RE))
+                mms((P(7), A("IHF"), A("CS")), *[(P(7, 128 * h, 128 * h + 128), half("TA", h), IDF) for h in range(2)])
+            if i == 6:
+                ts(P(6), P(7), pc(3), None, OP.min)
+                act(A("EB"), P(6))
+                if t == 1:
+                    dma(IO("ye"), A("EB"))
         if t == 0:
-            cp(A(XO, 3855, 4111), A(LX))
+            tables()
+            cp(A(XO, 3840, 4096), A(LX))
         else:
-            dma(IO("y", slice(0, 128), slice(0, 2048)), A(XO, dx, dx + 2048))
             dma(IO("y", slice(0, 128), slice(3840, 4096)), A(LX))
-        tt(A("TA"), A("P5", 0, 256), A("QT"), OP.add)
-        ts(A("TA"), A("TA"), 3840.0, None, OP.min)
-        cp(A("TA", 15, 256, 16), A(RE))
-        for h in range(2):
-            tr(A("P6", 128 * h, 128 * h + 128), half("TA", h))
-        cp(A("EB", 0, 256), A("P6", 0, 256))
-        if t == 1:
-            dma(IO("ye"), A("EB", 0, 256))
 
     for s in sorted(total):
         if known["g"].get(s, 0) < total[s]:

@@ -10,12 +10,12 @@ SCRATCH = {
     "XB": ("sbuf", [128, 4096], BF), "W": ("sbuf", [128, 4096], BF), "KT": ("sbuf", [128, 4112], BF),
     "WB": ("sbuf", [128, 16384], BF), "WF": ("sbuf", [128, 16384], F32),
     "VT": ("sbuf", [128, 4096], BF), "ST": ("sbuf", [128, 4096], F32),
-    "ZB": ("sbuf", [128, 264], BF), "CR": ("sbuf", [128, 194], BF), "CM": ("sbuf", [128, 11 * 128], BF),
+    "ZB": ("sbuf", [128, 264], BF), "CR": ("sbuf", [128, 194], BF), "CM": ("sbuf", [128, 12 * 128], BF),
     "IDF": ("sbuf", [128, 128], F32), "SHU": ("sbuf", [128, 128], F32), "TRI": ("sbuf", [128, 128], F32),
     "IHF": ("sbuf", [128, 128], F32), "DFV": ("sbuf", [128, 128], F32), "DFS": ("sbuf", [128, 128], F32),
     "MSK": ("sbuf", [128, 16], F32), "DEC": ("sbuf", [128, 32], F32), "S15": ("sbuf", [128, 8], F32),
     "PI": ("sbuf", [128, 8], I32), "PC": ("sbuf", [128, 16], F32), "SEL": ("sbuf", [128, 88], BF),
-    "ROW": ("sbuf", [2, 896], BF), "NG": ("sbuf", [128, 768], BF),
+    "ROW": ("sbuf", [2, 640], BF), "NG": ("sbuf", [128, 768], BF), "SW": ("sbuf", [128, 256], F32),
     "AT1": ("sbuf", [128, 256], F32), "Q2": ("sbuf", [128, 256], F32),
     "AM": ("sbuf", [128, 256], F32), "EB": ("sbuf", [128, 256], F32),
     "DHI": ("sbuf", [128, 256], BF), "DLO": ("sbuf", [128, 256], BF),
@@ -24,8 +24,7 @@ SCRATCH = {
     "BLB": ("sbuf", [128, 256], U16), "ELB": ("sbuf", [128, 256], U16), "VL": ("sbuf", [128, 256], U16),
     "VB": ("sbuf", [128, 256], U16), "QL": ("sbuf", [128, 256], U16), "L15": ("sbuf", [128, 32], U16),
     "TA": ("sbuf", [128, 256], F32), "TB": ("sbuf", [128, 256], F32), "TC": ("sbuf", [128, 256], F32),
-    "TD": ("sbuf", [128, 256], F32), "TE": ("sbuf", [128, 512], F32), "LEN": ("sbuf", [128, 256], F32),
-    "FS": ("sbuf", [128, 512], F32), "VI": ("sbuf", [128, 256], I32), "HI": ("sbuf", [128, 256], I32),
+    "TD": ("sbuf", [128, 256], F32), "VI": ("sbuf", [128, 256], I32), "HI": ("sbuf", [128, 256], I32),
     "AQ": ("sbuf", [128, 256], BF), "NOH": ("sbuf", [128, 256], BF), "S12": ("sbuf", [128, 512], BF),
     "HB": ("sbuf", [128, 256], BF), "KP2": ("sbuf", [128, 256], BF), "KP4": ("sbuf", [128, 256], BF),
     "KI": ("sbuf", [128, 256], BF), "INS": ("sbuf", [128, 256], BF), "TOP": ("sbuf", [128, 256], BF),
@@ -42,13 +41,16 @@ for _k in range(8):
 SEMAPHORES = ["qv", "qs", "qt", "qg"] + ["d%d" % k for k in range(NDMA)]
 SEMAPHORES += ["%s%d" % (a, k) for a in ("xs", "xr", "es", "er") for k in range(2)]
 
-ALIAS = {"SCV": (8192, 264), "SCS": (8456, 264), "Z2": (8720, 264), "D1": (8984, 264)}
+ALIAS = {"SCV": (8192, 264), "SCS": (8456, 264), "Z2": (8720, 264), "D1": (8984, 264), "TE": (9248, 512),
+         "LEN": (9760, 256), "FS": (10016, 512)}
 S_P, S_M, S_K, S_0, S_J, S_E, S_C = 0, 8, 16, 40, 48, 64, 72
-CMS = (1.0, -64.0, 64.0, 32768.0, 32768.0, 128.0, 2.0, float(ZC), 4096.0, 256.0, 16.0)
-IB, N64, P64, BI, BSU, I128, I2, IZ, I4K, I256, I16 = range(11)
+CMS = (1.0, -64.0, 64.0, 32768.0, 32768.0, 128.0, 2.0, float(ZC), 4096.0, 256.0, 16.0, -1.0)
+IB, N64, P64, BI, BSU, I128, I2, IZ, I4K, I256, I16, NI = range(12)
 BIG, TOPB = 32768.0, 8192.0
 KM = 4112
-VS = 128
+VS = (146, 128)
+VA = 96
+XS = 56
 SCOL = (3, 7, 11, 15)
 
 
@@ -225,45 +227,64 @@ def rank_program(g, core, T, topo):
         pick(A(nm), [[-k, 128 // k], [0, k]], OP.is_ge, 0.0, 0, 1)
         pick(A(nm), [[k, 128 // k], [0, k]], OP.is_ge, 0.0, k - 1, -1)
 
+    zero = lambda o, v=0: iota(o, [[0, o[1][0][1][4] - o[1][0][1][3]]], v, 0)
     iota(A("PI", 0, 1), [[0, 1]], 0, 1, False)
-    iota(A("TA"), [[1, 256]], 0, 0)
+    iota(A("TA"), [[1, 256]], 1, 0)
+    zero(A("SHU"))
+    pick(A("SHU"), [[-1, 128]], OP.not_equal, 1.0, -1, 1)
     iota(A("TB"), [[0, 2], [1, 128]], 1, 0)
     iota(A("TC"), [[128, 2], [0, 128]], 0, 0)
     fill(A("KT"), 0.0)
-    for nm, v in (("SHU", 0.0), ("SEL", 0.0), ("IDF", 0.0), ("TRI", 1.0), ("DFV", 0.0), ("DFS", 0.0), ("ZB", 0.0),
-                  ("S15", 0.0), ("HM", 0.0)):
-        fill(A(nm), v)
-    for c in range(3):
-        fill(A("XW0", c * ZC + 4096, c * ZC + ZC), 0.0)
-    fill(sel(S_P), 4096.0)
-    fill(sel(S_M), -4096.0)
     ts(pi(1), pi(0), 15, None, OP.bitwise_and)
     cp(pc(0), pi(1))
     ts(pc(1), pc(0), 256.0, None, OP.mult)
-    ts(A("AT1"), A("TA"), pc(1), 1.0, OP.add, OP.add)
+    ts(A("AT1"), A("TA"), pc(1), None, OP.add)
+    ts(pc(5), pc(0), 15.0, 8192.0, OP.is_equal, OP.mult)
+    fill(pc(6), 1.0)
     cp(A("PLO"), A("TB"))
     ts(A("PHI"), A("TC"), pc(1), None, OP.add)
     rows("KT", 1, 0, A("PLO"), "y")
     rows("KT", 1, 1, A("PHI"), "s")
-    ts(pc(5), pc(0), 15.0, 8192.0, OP.is_equal, OP.mult)
-    fill(pc(6), 1.0)
-    pick(A("SHU"), [[-1, 128]], OP.not_equal, 1.0, -1, 1)
-    pick(A("IDF"), [[-1, 128]], OP.not_equal, 1.0, 0, 1)
-    for k, rs in enumerate(((0, 1, 3, 4), (0, 1), (3, 4))):
-        selector(sel(S_K + 8 * k), [(r, 1) for r in rs])
-    for c in (S_P, S_M):
-        pick(sel(c), [[-16, 8]], OP.is_ge, 0.0, 0, 1)
-        pick(sel(c), [[16, 8]], OP.is_ge, 0.0, 15, -1)
 
-    dma(A("W", 2048, 4096), IO("w", slice(0, 128), slice(2048, 4096)), "g")
+    def constants():
+        for nm in ("SEL", "IDF"):
+            zero(A(nm))
+        zero(sel(S_P), 4096)
+        zero(sel(S_M), -4096)
+        for c in (S_P, S_M):
+            pick(sel(c), [[-16, 8]], OP.is_ge, 0.0, 0, 1)
+            pick(sel(c), [[16, 8]], OP.is_ge, 0.0, 15, -1)
+        pick(A("IDF"), [[-1, 128]], OP.not_equal, 1.0, 0, 1)
+        for k in (IB, NI):
+            zero(cm(k))
+            pick(cm(k), [[-1, 128]], OP.not_equal, CMS[k], 0, 1)
+        for k, rs in enumerate(((0, 1, 3, 4), (0, 1), (3, 4))):
+            selector(sel(S_K + 8 * k), [(r, 1) for r in rs])
+        for c in range(3):
+            zero(A("XW0", c * ZC + 4096, c * ZC + ZC))
+        zero(A("HM"))
+        cp(pc(7), pi(0))
+        ts(pc(7), pc(7), float(VA), None, OP.is_ge)
+        fill(A("ZB"), 0.0)
+        fill(A("VT"), 0.0)
 
     def late_constants():
+        iota(A("MSK"), [[1, 16]], 0, 0)
         iota(A("CR", 0, 130), [[1, 130]], -64, 0)
         iota(A("CR", 130, 194), [[1, 64]], -65, 0)
         iota(A("ROW", 0, 128), [[0, 128]], 1, 0)
         iota(A("ROW", 128, 256), [[0, 128]], -112, 0)
         iota(A("ROW", 256, 384), [[0, 128]], 10240, -10239)
-        iota(A("ROW", 384, 896), [[-1, 2], [0, 256]], 0, 0)
+        zero(A("ROW", 384, 640), -1)
+        for nm, v in (("TRI", 1), ("DFV", 0), ("DFS", 0), ("S15", 0), ("IHF", 0)):
+            zero(A(nm), v)
+        zero(A("XW1", 11952, 3 * ZC))
+        for k, v in enumerate(CMS):
+            if k not in (IB, NI):
+                zero(cm(k))
+                pick(cm(k), [[-1, 128]], OP.not_equal, v, -1 if k == BSU else 0, 1)
+        pick(A("IHF"), [[-1, 128]], OP.not_equal, 0.5, 0, 1)
+        pick(A("IHF"), [[0, 8], [-1, 16]], OP.not_equal, 0.0, 15, 0)
         selector(sel(S_0), [(0, 1)])
         selector(sel(S_J), [(0, 1), (1, 1), (12, -1), (13, -1)])
         selector(sel(S_J + 8), [(4, 16), (5, 16), (8, 1), (9, 1), (12, -17), (13, -17)])
@@ -277,56 +298,49 @@ def rank_program(g, core, T, topo):
                 pick(A(nm), [[-1, 128]], OP.not_equal, v, -k, 1)
             blocks(nm, 64)
         pick(A("DFV"), [[-64, 2], [-200, 64]], OP.not_equal, 1.0, 0, 1)
-        iota(A("MSK"), [[1, 16]], 0, 0)
-        iota(A("NG", 0, 768), [[-3, 2], [0, 384]], -1, 0)
-        iota(A("NG", 256, 257), [[0, 1]], -16384, 0)
-        iota(A("NG", 384, 512), [[0, 128]], -1, 0)
+        zero(A("NG", 0, 512), -1)
+        zero(A("NG", 512, 768), -4)
 
     def late_constants_v():
-        for k, v in enumerate(CMS):
-            ts(cm(k), A("SHU") if k == BSU else IDF, v, None, OP.mult)
-        ts(pc(2), pc(0), 15.0, 0.5, OP.not_equal, OP.mult)
-        ts(A("IHF"), IDF, pc(2), None, OP.mult)
         ts(pc(3), pc(0), 15.0, 256.0, OP.is_equal, OP.mult)
         ts(pc(3), pc(3), 3840.0, None, OP.add)
         ts(pc(4), pc(0), -1.0, 1.0, OP.mult, OP.add)
+        ts(A("Q2"), A("AT1"), -1.0, 2.0, OP.add, OP.mult)
+        ts(A("AM"), A("AT1"), 8191.0, None, OP.add)
         ts(A("DEC", 0, 16), A("MSK"), pc(4), 0.0, OP.add, OP.min)
         ts(A("DEC", 16, 32), A("DEC", 0, 16), 1024.0, None, OP.mult)
         ts(A("DEC", 0, 16), A("DEC", 0, 16), 256.0, None, OP.mult)
         ts(A("MSK"), A("MSK"), pc(0), None, OP.is_equal)
-        ts(A("Q2"), A("AT1"), -1.0, 2.0, OP.add, OP.mult)
-        ts(A("AM"), A("AT1"), 8191.0, None, OP.add)
-        for k, v in ((9, TOPB), (10, 2 * TOPB - 3)):
-            fill(pc(k), v)
-        fill(A("XW1", 11952, 3 * ZC), 0.0)
-        fill(A("K2", 0, 1), 0.0)
-        fill(A("I4", 0, 1), 0.0)
+        fill(pc(8), TOPB)
+        fill(pc(9), 2 * TOPB - 3)
 
     def scatter_data():
-        for nm, tile in (("VT", "M1"), ("ST", "CS")):
-            iota(A(nm), [[0, 4096]], 0, 0)
-            for r, pattern, k in ((0, [[0, 16], [1, 16]], 0), (8, [[1, 16], [0, 16]], 1), (12, [[0, 256]], 2)):
-                src = A(("M1", "M2", "C2")[k]) if nm == "VT" else A(("CS", "TE", "TE")[k], 256 * (k // 2), 256 * (k // 2) + 256)
+        ts(A("KI"), zb(256), pc(0), 64.0, OP.add, OP.add)
+        ts(A("K2", 4, 260), zb(256), pc(0), 64.0, OP.add, OP.add)
+        fill(A("K2", 0, 1), 0.0)
+        fill(A("I4", 0, 1), 0.0)
+        zero(A("ST"))
+        for nm, tiles in (("VT", (A("M1"), A("M2"), A("C2"))), ("ST", (A("CS"), A("TE", 0, 256), A("TE", 256, 512)))):
+            for r, pattern, src in zip((0, 8, 12), ([[0, 16], [1, 16]], [[1, 16], [0, 16]], [[0, 256]]), tiles):
                 iota(src, pattern, 64, 0)
                 rows(nm, 0, r, src)
-        ts(A("KI"), A("ZB", 0, 256), pc(0), 64.0, OP.add, OP.add)
-        rows("VT", 0, 4, A("KI"))
-        ts(A("K2", 4, 260), A("ZB", 0, 256), pc(0), 64.0, OP.add, OP.add)
+        rows("VT", 0, 4, A("KI"), "g")
         rows("ST", 0, 4, A("K2", 4, 260))
 
-    def exts(buf, off, h, b, c0, s, k=8, start=True, stop=True):
+    def exts(buf, off, h, b, c0, s, k=8, start=True, stop=True, p0=0, p1=128):
         for i in range(16):
-            mm(P(b, c0 + i, c0 + i + (k - 1) * 16 + 1, 16), A(buf, off + 2048 * h + i, off + 2048 * h + 2048, 16),
+            mm(P(b, c0 + i, c0 + i + (k - 1) * 16 + 1, 16, p0, p1),
+               A(buf, off + 2048 * h + i, off + 2048 * h + 16 * (p1 - p0), 16),
                sel(s, k), start, stop if stop is True else (stop == "last" and i == 15))
 
-    def carry(outs_, cols, dec=None):
+    def carry(outs_, cols, dec):
         k = len(cols)
+        mm(P(4, 0, 16 * k), zb(128), zb(16 * k), True, False)
+        for j in range(k):
+            mm(P(4, 16 * j, 16 * j + 16), IDF, A("DEC", dec, dec + 16), False, False)
         for j, col in enumerate(cols):
             ts(A("RH", 16 * j, 16 * j + 16), A("MSK"), col, None, OP.mult)
-        terms = [(P(4, 0, 16 * k), A("TRI"), A("RH", 0, 16 * k))]
-        if dec is not None:
-            terms += [(P(4, 16 * j, 16 * j + 16), IDF, A("DEC", dec, dec + 16)) for j in range(k)]
-        mms(*terms)
+        mm(P(4, 0, 16 * k), A("TRI"), A("RH", 0, 16 * k), False, True)
         for j, o in enumerate(outs_):
             most(o, P(4, 16 * j, 16 * j + 16))
 
@@ -343,13 +357,13 @@ def rank_program(g, core, T, topo):
 
     def tables():
         mm(P(4, 0, 1), A("SHU"), A("EB", 0, 1))
-        tt(P(7), P(6), A("AT1"), OP.subtract)
+        tt(P(3), P(6), A("AT1"), OP.subtract)
         ts(P(6, 256, 257), P(4, 0, 1), pc(5), None, OP.add)
         tt(A("TD"), P(6, 1, 257), A("AT1"), OP.subtract)
-        tt(P(5), P(7), A("TD"), OP.is_gt)
-        act(A("TC"), P(7), AF.Relu, pc(6), -1.0)
+        tt(P(5), P(3), A("TD"), OP.is_gt)
+        act(A("TC"), P(3), AF.Relu, pc(6), -1.0)
         tt(P(5, 256, 512), P(5), A("TD"), OP.mult)
-        act(A("NB"), P(7), AF.Copy, None, BIG)
+        act(A("NB"), P(3), AF.Copy, None, BIG)
         tt(P(5), P(5, 256, 512), A("TC"), OP.subtract)
         cp(A("DHI"), P(5))
         rows("KT", 1, 3, A("DHI"), "s")
@@ -359,14 +373,21 @@ def rank_program(g, core, T, topo):
     def tables2():
         tt(A("TC"), P(5), A("AT1"), OP.add)
         cp(A("BLB"), A("TC"))
-        ts(P(7, 256, 512), P(7), 4.0, 4.0, OP.mult, OP.add)
-        tt(A("LEN"), P(7, 256, 512), A("NB"), OP.min)
+        ts(P(3, 256, 512), P(3), 4.0, 4.0, OP.mult, OP.add)
+        tt(A("LEN"), P(3, 256, 512), A("NB"), OP.min)
         for k in range(4):
             dma(A("HM", 66 * k, 66 * k + 64), A("NB", 0, 256, 1, 32 * k, 32 * k + 32))
 
-    cp(P(6), A("VI"))
+    def weapon_sums(h):
+        exts("W", 0, h, h, 0, S_P)
+        ts(half("SW", h), P(h, 0, 128), pc(7), None, OP.mult)
+
     cp(A("EB"), A("VI"))
+    cp(P(6), A("VI"))
     tables()
+    dma(A("W", 2048, 4096), IO("w", slice(0, 128), slice(2048, 4096)), "y")
+    constants()
+    tables2()
     late_constants()
 
     for t in range(2):
@@ -376,43 +397,55 @@ def rank_program(g, core, T, topo):
             tt(A("WB", off + 2048 * h + 16 * a, off + 2048 * h + 16 * b), IND(X, 0, 4112, lst, 128 * h + a, 128 * h + b),
                A("W", 2048 * h + 16 * a, 2048 * h + 16 * b), OP.min)
 
-        def xa(h, a=0, b=128):
+        def xa(h, a, b):
             xg("VL", 8192, h, a, b)
-            if b == 128:
-                mm(P(h, 0, 128), zb(128), zb(128), True, False)
-                exts("WB", 8192, h, h, 0, S_P, 8, False, False)
 
-        def xb(h, a=0, b=128):
-            xg("VB", 12288, h, a, b)
-            if b == 128:
-                exts("WB", 12288, h, h, 0, S_M, 8, False, "last")
+        def asum(h):
+            mm(P(h, 0, 128), IDF, half("SW", h), True, False)
+            exts("WB", 8192, h, h, 0, S_P, 8, False, False, 0, VA)
+
+        def xb(h):
+            xg("VB", 12288, h, 0, 128)
+            exts("WB", 12288, h, h, 0, S_M, 8, False, "last")
+
+        def xr(h):
+            act(A(XO, 512 * h, 512 * h + 512), IND(X, 0, 4112, "VL", 128 * h + VA, 128 * h + 128))
+
+        def sub(h):
+            mms((P(6 + h, 0, 512), cm(IB), A("W", 2048 * h + 16 * VA, 2048 * h + 2048)),
+                (P(6 + h, 0, 512), cm(NI), A(XO, 512 * h, 512 * h + 512)))
+
+        def rr(h):
+            act(A(XO, 1024 + 2048 * h, 1536 + 2048 * h), P(6 + h, 0, 512), AF.Relu)
+
+        def rsum(h):
+            exts(XO, 1024, h, h, 0, S_M, 8, False, False, VA, 128)
 
         def kid(h):
             act(A("XB", 2048 * h, 2048 * h + 2048), IND("KT", 0, 4112, "VL", 128 * h, 128 * h + 128))
 
-        def kids(h, s):
+        def ksum(h):
             exts("XB", 0, h, 2 + h, 0, S_K, 24)
+
+        def kids(h, s):
             act(A("FS", 256 * h, 256 * h + 256), P(2 + h))
-            mm(P(6 + h, 0, 128), A("FS", 256 * h, 256 * h + 128), IDF)
-            if s < 3:
-                mm(P(4 + h, 0, 128), A("FS", 256 * h + 128, 256 * h + 256), IDF, True, False)
-            else:
-                mm(P(4 + h, 0, 128), IDF, A("FS", 256 * h + 128, 256 * h + 256), True, False)
+            mm(P(4 + h, 128, 256), A("FS", 256 * h, 256 * h + 128), IDF)
             if s == 1:
                 act(half("NOH", h), P(2 + h, 256, 384), AF.Relu, None, -1.0)
 
         def relu(h):
             act(half("TA", h), P(h, 0, 128), AF.Relu)
 
+        def vb(h, s):
+            cp(half("VB", h), P(4 + h, 128, 256))
+            f3 = A("FS", 256 * h + 128, 256 * h + 256)
+            mm(P(4 + h, 0, 128), *((f3, IDF) if s < 3 else (IDF, f3)), True, False)
+
         def choose(h, s):
             tt(half("TB", h), P(2 + h, 256, 384), half("TA", h), OP.min)
-            if s < 3:
-                mm(P(4 + h, 0, 128), half("TB", h), IDF, False, True)
-            else:
-                mm(P(4 + h, 0, 128), IDF, half("TB", h), False, True)
+            mm(P(4 + h, 0, 128), *((half("TB", h), IDF) if s < 3 else (IDF, half("TB", h))), False, True)
 
         vl = lambda h: ts(half("VL", h), P(4 + h, 0, 128), 1.0, None, OP.add)
-        vb = lambda h: cp(half("VB", h), P(6 + h, 0, 128))
 
         def digits(h):
             ts(half("AQ", h), P(4 + h, 0, 128), 1.0 / 64, 160 - 31.5 / 64, OP.mult, OP.add)
@@ -429,104 +462,139 @@ def rank_program(g, core, T, topo):
         def column(h, q, i):
             c = 256 * h + 16 * q + i
             s1, s2 = A("S12", c, c + 1), A("S12", c + 128, c + 129)
+            late = h == 1 and q >= 6
             if i in SCOL:
-                o, b, last = 7800 + 130 * (slots[1] % 32), 2 + h, SCOL[-1]
+                o, b, last = 7800 + 130 * (slots[1] % 32), 2 + h - late, SCOL[-1]
                 slots[1] += 1
                 act(A(XO, o, o + 64), A("CR", 130, 194), AF.Relu, s1, -1.0)
                 act(A(XO, o + 64, o + 130), A("CR", 64, 130), AF.Relu, s2, -1.0)
             else:
-                o, b, last = 130 * (slots[0] % 60), h, max(k for k in range(16) if k not in SCOL)
+                o, b, last = 130 * ((slots[0] + 30) % 60), h - late, max(k for k in range(16) if k not in SCOL)
                 slots[0] += 1
                 ts(A(XO, o, o + 130), A("CR", 0, 130), s1, s2, OP.max, OP.min)
             mm(P(b, 66 * (q // 2), 66 * (q // 2) + 66, 1, 64 * (q % 2), 64 * (q % 2) + 64), A(XO, o, o + 64),
-               A(XO, o + 64, o + 130), False, i == last and q >= 6)
+               A(XO, o + 64, o + 130), False, i == last and (q >= 6 or (h == 1 and q >= 4)))
 
-        def differences(h):
-            mm(P(4, 0, 264), A("DFV"), A("SCV"), h == 0, False)
-            mm(P(4, 0, 264), A("DFS"), A("SCS"), False, h == 1)
+        def sums(bv, bs, a, b):
+            act(A("SCS", a, b), P(bs, a, b))
+            cp(A("SCV", a, b), P(bv, a, b))
+
+        def differences(bank, a, b, first):
+            mm(P(bank, a, b), A("DFS"), A("SCS", a, b), first, False)
+            mm(P(bank, a, b), A("DFV"), A("SCV", a, b), False, not first)
+
+        def counts(bank, a, b):
+            tt(A("D1", a, b - 2), P(bank, a, b - 2), A("Z2", a + 1, b - 1), OP.subtract)
+            tt(P(6, a, b - 2), P(bank, a + 2, b), A("D1", a, b - 2), OP.add)
+            tt(A("FL", a, b - 2), P(6, a, b - 2), A("HM", a, b - 2), OP.is_gt)
+
+        def marked(ks):
+            for k in ks:
+                dma(A(XO, 0, 4096, 1, 32 * k, 32 * k + 32, 16), A("FL", 66 * k, 66 * k + 64), "y")
+            for k in ks:
+                dma(A("HB", 0, 256, 1, 32 * k, 32 * k + 32), A("FL", 66 * k, 66 * k + 64), "s" if k == 3 else "y")
 
         for h in range(2):
             ts(half("VL", h), half("HI", h), 1.0, None, OP.add)
-        for s in range(4):
-            if s == 0:
-                kid(0)
-                xa(0)
-                kids(0, s)
-                kid(1)
-                xa(1)
-                tables2()
-            else:
-                relu(1)
-                kid(0)
-                xa(0, 0, 96)
-                choose(1, s - 1)
-                xa(0, 96, 128)
-                vl(1)
-                kids(0, s)
-                kid(1)
-                xa(1)
-            vb(0)
-            kids(1, s)
-            xb(0)
-            vb(1)
-            relu(0)
-            xb(1, 0, 96)
-            choose(0, s)
-            if s == 3:
+        if t == 0:
+            weapon_sums(0)
+        xr(0)
+        sub(0)
+        rr(0)
+        xa(0, 0, VA)
+        if t == 1:
+            tables2()
+        else:
+            scatter_data()
+        zero(A("WF", 0, 8192))
+        zero(A("WB", 0, 8192))
+        act(A("XB", 0, 1024), IND("KT", 0, 4112, "VL", 0, 64))
+        cp(A("XB", 1024, 2048), IND("KT", 0, 4112, "VL", 64, 128))
+        ksum(0)
+        xa(1, 0, XS)
+        kids(0, 0)
+        if t == 0:
+            weapon_sums(1)
+        for k in range(8):
+            h, s, s2 = k % 2, k // 2, (k + 1) // 2
+            more = k < 7
+            if more:
+                xr(1 - h)
+            vb(h, s)
+            asum(h)
+            if more:
+                sub(1 - h)
+                kid(1 - h)
+            rsum(h)
+            xb(h)
+            if more:
+                ksum(1 - h)
+                relu(h)
+                if k:
+                    xa(1 - h, 0, XS)
+                rr(1 - h)
+                choose(h, s)
+                kids(1 - h, s2)
+                xa(1 - h, XS, VA)
+            if t == 0 and k == 4:
+                late_constants_v()
+            if s < 3:
+                vl(h)
+            if k == 6:
                 digits(0)
                 act(A("S12", 0, 256), P(6))
-            xb(1, 96, 128)
-            if s < 3:
-                vl(0)
-            if s == 0:
-                if t == 0:
-                    late_constants_v()
-                    scatter_data()
-                iota(A("WB", 0, 8192), [[0, 8192]], 0, 0)
-                iota(A("WF", 0, 8192), [[0, 8192]], 0, 0)
         relu(1)
         for h in range(2):
             for q in range(8):
                 for i in range(16):
                     column(h, q, i)
-                if h == 0 and q == 0:
+                if (h, q) == (0, 0):
                     choose(1, 3)
-                if h == 0 and q == 1:
+                if (h, q) == (0, 1):
                     digits(1)
-                if h == 0 and q == 3:
+                if (h, q) == (0, 3):
                     cp(A("S12", 256, 512), P(7))
-                if h == 1 and q == 1:
-                    act(A("SCS"), P(2, 0, 264))
-                    cp(A("SCV"), P(0, 0, 264))
-                if h == 1 and q == 2:
-                    differences(0)
+                if (h, q) == (1, 1):
+                    sums(0, 2, 0, 264)
+                if (h, q) == (1, 2):
+                    differences(4, 0, 198, True)
+                    differences(5, 198, 264, True)
+                    for b in (0, 2):
+                        mm(P(b, 198, 264), zb(128), zb(66), True, False)
+                if (h, q) == (1, 6):
+                    sums(1, 3, 0, 198)
+                    differences(4, 0, 198, False)
         if t == 0:
             dma(A("HI"), IO("start", slice(0, 128), slice(256, 512)), "y")
-        act(A("SCS"), P(3, 0, 264))
-        cp(A("SCV"), P(1, 0, 264))
-        differences(1)
-        act(A("Z2"), P(4, 0, 264), AF.Copy, None, 2.0)
-        tt(A("D1", 0, 262), P(4, 0, 262), A("Z2", 1, 263), OP.subtract)
-        tt(P(5, 0, 262), P(4, 2, 264), A("D1", 0, 262), OP.add)
-        tt(A("FL", 0, 262), P(5, 0, 262), A("HM", 0, 262), OP.is_gt)
-        for k in range(4):
-            dma(A(XO, 0, 4096, 1, 32 * k, 32 * k + 32, 16), A("FL", 66 * k, 66 * k + 64), "ys"[k % 2])
-        for k in range(4):
-            dma(A("HB", 0, 256, 1, 32 * k, 32 * k + 32), A("FL", 66 * k, 66 * k + 64), "ys"[k % 2])
-        copy = lambda c: ts(A(X, c * ZC, c * ZC + 4096), A(X, 0, 4096), -float(c), 0.0, OP.add, OP.max)
-        copy(1)
+        act(A("Z2", 0, 198), P(4, 0, 198), AF.Copy, None, 2.0)
+        sums(0, 2, 198, 264)
+        differences(5, 198, 264, False)
+        counts(4, 0, 198)
+        marked(range(3))
+        act(A("Z2", 198, 264), P(5, 198, 264), AF.Copy, None, 2.0)
+        counts(5, 198, 264)
+        marked([3])
+        for c in (1, 2):
+            ts(A(X, c * ZC, c * ZC + 4096), A(X, 0, 4096), -float(c), 0.0, OP.add, OP.max)
 
-        act(A("XB", 2048, 4096), IND(XO, 0, 4096, "BLB", 128, 256))
-        cp(A("XB", 0, 2048), IND(XO, 0, 4096, "BLB", 0, 128))
+        def shared(buf, off, win, h):
+            for f, a in ((act, 128 * h), (cp, 128 * h + 64)):
+                f(A(buf, off + 16 * a, off + 16 * a + 1024), win(a, a + 64))
+
+        mm(P(2), zb(128), zb(256), True, False)
         for h in (1, 0):
+            shared("XB", 0, lambda a, b: IND(XO, 0, 4096, "BLB", a, b), h)
             exts("XB", 0, h, h, 0, S_0)
+            if h == 1:
+                mm(P(2, 0, 255), cm(BI), A("HB", 1, 256), False, False)
+                mm(P(2, 255, 256), cm(BSU), A("HB", 0, 1), False, False)
+        act(half("M1", 1), P(1, 0, 128))
         ts(A("KP2"), A("HB"), -2.0, 2.0, OP.mult, OP.add)
         scan(A("K2", 1, 257), A("KP2"), zb(256), OP.add, OP.add)
+        act(half("M1", 0), P(0, 0, 128))
         ts(A("KP4"), A("HB"), -4.0, 4.0, OP.mult, OP.add)
-        act(half("M1", 1), P(1, 0, 128))
-        cp(half("M1", 0), P(0, 0, 128))
-        mms((P(2), zb(128), zb(256)), (P(2, 0, 255), cm(BI), A("HB", 1, 256)), (P(2, 255, 256), cm(BSU), A("HB", 0, 1)),
-            (P(2, 128, 256), half("M1", 1), cm(BI)), (P(2, 0, 128), half("M1", 0), cm(BI)))
+        for h in (1, 0):
+            mm(P(2, 128 * h, 128 * h + 128), half("M1", h), cm(BI), False, h == 0)
         tt(A("TC"), P(2), A("LEN"), OP.min)
         ng4 = A("NG", 512, 768)
         scan(A("TA"), ng4, A("TC"), OP.add, OP.max)
@@ -539,12 +607,12 @@ def rank_program(g, core, T, topo):
         scan(A("I4", 1, 257), A("KI"), zb(256), OP.add, OP.add)
         mms((P(4, 32, 33), A("TRI"), A("I4", 256, 257)), (P(4, 32, 33), A("TRI"), A("K2", 256, 257)))
         mm(P(4, 33, 34), A("TRI"), A("K2", 256, 257))
+        mm(P(4, 34, 35), A("TRI"), A("I4", 256, 257))
         tt(A("TA"), P(5), A("I4", 0, 256), OP.subtract)
         scan(A("TB"), A("TA"), A("TA"), OP.min, OP.min, BIG)
-        cp(A("CC", 0, 2), P(4, 32, 34))
-        ts(cc(2), A("TB", 255, 256), -1.0, cc(0), OP.mult, OP.add)
-        ts(cc(2), cc(2), cc(1), None, OP.subtract)
-        ts(A("RH", 0, 16), A("MSK"), cc(2), None, OP.mult)
+        cp(A("CC", 0, 3), P(4, 32, 35))
+        ts(cc(3), A("TB", 255, 256), -1.0, cc(2), OP.mult, OP.add)
+        ts(A("RH", 0, 16), A("MSK"), cc(3), None, OP.mult)
         mm(P(4, 0, 16), A("TRI"), A("RH", 0, 16))
         tt(A("TOP"), P(5), A("TC"), OP.is_lt)
         mms((P(6), IDF, A("K2", 0, 256)), (P(6), cm(BI), A("HB")), (P(6), cm(IB), A("TOP")))
@@ -555,108 +623,136 @@ def rank_program(g, core, T, topo):
         tt(A("TA"), P(6), A("TD"), OP.subtract)
         tt(A("TA"), P(7), A("TA"), OP.min)
         cp(A("QL"), A("TA"))
-        act(IND("WF", 0, 16384, "QL", VS, 256), A("ST", 16 * VS, 4096), AF.Silu)
-        ts(A("ELB"), P(2), -1.0, None, OP.add)
-        tt(P(5), A("K2", 1, 257), A("TD"), OP.subtract)
-        tt(P(3), A("K2", 1, 257), A("I4", 1, 257), OP.add)
-        cp(A("DHI"), P(5))
-        tt(A("DLO"), P(5), A("DHI"), OP.subtract)
-        rows(XO, KM + 4096, 0, A("DHI"), "y")
-        rows(XO, KM + 4096, 1, A("DLO"), "y")
-        ts(P(3), P(3), cc(0), None, OP.add)
-        cp(A("PHI"), P(3))
-        tt(A("PLO"), P(3), A("PHI"), OP.subtract)
-        rows(XO, KM, 0, A("PHI"), "y")
-        rows(XO, KM, 1, A("PLO"), "y")
-        cp(IND("WB", 0, 16384, "QL", 0, VS), A("VT", 0, 16 * VS))
+        act(IND("WF", 0, 16384, "QL", VS[t], 256), A("ST", 16 * VS[t], 4096), AF.Silu)
+        cp(IND("WB", 0, 16384, "QL", 0, VS[t]), A("VT", 0, 16 * VS[t]))
         dma(A("FB"), A("WF", 0, 8192, 1, 12, 128, 16), "g")
         dma(A("FA"), A("WB", 0, 8192, 1, 12, 128, 16), "y")
         src = A("WF", 0, 8192, 1, 0, 128, 4)
         dma(A("WB", 0, 8192, 1, 1, 128, 4), (src[0], src[1] + A("FA")[1]), "g")
-        act(A("XB"), IND(XO, KM, KM + 8192, "ELB", 0, 256))
-        copy(2)
+        tt(P(5), A("K2", 1, 257), A("TD"), OP.subtract)
+        act(A("DHI"), P(5))
+        tt(P(3), A("K2", 1, 257), A("I4", 1, 257), OP.add)
+        rows(XO, KM + 4096, 0, A("DHI"), "s")
+        ts(P(3), P(3), cc(0), None, OP.add)
+        act(A("PHI"), P(3))
+        tt(A("DLO"), P(5), A("DHI"), OP.subtract)
+        rows(XO, KM + 4096, 1, A("DLO"), "y")
+        rows(XO, KM, 0, A("PHI"), "s")
+        tt(A("PLO"), P(3), A("PHI"), OP.subtract)
+        rows(XO, KM, 1, A("PLO"), "y")
+        ts(A("ELB"), P(2), -1.0, None, OP.add)
+        ends = lambda h: act(A("XB", 2048 * h, 2048 * h + 2048), IND(XO, KM, KM + 8192, "ELB", 128 * h, 128 * h + 128))
 
-        mms((P(0, 0, 512), A("ROW", 0, 128, 1, 0, 1), A("ROW", 384, 896, 1, 0, 1)),
-            *[(P(0, 256 * k, 256 * k + 256), cm(I128), A(nm, o, 512, 2))
-              for nm in ("FA", "FB") for k, o in ((0, 0), (0, 1), (1, 1))])
-        scan(A("TE"), A("NG", 0, 512), P(0, 0, 512), OP.add, OP.max)
-        carry([cc(4), cc(5)], [A("TE", 255, 256), A("TE", 511, 512)], 0)
+        one = A("ROW", 0, 128, 1, 0, 1)
+        mms((P(7), one, A("ROW", 384, 640, 1, 0, 1)), *[(P(7), cm(I128), A(nm, 1, 512, 2)) for nm in ("FA", "FB")])
+        mms(*[(P(0), cm(I128), A(nm, o, 512, 2)) for nm in ("FA", "FB") for o in (0, 1)])
         ng1 = A("NG", 0, 256)
+        ends(0)
+        scan(A("TE", 256, 512), ng1, P(7), OP.add, OP.max)
+        scan(A("TE", 0, 256), ng1, P(0), OP.add, OP.max)
+        carry([cc(4), cc(5)], [A("TE", 255, 256), A("TE", 511, 512)], 0)
         scan(P(1), ng1, P(0), OP.add, OP.max, cc(4))
-        scan(A("TB"), ng1, P(0, 256, 512), OP.add, OP.max, cc(5))
+        scan(A("TB"), ng1, P(7), OP.add, OP.max, cc(5))
+        ts(A("M1"), P(1), TOPB, None, OP.is_lt)
+        mm(P(2), cm(I2), A("M1"), True, False)
         tt(A("TA"), P(1), A("TB"), OP.subtract)
-        act(P(3), A("TB"), AF.Identity, pc(10), -2.0)
         tt(A("TC"), P(1), A("TA"), OP.add)
-        act(A("M1"), P(1), AF.Sign, pc(9), -1.0)
         ts(A("M2"), A("TC"), TOPB, None, OP.is_lt)
-        mms((P(2), cm(I2), A("M2")), (P(2), cm(I2), A("M1")))
+        mm(P(2), cm(I2), A("M2"), False, True)
+        ts(P(3), A("TB"), -2.0, 2 * TOPB - 3, OP.mult, OP.add)
         tt(A("CS"), P(2), A("TA"), OP.mult)
-        act(A("C2"), P(2))
         tt(P(1), P(3), A("CS"), OP.min)
         tt(A("TC"), A("Q2"), P(1), OP.subtract)
         cp(A("QL"), A("TC"))
-        act(A("WB", 10240, 12288), IND("WB", 0, 8192, "QL", 128, 256))
-        cp(A("WB", 8192, 10240), IND("WB", 0, 8192, "QL", 0, 128))
-        for r in range(16):
-            mm(P(7, 256 + r, 384, 16, 0, 16), A("C2", r, 256, 16), sel(S_C))
+        shared("WB", 8192, lambda a, b: IND("WB", 0, 8192, "QL", a, b), 1)
+        exts("WB", 8192, 1, 6, 0, S_J, 16)
+        shared("WB", 8192, lambda a, b: IND("WB", 0, 8192, "QL", a, b), 0)
         mm(P(0, 0, 512), zb(128), A("NG", 0, 512), True, False)
         mm(P(0), cm(IZ), A("M1"), False, False)
         mm(P(0), cm(IZ), A("M2"), False, False)
         mm(P(4, 0, 32), zb(128), zb(32), True, False)
-        for h in (1, 0):
-            exts("WB", 8192, h, 5 + h, 0, S_J, 16)
-        act(A("FA", 256, 512), P(6))
-        cp(A("FA", 0, 256), P(5))
+        exts("WB", 8192, 0, 5, 0, S_J, 16)
+        ends(1)
+        cp(A("FA", 256, 512), P(6))
+        cp(A("C2"), P(2))
         weights = ((1, 0, IB), (1, 1, I16), (0, 0, I256), (0, 1, IB), (0, 2, IZ))
         for h in (1, 0):
+            if h == 0:
+                for r in range(16):
+                    mm(P(7, r, 256, 16, 0, 16), A("WB", 8192 + 16 * r + 15, 12288, 256), sel(S_J, 16))
+                cp(A("FA", 0, 256), P(5))
             for k, (l, d, wt) in enumerate(weights[:4]):
                 mm(P(0, 256 * l + 128 * h, 256 * l + 128 * h + 128), A("FA", 256 * h + 128 * d, 256 * h + 128 * d + 128),
                    cm(wt), False, h == 0 and k == 3)
-            for r in range(8 - 8 * h, 16 - 8 * h):
-                mm(P(7, r, 256, 16, 0, 16), A("WB", 8192 + 16 * r + 15, 12288, 256), sel(S_J, 16))
-        cp(A("VB"), P(0, 256, 512))
-        act(A("FB", 0, 384, 1, 0, 16), P(7, 0, 384, 1, 0, 16))
+        for r in range(16):
+            mm(P(7, 256 + r, 384, 16, 0, 16), A("C2", r, 256, 16), sel(S_C))
+        lists = [(A("VB"), P(0, 256, 512)), (A("VL"), P(0))]
+        cp(*lists[t])
+        cp(A("FB", 0, 384, 1, 0, 16), P(7, 0, 384, 1, 0, 16))
         for k, (l, d, wt) in enumerate(weights):
             mm(P(4, 16 * l, 16 * l + 16), A("FB", 128 * d, 128 * d + 128, 1, 0, 16),
                A("CM", 128 * wt, 128 * wt + 16, 1, 0, 16), False, k == 4)
-        cp(A("VL"), P(0))
+        cp(*lists[1 - t])
         LX, ES, RE = ["%s%d" % (nm, t) for nm in ("LX", "ES", "RE")]
         SZ = lambda lst, a, b: IND("XB", 0, 4096, lst, a, b)
         XI = lambda lst, a, b: IND(X, 0, 3 * ZC, lst, a, b)
-        act(A("WB", 14336, 16384), SZ("VB", 128, 256))
-        cp(A("L15"), P(4, 0, 32))
-        cp(A("TZ"), SZ("L15", 16, 32))
-        mms((P(4, 0, 16), zb(128), zb(16)),
-            *[(P(4, 8 * h, 8 * h + 8), half("CS", h), A("S15")) for h in range(2)],
-            *[(P(4, 8 * h, 8 * h + 8), half("TZ", h), sel(S_E)) for h in range(2)])
-        cp(A("TX"), XI("L15", 0, 16))
-        ts(A(ES), P(4, 0, 16), 4096.0, None, OP.min)
-        send(ES, RE, "es%d" % t, "er%d" % t)
-        send("TX", LX, "xs%d" % t, "xr%d" % t)
-        cp(A("WB", 12288, 14336), SZ("VB", 0, 128))
-        for h in (1, 0):
-            exts("WB", 12288, h, 5, 128 * h, S_E)
-        act(A(XO, KM + 2048, KM + 4096), XI("VL", 128, 256))
-        cp(A(XO, KM, KM + 2048), XI("VL", 0, 128))
-        act(A("TA"), P(5))
-        for i in range(15):
-            (act if i % 3 == 2 else cp)(A(XO, 256 * i, 256 * i + 256), A(XO, KM + i, KM + 4096, 16))
-            if t == 1 and i in (7, 14):
-                a = 0 if i == 7 else 2048
-                dma(IO("y", slice(0, 128), slice(a, 256 * i + 256)), A(XO, a, 256 * i + 256), "ys"[i % 2])
-            if i == 3:
-                cp(A("TA", 15, 256, 16), A(RE))
-                mms((P(7), A("IHF"), A("CS")), *[(P(7, 128 * h, 128 * h + 128), half("TA", h), IDF) for h in range(2)])
-            if i == 6:
-                ts(P(6), P(7), pc(3), None, OP.min)
-                act(A("EB"), P(6))
-                if t == 1:
-                    dma(IO("ye"), A("EB"))
+        sz = lambda f, a, b: f(A("WB", 12288 + 16 * a, 12288 + 16 * b), SZ("VB", a, b))
+        xi = lambda f, a, b: f(A(XO, KM + 16 * a, KM + 16 * b), XI("VL", a, b))
+        order = lambda f, i: f(A(XO, 256 * i, 256 * i + 256), A(XO, KM + i, KM + 4096, 16))
+
+        def last_places():
+            cp(A("L15"), P(4, 0, 32))
+            cp(A("TZ"), SZ("L15", 16, 32))
+            mms((P(4, 0, 16), zb(128), zb(16)),
+                *[(P(4, 8 * h, 8 * h + 8), half("CS", h), A("S15")) for h in range(2)],
+                *[(P(4, 8 * h, 8 * h + 8), half("TZ", h), sel(S_E)) for h in range(2)])
+            cp(A("TX"), XI("L15", 0, 16))
+            ts(A(ES), P(4, 0, 16), 4096.0, None, OP.min)
+            send(ES, RE, "es%d" % t, "er%d" % t)
+            send("TX", LX, "xs%d" % t, "xr%d" % t)
+            mm(P(7), A("IHF"), A("CS"), True, False)
+
+        def new_ends():
+            cp(A("TA", 15, 256, 16), A(RE))
+            for h in range(2):
+                mm(P(7, 128 * h, 128 * h + 128), half("TA", h), IDF, False, h == 1)
+
         if t == 0:
+            sz(act, 120, 256)
+            last_places()
+            sz(cp, 0, 120)
+            for h in (1, 0):
+                exts("WB", 12288, h, 5, 128 * h, S_E)
+            xi(act, 128, 256)
+            xi(cp, 0, 96)
+            act(A("TA"), P(5))
+            new_ends()
+            xi(cp, 96, 128)
+            ts(P(6), P(7), pc(3), None, OP.min)
+            act(A("EB"), P(6))
             tables()
+            for i in range(15):
+                order(act if i % 3 == 0 else cp, i)
             cp(A(XO, 3840, 4096), A(LX))
         else:
+            xi(act, 112, 256)
+            last_places()
+            xi(cp, 0, 112)
+            sz(act, 128, 256)
+            exts("WB", 12288, 1, 6, 128, S_E)
+            for i in range(15):
+                order(cp, i)
+                if i in (3, 7, 11, 14):
+                    dma(IO("y", slice(0, 128), slice(i // 4 * 1024, 256 * i + 256)), A(XO, i // 4 * 1024, 256 * i + 256))
             dma(IO("y", slice(0, 128), slice(3840, 4096)), A(LX))
+            sz(act, 64, 128)
+            sz(cp, 0, 64)
+            exts("WB", 12288, 0, 5, 0, S_E)
+            act(half("TA", 1), P(6, 128, 256))
+            cp(half("TA", 0), P(5, 0, 128))
+            new_ends()
+            ts(A("EB"), P(7), pc(3), None, OP.min)
+            dma(IO("ye"), A("EB"), "s")
 
     for s in sorted(total):
         if known["g"].get(s, 0) < total[s]:

@@ -5,17 +5,20 @@ AF = ActivationFunctionType
 F32, BF, I32, U16 = "float32", "bfloat16", "int32", "uint16"
 NDMA = 110
 ZC = 4128
+NB_ = 13
 SCRATCH = {
     "XW0": ("sbuf", [128, 3 * ZC], BF), "XW1": ("sbuf", [128, 3 * ZC], BF),
     "XB": ("sbuf", [128, 4096], BF), "W": ("sbuf", [128, 4096], BF), "KT": ("sbuf", [128, 4112], BF),
     "WB": ("sbuf", [128, 16384], BF), "WF": ("sbuf", [128, 16384], F32),
     "VT": ("sbuf", [128, 4096], BF), "ST": ("sbuf", [128, 4096], F32),
-    "ZB": ("sbuf", [128, 264], BF), "CR": ("sbuf", [128, 194], BF), "CM": ("sbuf", [128, 12 * 128], BF),
+    "ZB": ("sbuf", [128, 264], BF), "CR": ("sbuf", [128, 64], BF), "CM": ("sbuf", [128, 12 * 128], BF),
     "IDF": ("sbuf", [128, 128], F32), "SHU": ("sbuf", [128, 128], F32), "TRI": ("sbuf", [128, 128], F32),
-    "IHF": ("sbuf", [128, 128], F32), "DFV": ("sbuf", [128, 128], F32), "DFS": ("sbuf", [128, 128], F32),
+    "IHF": ("sbuf", [128, 128], F32), "NID": ("sbuf", [128, 128], F32), "DFS": ("sbuf", [128, 128], F32),
     "MSK": ("sbuf", [128, 16], F32), "DEC": ("sbuf", [128, 32], F32), "S15": ("sbuf", [128, 8], F32),
-    "PI": ("sbuf", [128, 8], I32), "PC": ("sbuf", [128, 16], F32), "SEL": ("sbuf", [128, 88], BF),
-    "ROW": ("sbuf", [2, 640], BF), "NG": ("sbuf", [128, 768], BF), "SW": ("sbuf", [128, 256], F32),
+    "PI": ("sbuf", [128, 8], I32), "PC": ("sbuf", [128, 24], F32), "SEL": ("sbuf", [128, 88], BF),
+    "ROW": ("sbuf", [2, 640], BF), "NG": ("sbuf", [128, 512], BF), "SW": ("sbuf", [128, 512], BF),
+    "STEP": ("sbuf", [128, 128 * NB_], BF), "FS": ("sbuf", [128, 512], BF), "HD": ("sbuf", [128, 256], BF),
+    "SC": ("sbuf", [128, 264], F32),
     "AT1": ("sbuf", [128, 256], F32), "Q2": ("sbuf", [128, 256], F32),
     "AM": ("sbuf", [128, 256], F32), "EB": ("sbuf", [128, 256], F32),
     "DHI": ("sbuf", [128, 256], BF), "DLO": ("sbuf", [128, 256], BF),
@@ -29,7 +32,7 @@ SCRATCH = {
     "HB": ("sbuf", [128, 256], BF), "KP2": ("sbuf", [128, 256], BF), "KP4": ("sbuf", [128, 256], BF),
     "KI": ("sbuf", [128, 256], BF), "INS": ("sbuf", [128, 256], BF), "TOP": ("sbuf", [128, 256], BF),
     "K2": ("sbuf", [128, 260], F32), "I4": ("sbuf", [128, 260], F32), "CC": ("sbuf", [128, 16], F32),
-    "RH": ("sbuf", [128, 32], F32), "FA": ("sbuf", [128, 512], BF), "FB": ("sbuf", [128, 512], BF),
+    "RH": ("sbuf", [128, 48], F32), "FA": ("sbuf", [128, 512], BF), "FB": ("sbuf", [128, 512], BF),
     "M1": ("sbuf", [128, 256], BF), "M2": ("sbuf", [128, 256], BF), "C2": ("sbuf", [128, 256], BF),
     "CS": ("sbuf", [128, 256], F32), "TX": ("sbuf", [128, 256], BF), "TZ": ("sbuf", [128, 256], BF),
     "LX0": ("sbuf", [128, 256], BF), "LX1": ("sbuf", [128, 256], BF),
@@ -41,17 +44,16 @@ for _k in range(8):
 SEMAPHORES = ["qv", "qs", "qt", "qg"] + ["d%d" % k for k in range(NDMA)]
 SEMAPHORES += ["%s%d" % (a, k) for a in ("xs", "xr", "es", "er") for k in range(2)]
 
-ALIAS = {"SCV": (8192, 264), "SCS": (8456, 264), "Z2": (8720, 264), "D1": (8984, 264), "TE": (9248, 512),
-         "LEN": (9760, 256), "FS": (10016, 512)}
-S_P, S_M, S_K, S_0, S_J, S_E, S_C = 0, 8, 16, 40, 48, 64, 72
-CMS = (1.0, -64.0, 64.0, 32768.0, 32768.0, 128.0, 2.0, float(ZC), 4096.0, 256.0, 16.0, -1.0)
-IB, N64, P64, BI, BSU, I128, I2, IZ, I4K, I256, I16, NI = range(12)
+ALIAS = {"VF": (8192, 256), "Z2": (8720, 264), "D1": (8984, 264), "TE": (9248, 512), "LEN": (9760, 256)}
+S_P, S_M, S_K, S_0, S_J, S_E, S_C = 0, 8, 16, 48, 56, 72, 80
+CMS = (1.0, -64.0, -128.0, 32768.0, 32768.0, 128.0, 2.0, float(ZC), 4096.0, 256.0, 16.0, -1.0)
+IB, N64, N128, BI, BSU, I128, I2, IZ, I4K, I256, I16, NI = range(12)
 BIG, TOPB = 32768.0, 8192.0
 KM = 4112
-VS = (146, 128)
+VS = (128, 128)
+EN = 96
 VA = 96
-XS = 56
-SCOL = (3, 7, 11, 15)
+XS = 64
 
 
 def rank_program(g, core, T, topo):
@@ -167,8 +169,8 @@ def rank_program(g, core, T, topo):
         first = num(first)
         op("v", lambda: g.vector.tensor_tensor_scan(o[0], a[0], b[0], first[0], f1, f2), a[1] + b[1] + first[1], o[1])
 
-    def most(o, a):
-        op("v", lambda: g.vector.tensor_reduce(o[0], a[0], AxisListType.X, OP.max), a[1], o[1])
+    def most(o, a, f=OP.max):
+        op("v", lambda: g.vector.tensor_reduce(o[0], a[0], AxisListType.X, f), a[1], o[1])
 
     def act(o, a, f=AF.Copy, bias=None, scale=1.0):
         w, r = outs(o)
@@ -214,7 +216,6 @@ def rank_program(g, core, T, topo):
     dma(A("VI"), IO("ends"), "y")
     dma(A("HI"), IO("start", slice(0, 128), slice(0, 256)), "s")
     dma(A("XW0", 0, 4096), IO("x"), "y")
-    dma(A("W", 0, 2048), IO("w", slice(0, 128), slice(0, 2048)), "s")
 
     def pick(o, pattern, f, v, base, mul):
         op("g", lambda: g.affine_select(o[0], o[0], pattern, f, v, base, mul), o[1], o[1])
@@ -234,20 +235,24 @@ def rank_program(g, core, T, topo):
     pick(A("SHU"), [[-1, 128]], OP.not_equal, 1.0, -1, 1)
     iota(A("TB"), [[0, 2], [1, 128]], 1, 0)
     iota(A("TC"), [[128, 2], [0, 128]], 0, 0)
+    fill(A("VT"), 0.0)
+    act(A("WB", 0, 4096), A("VT"))
     fill(A("KT"), 0.0)
     ts(pi(1), pi(0), 15, None, OP.bitwise_and)
     cp(pc(0), pi(1))
     ts(pc(1), pc(0), 256.0, None, OP.mult)
     ts(A("AT1"), A("TA"), pc(1), None, OP.add)
     ts(pc(5), pc(0), 15.0, 8192.0, OP.is_equal, OP.mult)
-    fill(pc(6), 1.0)
+    for k, v in ((6, 1.0), (10, 4096.0), (11, 4.0), (12, -2.0), (13, -4 * BIG), (14, 160 - 63.5 / 128),
+                 (15, -160.0 * 128), (16, 160 - 31.5 / 64), (17, 2 * TOPB - 3)):
+        fill(pc(k), v)
     cp(A("PLO"), A("TB"))
     ts(A("PHI"), A("TC"), pc(1), None, OP.add)
     rows("KT", 1, 0, A("PLO"), "y")
     rows("KT", 1, 1, A("PHI"), "s")
 
     def constants():
-        for nm in ("SEL", "IDF"):
+        for nm in ("SEL", "IDF", "NID"):
             zero(A(nm))
         zero(sel(S_P), 4096)
         zero(sel(S_M), -4096)
@@ -255,30 +260,33 @@ def rank_program(g, core, T, topo):
             pick(sel(c), [[-16, 8]], OP.is_ge, 0.0, 0, 1)
             pick(sel(c), [[16, 8]], OP.is_ge, 0.0, 15, -1)
         pick(A("IDF"), [[-1, 128]], OP.not_equal, 1.0, 0, 1)
+        pick(A("NID"), [[-1, 128]], OP.not_equal, -1.0, 0, 1)
         for k in (IB, NI):
             zero(cm(k))
             pick(cm(k), [[-1, 128]], OP.not_equal, CMS[k], 0, 1)
-        for k, rs in enumerate(((0, 1, 3, 4), (0, 1), (3, 4))):
-            selector(sel(S_K + 8 * k), [(r, 1) for r in rs])
+        for k, terms in enumerate((((1, 1), (3, 1)), ((0, 1), (4, 1), (2, -1)), ((3, 1), (4, 1)), ((2, 1),))):
+            selector(sel(S_K + 8 * k), terms)
         for c in range(3):
             zero(A("XW0", c * ZC + 4096, c * ZC + ZC))
         zero(A("HM"))
-        cp(pc(7), pi(0))
-        ts(pc(7), pc(7), float(VA), None, OP.is_ge)
+        fill(A("SW"), 0.0)
         fill(A("ZB"), 0.0)
-        fill(A("VT"), 0.0)
+        act(A("WB", 4096, 6144), A("VT", 0, 2048), AF.Silu)
+        fill(A("WB", 6144, 8192), 0.0)
 
     def late_constants():
         iota(A("MSK"), [[1, 16]], 0, 0)
-        iota(A("CR", 0, 130), [[1, 130]], -64, 0)
-        iota(A("CR", 130, 194), [[1, 64]], -65, 0)
+        iota(A("CR"), [[1, 64]], 0, 0)
         iota(A("ROW", 0, 128), [[0, 128]], 1, 0)
-        iota(A("ROW", 128, 256), [[0, 128]], -112, 0)
-        iota(A("ROW", 256, 384), [[0, 128]], 10240, -10239)
+        iota(A("ROW", 128, 384, 2), [[0, 128]], -159, 159)
+        iota(A("ROW", 129, 384, 2), [[0, 128]], 10240, -10239)
+        zero(A("STEP"), -1)
+        iota(A("STEP", 0, 128 * NB_, 64), [[0, 2 * NB_]], -128, 0)
+        zero(A("SC"))
         zero(A("ROW", 384, 640), -1)
-        for nm, v in (("TRI", 1), ("DFV", 0), ("DFS", 0), ("S15", 0), ("IHF", 0)):
+        for nm, v in (("TRI", 1), ("DFS", 0), ("S15", 0), ("IHF", 0)):
             zero(A(nm), v)
-        zero(A("XW1", 11952, 3 * ZC))
+        zero(A("XW1", 10240, 3 * ZC))
         for k, v in enumerate(CMS):
             if k not in (IB, NI):
                 zero(cm(k))
@@ -289,17 +297,15 @@ def rank_program(g, core, T, topo):
         selector(sel(S_J), [(0, 1), (1, 1), (12, -1), (13, -1)])
         selector(sel(S_J + 8), [(4, 16), (5, 16), (8, 1), (9, 1), (12, -17), (13, -17)])
         selector(sel(S_E), [(0, 0.5), (1, 0.5)])
-        selector(sel(S_C), [(15, 0.5)])
+        selector(sel(S_C), [(15, 1)])
         selector(A("S15"), [(15, 0.5)])
         pick(A("TRI"), [[1, 128]], OP.is_ge, 0.0, -1, -1)
         blocks("TRI", 16)
-        for nm, terms in (("DFV", ((-1, -1.0), (0, 2.0), (1, -1.0))), ("DFS", ((0, 1.0), (1, -2.0), (2, 1.0)))):
-            for k, v in terms:
-                pick(A(nm), [[-1, 128]], OP.not_equal, v, -k, 1)
-            blocks(nm, 64)
-        pick(A("DFV"), [[-64, 2], [-200, 64]], OP.not_equal, 1.0, 0, 1)
-        zero(A("NG", 0, 512), -1)
-        zero(A("NG", 512, 768), -4)
+        for k, v in ((0, 1.0), (1, -2.0), (2, 1.0)):
+            pick(A("DFS"), [[-1, 128]], OP.not_equal, v, -k, 1)
+        blocks("DFS", 64)
+        zero(A("NG", 0, 256), -1)
+        zero(A("NG", 256, 512), -4)
 
     def late_constants_v():
         ts(pc(3), pc(0), 15.0, 256.0, OP.is_equal, OP.mult)
@@ -311,8 +317,6 @@ def rank_program(g, core, T, topo):
         ts(A("DEC", 16, 32), A("DEC", 0, 16), 1024.0, None, OP.mult)
         ts(A("DEC", 0, 16), A("DEC", 0, 16), 256.0, None, OP.mult)
         ts(A("MSK"), A("MSK"), pc(0), None, OP.is_equal)
-        fill(pc(8), TOPB)
-        fill(pc(9), 2 * TOPB - 3)
 
     def scatter_data():
         ts(A("KI"), zb(256), pc(0), 64.0, OP.add, OP.add)
@@ -333,7 +337,7 @@ def rank_program(g, core, T, topo):
                A(buf, off + 2048 * h + i, off + 2048 * h + 16 * (p1 - p0), 16),
                sel(s, k), start, stop if stop is True else (stop == "last" and i == 15))
 
-    def carry(outs_, cols, dec):
+    def carry(outs_, cols, dec, meanwhile):
         k = len(cols)
         mm(P(4, 0, 16 * k), zb(128), zb(16 * k), True, False)
         for j in range(k):
@@ -341,6 +345,7 @@ def rank_program(g, core, T, topo):
         for j, col in enumerate(cols):
             ts(A("RH", 16 * j, 16 * j + 16), A("MSK"), col, None, OP.mult)
         mm(P(4, 0, 16 * k), A("TRI"), A("RH", 0, 16 * k), False, True)
+        meanwhile()
         for j, o in enumerate(outs_):
             most(o, P(4, 16 * j, 16 * j + 16))
 
@@ -355,37 +360,48 @@ def rank_program(g, core, T, topo):
         hist[dst] = [{"reg": (0, 128, 1, 0, 256, 1), "w": True, "q": "remote", "sem": rs, "val": nb, "vc": {}, "n": 0,
                       "dma": True}]
 
-    def tables():
-        mm(P(4, 0, 1), A("SHU"), A("EB", 0, 1))
-        tt(P(3), P(6), A("AT1"), OP.subtract)
+    def tables(meanwhile):
+        DL, D = P(3, 256, 512), P(5, 256, 512)
+        mm(P(4, 0, 1), A("SHU"), cc(6))
+        tt(DL, P(6), A("AT1"), OP.subtract)
         ts(P(6, 256, 257), P(4, 0, 1), pc(5), None, OP.add)
         tt(A("TD"), P(6, 1, 257), A("AT1"), OP.subtract)
-        tt(P(5), P(3), A("TD"), OP.is_gt)
-        act(A("TC"), P(3), AF.Relu, pc(6), -1.0)
-        tt(P(5, 256, 512), P(5), A("TD"), OP.mult)
-        act(A("NB"), P(3), AF.Copy, None, BIG)
-        tt(P(5), P(5, 256, 512), A("TC"), OP.subtract)
-        cp(A("DHI"), P(5))
+        tt(P(5), DL, A("TD"), OP.is_gt)
+        act(A("HD"), DL, AF.Relu, pc(6), -1.0)
+        rows("KT", 1, 2, A("HD"), "s")
+        tt(D, P(5), A("TD"), OP.mult)
+        if meanwhile:
+            act(A("DLO"), D, AF.Identity, pc(14), 1.0 / 128)
+            act(A("DHI"), A("DLO"), AF.Identity, pc(15), 128.0)
+        else:
+            ts(A("DLO"), D, 1.0 / 128, 160 - 63.5 / 128, OP.mult, OP.add)
+            ts(A("DHI"), A("DLO"), -160.0, 128.0, OP.add, OP.mult)
         rows("KT", 1, 3, A("DHI"), "s")
-        tt(A("DLO"), P(5), A("DHI"), OP.subtract)
+        if meanwhile:
+            meanwhile()
+        tt(A("DLO"), D, A("DHI"), OP.subtract)
         rows("KT", 1, 4, A("DLO"), "y")
+        act(A("NB"), DL, AF.Copy, None, BIG)
+        act(A("TE", 0, 256), DL, AF.Identity, pc(11), 4.0)
+        act(A("EB"), P(6))
 
     def tables2():
-        tt(A("TC"), P(5), A("AT1"), OP.add)
-        cp(A("BLB"), A("TC"))
-        ts(P(3, 256, 512), P(3), 4.0, 4.0, OP.mult, OP.add)
-        tt(A("LEN"), P(3, 256, 512), A("NB"), OP.min)
+        tt(A("TC"), P(5, 256, 512), A("AT1"), OP.add)
+        ts(A("BLB"), A("TC"), 4095.0, None, OP.min)
+        tt(A("LEN"), A("TE", 0, 256), A("NB"), OP.min)
         for k in range(4):
             dma(A("HM", 66 * k, 66 * k + 64), A("NB", 0, 256, 1, 32 * k, 32 * k + 32))
 
     def weapon_sums(h):
-        exts("W", 0, h, h, 0, S_P)
-        ts(half("SW", h), P(h, 0, 128), pc(7), None, OP.mult)
+        part = lambda k: A("SW", 128 * k, 128 * k + 128, 1, VA, 128)
+        cp(part(2 * h), P(h, 0, 128, 1, VA, 128))
+        tt(part(2 * h + 1), P(h, 0, 128, 1, VA, 128), part(2 * h), OP.subtract)
 
-    cp(A("EB"), A("VI"))
+    cp(cc(6), A("VI", 0, 1))
     cp(P(6), A("VI"))
-    tables()
-    dma(A("W", 2048, 4096), IO("w", slice(0, 128), slice(2048, 4096)), "y")
+    tables(None)
+    for a, b in ((0, 16 * VA), (16 * VA, 2048 + 16 * XS), (2048 + 16 * XS, 4096)):
+        dma(A("W", a, b), IO("w", slice(0, 128), slice(a, b)))
     constants()
     tables2()
     late_constants()
@@ -401,7 +417,8 @@ def rank_program(g, core, T, topo):
             xg("VL", 8192, h, a, b)
 
         def asum(h):
-            mm(P(h, 0, 128), IDF, half("SW", h), True, False)
+            for k in range(2):
+                mm(P(h, 0, 128), cm(IB), half("SW", 2 * h + k), k == 0, False)
             exts("WB", 8192, h, h, 0, S_P, 8, False, False, 0, VA)
 
         def xb(h):
@@ -425,63 +442,69 @@ def rank_program(g, core, T, topo):
             act(A("XB", 2048 * h, 2048 * h + 2048), IND("KT", 0, 4112, "VL", 128 * h, 128 * h + 128))
 
         def ksum(h):
-            exts("XB", 0, h, 2 + h, 0, S_K, 24)
+            exts("XB", 0, h, 2 + h, 0, S_K, 32)
+
+        def second(o, h, turn, stop):
+            for k in range(2):
+                f = half("FS", 2 * h + k)
+                mm(o, *((f, cm(IB)) if turn else (cm(IB), f)), k == 0, stop and k == 1)
 
         def kids(h, s):
             act(A("FS", 256 * h, 256 * h + 256), P(2 + h))
-            mm(P(4 + h, 128, 256), A("FS", 256 * h, 256 * h + 128), IDF)
+            second(P(4 + h, 128, 256), h, True, True)
             if s == 1:
-                act(half("NOH", h), P(2 + h, 256, 384), AF.Relu, None, -1.0)
+                act(half("NOH", h), P(2 + h, 384, 512))
 
         def relu(h):
-            act(half("TA", h), P(h, 0, 128), AF.Relu)
+            act(half("TA", h), P(h, 0, 128), AF.Relu, pc(10), -1.0)
 
         def vb(h, s):
             cp(half("VB", h), P(4 + h, 128, 256))
-            f3 = A("FS", 256 * h + 128, 256 * h + 256)
-            mm(P(4 + h, 0, 128), *((f3, IDF) if s < 3 else (IDF, f3)), True, False)
+            second(P(4 + h, 0, 128), h, s < 3, False)
 
         def choose(h, s):
             tt(half("TB", h), P(2 + h, 256, 384), half("TA", h), OP.min)
-            mm(P(4 + h, 0, 128), *((half("TB", h), IDF) if s < 3 else (IDF, half("TB", h))), False, True)
+            mm(P(4 + h, 0, 128), *((half("TB", h), A("NID")) if s < 3 else (A("NID"), half("TB", h))), False, True)
 
         vl = lambda h: ts(half("VL", h), P(4 + h, 0, 128), 1.0, None, OP.add)
 
         def digits(h):
-            ts(half("AQ", h), P(4 + h, 0, 128), 1.0 / 64, 160 - 31.5 / 64, OP.mult, OP.add)
-            f3 = A("FS", 256 * h + 128, 256 * h + 256)
-            mms((P(6 + h), A("ROW", 0, 128), A("ROW", 128, 384)),
-                (P(6 + h, 128, 256), IDF, f3), (P(6 + h, 128, 256), IDF, half("TB", h)),
-                (P(6 + h, 128, 256), cm(P64), half("NOH", h)),
-                (P(6 + h, 0, 128), cm(IB), half("AQ", h)), (P(6 + h, 128, 256), cm(N64), half("AQ", h)))
-            for b in (h, 2 + h):
-                mm(P(b, 0, 264), zb(128), zb(264), True, False)
+            act(half("AQ", h), P(4 + h, 0, 128), AF.Identity, pc(16), 1.0 / 64)
+            act(half("VF", h), P(4 + h, 0, 128))
+            ev, od = P(6 + h, 0, 256, 2), P(6 + h, 1, 256, 2)
+            mms((P(6 + h), A("ROW", 0, 128), A("ROW", 128, 384)), (od, cm(N128), half("NOH", h)),
+                (ev, cm(IB), half("AQ", h)), (od, cm(N64), half("AQ", h)), (od, IDF, half("VF", h)))
+            mm(P(h, 0, 256), zb(128), zb(256), True, False)
 
-        slots = [0, 0]
+        def starts(h, q):
+            ts(A("WB", 0, 8192, 64), A("S12", 256 * h + 32 * q, 256 * h + 32 * q + 128), 0.0, None, OP.max)
 
-        def column(h, q, i):
-            c = 256 * h + 16 * q + i
-            s1, s2 = A("S12", c, c + 1), A("S12", c + 128, c + 129)
-            late = h == 1 and q >= 6
-            if i in SCOL:
-                o, b, last = 7800 + 130 * (slots[1] % 32), 2 + h - late, SCOL[-1]
-                slots[1] += 1
-                act(A(XO, o, o + 64), A("CR", 130, 194), AF.Relu, s1, -1.0)
-                act(A(XO, o + 64, o + 130), A("CR", 64, 130), AF.Relu, s2, -1.0)
-            else:
-                o, b, last = 130 * ((slots[0] + 30) % 60), h - late, max(k for k in range(16) if k not in SCOL)
-                slots[0] += 1
-                ts(A(XO, o, o + 130), A("CR", 0, 130), s1, s2, OP.max, OP.min)
-            mm(P(b, 66 * (q // 2), 66 * (q // 2) + 66, 1, 64 * (q % 2), 64 * (q % 2) + 64), A(XO, o, o + 64),
-               A(XO, o + 64, o + 130), False, i == last and (q >= 6 or (h == 1 and q >= 4)))
+        slot = lambda h, q: 2048 * ((8 * h + q + 2) % 5)
 
-        def sums(bv, bs, a, b):
-            act(A("SCS", a, b), P(bs, a, b))
-            cp(A("SCV", a, b), P(bv, a, b))
+        def ramps(h, q, a, b):
+            for c in range(2 * a, 2 * b):
+                k, o = 256 * h + 32 * q + c, slot(h, q) + 64 * c
+                act(A(XO, o, o + 64), A("CR"), AF.Relu, A("S12", k, k + 1), -1.0)
+
+        def products(h, q, a, b):
+            bank = h - (h == 1 and q >= 6)
+            for i in range(a, b):
+                o = slot(h, q) + 128 * i
+                mm(P(bank, 64 * (q // 2), 64 * (q // 2) + 64, 1, 64 * (q % 2), 64 * (q % 2) + 64),
+                   A(XO, o, o + 64), A(XO, o + 64, o + 128), False, i == 15 and (q >= 6 or (h == 1 and q >= 4)))
+
+        def group(h, q):
+            o, w = slot(h, q), 2048 * (q % 4)
+            scan(A(XO, o, o + 128 * NB_), A("STEP"), A("WB", w, w + 128 * NB_), OP.add, OP.max)
+            ramps(h, q, NB_, 16)
+            products(h, q, 0, 16)
+
+        def sums(bank, ks):
+            for k in ks:
+                act(A("SC", 66 * k, 66 * k + 64), P(bank, 64 * k, 64 * k + 64))
 
         def differences(bank, a, b, first):
-            mm(P(bank, a, b), A("DFS"), A("SCS", a, b), first, False)
-            mm(P(bank, a, b), A("DFV"), A("SCV", a, b), False, not first)
+            mm(P(bank, a, b), A("DFS"), A("SC", a, b), first, not first)
 
         def counts(bank, a, b):
             tt(A("D1", a, b - 2), P(bank, a, b - 2), A("Z2", a + 1, b - 1), OP.subtract)
@@ -490,31 +513,36 @@ def rank_program(g, core, T, topo):
 
         def marked(ks):
             for k in ks:
-                dma(A(XO, 0, 4096, 1, 32 * k, 32 * k + 32, 16), A("FL", 66 * k, 66 * k + 64), "y")
-            for k in ks:
-                dma(A("HB", 0, 256, 1, 32 * k, 32 * k + 32), A("FL", 66 * k, 66 * k + 64), "s" if k == 3 else "y")
+                dma(A(XO, 0, 4096, 1, 32 * k, 32 * k + 32, 16), A("FL", 66 * k, 66 * k + 64), "ys"[k % 2])
 
         for h in range(2):
             ts(half("VL", h), half("HI", h), 1.0, None, OP.add)
+        def first_kids():
+            act(A("XB", 0, 1024), IND("KT", 0, 4112, "VL", 0, 64))
+            cp(A("XB", 1024, 2048), IND("KT", 0, 4112, "VL", 64, 128))
+            ksum(0)
+
         if t == 0:
-            weapon_sums(0)
-        xr(0)
-        sub(0)
-        rr(0)
-        xa(0, 0, VA)
-        if t == 1:
-            tables2()
-        else:
             scatter_data()
+            late_constants_v()
+            first_kids()
+            xr(0)
+            kids(0, 0)
+            xa(0, 0, VA)
+            exts("W", 16 * VA, 0, 0, 0, S_P, 8, True, True, VA, 128)
+            sub(0)
+            rr(0)
+            weapon_sums(0)
+        else:
+            xr(0)
+            sub(0)
+            rr(0)
+            xa(0, 0, VA)
+            zero(A("WB", 0, 8192))
+            first_kids()
+            xa(1, 0, XS)
+            kids(0, 0)
         zero(A("WF", 0, 8192))
-        zero(A("WB", 0, 8192))
-        act(A("XB", 0, 1024), IND("KT", 0, 4112, "VL", 0, 64))
-        cp(A("XB", 1024, 2048), IND("KT", 0, 4112, "VL", 64, 128))
-        ksum(0)
-        xa(1, 0, XS)
-        kids(0, 0)
-        if t == 0:
-            weapon_sums(1)
         for k in range(8):
             h, s, s2 = k % 2, k // 2, (k + 1) // 2
             more = k < 7
@@ -526,99 +554,112 @@ def rank_program(g, core, T, topo):
                 sub(1 - h)
                 kid(1 - h)
             rsum(h)
+            if (t, k) == (0, 0):
+                exts("W", 16 * VA, 1, 1, 0, S_P, 8, True, True, VA, 128)
+            if k == 7:
+                ramps(0, 0, 0, 12)
+                products(0, 0, 0, 8)
             xb(h)
+            if (t, k) == (1, 0):
+                tables2()
             if more:
                 ksum(1 - h)
                 relu(h)
-                if k:
+                if k or t == 0:
                     xa(1 - h, 0, XS)
                 rr(1 - h)
                 choose(h, s)
                 kids(1 - h, s2)
                 xa(1 - h, XS, VA)
-            if t == 0 and k == 4:
-                late_constants_v()
+                if (t, k) == (0, 0):
+                    weapon_sums(1)
             if s < 3:
                 vl(h)
             if k == 6:
                 digits(0)
                 act(A("S12", 0, 256), P(6))
         relu(1)
+        ramps(0, 0, 12, 16)
+        products(0, 0, 8, 16)
         for h in range(2):
             for q in range(8):
-                for i in range(16):
-                    column(h, q, i)
-                if (h, q) == (0, 0):
+                if q % 4 == 0:
+                    starts(h, q)
+                if h or q:
+                    group(h, q)
+                if (h, q) == (0, 2):
                     choose(1, 3)
-                if (h, q) == (0, 1):
+                if (h, q) == (0, 4):
                     digits(1)
-                if (h, q) == (0, 3):
-                    cp(A("S12", 256, 512), P(7))
+                if (h, q) == (0, 5):
+                    act(A("S12", 256, 512), P(7))
+                if (h, q) == (1, 0):
+                    sums(0, range(4))
                 if (h, q) == (1, 1):
-                    sums(0, 2, 0, 264)
-                if (h, q) == (1, 2):
                     differences(4, 0, 198, True)
                     differences(5, 198, 264, True)
-                    for b in (0, 2):
-                        mm(P(b, 198, 264), zb(128), zb(66), True, False)
+                    mm(P(0, 192, 256), zb(128), zb(64), True, False)
                 if (h, q) == (1, 6):
-                    sums(1, 3, 0, 198)
+                    sums(1, range(3))
                     differences(4, 0, 198, False)
         if t == 0:
             dma(A("HI"), IO("start", slice(0, 128), slice(256, 512)), "y")
+        fill(A("WB", 0, 8192, 64), 0.0)
         act(A("Z2", 0, 198), P(4, 0, 198), AF.Copy, None, 2.0)
-        sums(0, 2, 198, 264)
+        sums(0, [3])
         differences(5, 198, 264, False)
         counts(4, 0, 198)
         marked(range(3))
         act(A("Z2", 198, 264), P(5, 198, 264), AF.Copy, None, 2.0)
         counts(5, 198, 264)
         marked([3])
-        for c in (1, 2):
-            ts(A(X, c * ZC, c * ZC + 4096), A(X, 0, 4096), -float(c), 0.0, OP.add, OP.max)
+        dma(A("HB"), A(XO, 0, 4096, 1, 0, 128, 16))
+        copy = lambda c, a, b: ts(A(X, c * ZC + a, c * ZC + b), A(X, a, b), -float(c), 0.0, OP.add, OP.max)
+        copy(1, 0, 4096)
+        act(A(X, 2 * ZC, 2 * ZC + 2048), A(X, 0, 2048), AF.Relu, pc(12))
 
         def shared(buf, off, win, h):
             for f, a in ((act, 128 * h), (cp, 128 * h + 64)):
                 f(A(buf, off + 16 * a, off + 16 * a + 1024), win(a, a + 64))
 
         mm(P(2), zb(128), zb(256), True, False)
+        mm(P(7), IDF, A("AM"), True, False)
         for h in (1, 0):
             shared("XB", 0, lambda a, b: IND(XO, 0, 4096, "BLB", a, b), h)
             exts("XB", 0, h, h, 0, S_0)
-            if h == 1:
-                mm(P(2, 0, 255), cm(BI), A("HB", 1, 256), False, False)
-                mm(P(2, 255, 256), cm(BSU), A("HB", 0, 1), False, False)
         act(half("M1", 1), P(1, 0, 128))
         ts(A("KP2"), A("HB"), -2.0, 2.0, OP.mult, OP.add)
         scan(A("K2", 1, 257), A("KP2"), zb(256), OP.add, OP.add)
         act(half("M1", 0), P(0, 0, 128))
-        ts(A("KP4"), A("HB"), -4.0, 4.0, OP.mult, OP.add)
+        ts(A("RH", 32, 48), zb(16), A("K2", 256, 257), None, OP.subtract)
+        mm(P(2, 0, 255), cm(BI), A("HB", 1, 256), False, False)
+        mm(P(2, 255, 256), cm(BSU), A("HB", 0, 1), False, False)
         for h in (1, 0):
             mm(P(2, 128 * h, 128 * h + 128), half("M1", h), cm(BI), False, h == 0)
+        mm(P(7), cm(I4K), A("HB"), False, True)
+        mm(P(6), cm(BI), A("HB"), True, False)
         tt(A("TC"), P(2), A("LEN"), OP.min)
-        ng4 = A("NG", 512, 768)
+        ng4 = A("NG", 256, 512)
         scan(A("TA"), ng4, A("TC"), OP.add, OP.max)
-        carry([P(3, 0, 1)], [A("TA", 255, 256)], 16)
-        mms((P(7), IDF, A("AM")), (P(7), cm(I4K), A("HB")))
+        carry([P(3, 0, 1)], [A("TA", 255, 256)], 16, lambda: ts(A("KP4"), A("HB"), -4.0, 4.0, OP.mult, OP.add))
+        mm(P(6), IDF, A("K2", 0, 256), False, False)
         scan(P(3, 1, 257), ng4, A("TC"), OP.add, OP.max, P(3, 0, 1))
         tt(A("KI"), P(3, 1, 257), A("KP4"), OP.min)
-        ts(P(5), P(3), 4.0, BIG, OP.is_gt, OP.mult)
+        act(P(5), P(3), AF.Relu, pc(13), BIG)
         act(A("INS"), P(3, 1, 257), AF.Sign)
         scan(A("I4", 1, 257), A("KI"), zb(256), OP.add, OP.add)
-        mms((P(4, 32, 33), A("TRI"), A("I4", 256, 257)), (P(4, 32, 33), A("TRI"), A("K2", 256, 257)))
-        mm(P(4, 33, 34), A("TRI"), A("K2", 256, 257))
-        mm(P(4, 34, 35), A("TRI"), A("I4", 256, 257))
+        mms((P(0, 0, 1), A("TRI"), A("K2", 256, 257)), (P(0, 0, 1), A("TRI"), A("I4", 256, 257)))
+        mm(P(0, 2, 3), A("TRI"), A("I4", 256, 257))
         tt(A("TA"), P(5), A("I4", 0, 256), OP.subtract)
         scan(A("TB"), A("TA"), A("TA"), OP.min, OP.min, BIG)
-        cp(A("CC", 0, 3), P(4, 32, 35))
-        ts(cc(3), A("TB", 255, 256), -1.0, cc(2), OP.mult, OP.add)
-        ts(A("RH", 0, 16), A("MSK"), cc(3), None, OP.mult)
-        mm(P(4, 0, 16), A("TRI"), A("RH", 0, 16))
+        ts(A("RH", 0, 16), A("MSK"), A("TB", 255, 256), None, OP.mult)
+        ts(A("RH", 16, 32), A("MSK"), P(0, 2, 3), -1.0, OP.mult, OP.mult)
+        mms(*[(P(4, 0, 16), A("TRI"), A("RH", o, o + 16)) for o in (32, 0, 16)])
         tt(A("TOP"), P(5), A("TC"), OP.is_lt)
-        mms((P(6), IDF, A("K2", 0, 256)), (P(6), cm(BI), A("HB")), (P(6), cm(IB), A("TOP")))
+        mm(P(6), cm(IB), A("TOP"), False, True)
         mms((P(2), IDF, A("EB")), (P(2), cm(I4K), A("INS")))
-        most(cc(3), P(4, 0, 16))
-        ts(cc(3), cc(3), -1.0, cc(1), OP.mult, OP.subtract)
+        cp(cc(0), P(0, 0, 1))
+        most(cc(3), P(4, 0, 16), OP.min)
         ts(A("TD"), A("TB"), cc(0), cc(3), OP.subtract, OP.min)
         tt(A("TA"), P(6), A("TD"), OP.subtract)
         tt(A("TA"), P(7), A("TA"), OP.min)
@@ -641,25 +682,29 @@ def rank_program(g, core, T, topo):
         tt(A("PLO"), P(3), A("PHI"), OP.subtract)
         rows(XO, KM, 1, A("PLO"), "y")
         ts(A("ELB"), P(2), -1.0, None, OP.add)
-        ends = lambda h: act(A("XB", 2048 * h, 2048 * h + 2048), IND(XO, KM, KM + 8192, "ELB", 128 * h, 128 * h + 128))
+        copy(2, 2048, 4096)
+        ends = lambda f, a, b: f(A("XB", 16 * a, 16 * b), IND(XO, KM, KM + 8192, "ELB", a, b))
 
         one = A("ROW", 0, 128, 1, 0, 1)
-        mms((P(7), one, A("ROW", 384, 640, 1, 0, 1)), *[(P(7), cm(I128), A(nm, 1, 512, 2)) for nm in ("FA", "FB")])
-        mms(*[(P(0), cm(I128), A(nm, o, 512, 2)) for nm in ("FA", "FB") for o in (0, 1)])
+        mm(P(7), one, A("ROW", 384, 640, 1, 0, 1), True, False)
+        for nm in ("FA", "FB"):
+            mm(P(7), cm(I128), A(nm, 1, 512, 2), False, nm == "FB")
+            for o in (0, 1):
+                mm(P(0), cm(I128), A(nm, o, 512, 2), (nm, o) == ("FA", 0), (nm, o) == ("FB", 1))
         ng1 = A("NG", 0, 256)
-        ends(0)
         scan(A("TE", 256, 512), ng1, P(7), OP.add, OP.max)
         scan(A("TE", 0, 256), ng1, P(0), OP.add, OP.max)
-        carry([cc(4), cc(5)], [A("TE", 255, 256), A("TE", 511, 512)], 0)
+        carry([cc(4), cc(5)], [A("TE", 255, 256), A("TE", 511, 512)], 0, lambda: None)
         scan(P(1), ng1, P(0), OP.add, OP.max, cc(4))
         scan(A("TB"), ng1, P(7), OP.add, OP.max, cc(5))
+        act(P(3), A("TB"), AF.Identity, pc(17), -2.0)
+        ends(act, 0, EN)
         ts(A("M1"), P(1), TOPB, None, OP.is_lt)
         mm(P(2), cm(I2), A("M1"), True, False)
         tt(A("TA"), P(1), A("TB"), OP.subtract)
         tt(A("TC"), P(1), A("TA"), OP.add)
         ts(A("M2"), A("TC"), TOPB, None, OP.is_lt)
         mm(P(2), cm(I2), A("M2"), False, True)
-        ts(P(3), A("TB"), -2.0, 2 * TOPB - 3, OP.mult, OP.add)
         tt(A("CS"), P(2), A("TA"), OP.mult)
         tt(P(1), P(3), A("CS"), OP.min)
         tt(A("TC"), A("Q2"), P(1), OP.subtract)
@@ -671,10 +716,12 @@ def rank_program(g, core, T, topo):
         mm(P(0), cm(IZ), A("M1"), False, False)
         mm(P(0), cm(IZ), A("M2"), False, False)
         mm(P(4, 0, 32), zb(128), zb(32), True, False)
+        for r in range(16):
+            mms(*[(P(7, 256 + r, 384, 16, 0, 16), A(nm, r, 256, 16), sel(S_C)) for nm in ("M1", "M2")])
         exts("WB", 8192, 0, 5, 0, S_J, 16)
-        ends(1)
-        cp(A("FA", 256, 512), P(6))
-        cp(A("C2"), P(2))
+        act(A("FA", 256, 512), P(6))
+        ends(act, EN, 192)
+        ends(cp, 192, 224)
         weights = ((1, 0, IB), (1, 1, I16), (0, 0, I256), (0, 1, IB), (0, 2, IZ))
         for h in (1, 0):
             if h == 0:
@@ -684,8 +731,7 @@ def rank_program(g, core, T, topo):
             for k, (l, d, wt) in enumerate(weights[:4]):
                 mm(P(0, 256 * l + 128 * h, 256 * l + 128 * h + 128), A("FA", 256 * h + 128 * d, 256 * h + 128 * d + 128),
                    cm(wt), False, h == 0 and k == 3)
-        for r in range(16):
-            mm(P(7, 256 + r, 384, 16, 0, 16), A("C2", r, 256, 16), sel(S_C))
+        ends(cp, 224, 256)
         lists = [(A("VB"), P(0, 256, 512)), (A("VL"), P(0))]
         cp(*lists[t])
         cp(A("FB", 0, 384, 1, 0, 16), P(7, 0, 384, 1, 0, 16))
@@ -702,55 +748,66 @@ def rank_program(g, core, T, topo):
 
         def last_places():
             cp(A("L15"), P(4, 0, 32))
+            if t == 1:
+                cp(A("TX"), XI("L15", 0, 16))
+                send("TX", LX, "xs%d" % t, "xr%d" % t)
             cp(A("TZ"), SZ("L15", 16, 32))
             mms((P(4, 0, 16), zb(128), zb(16)),
                 *[(P(4, 8 * h, 8 * h + 8), half("CS", h), A("S15")) for h in range(2)],
                 *[(P(4, 8 * h, 8 * h + 8), half("TZ", h), sel(S_E)) for h in range(2)])
-            cp(A("TX"), XI("L15", 0, 16))
+            if t == 0:
+                cp(A("TX"), XI("L15", 0, 16))
+            else:
+                xi(cp, 0, 16)
             ts(A(ES), P(4, 0, 16), 4096.0, None, OP.min)
             send(ES, RE, "es%d" % t, "er%d" % t)
-            send("TX", LX, "xs%d" % t, "xr%d" % t)
+            if t == 0:
+                send("TX", LX, "xs%d" % t, "xr%d" % t)
             mm(P(7), A("IHF"), A("CS"), True, False)
 
-        def new_ends():
-            cp(A("TA", 15, 256, 16), A(RE))
-            for h in range(2):
-                mm(P(7, 128 * h, 128 * h + 128), half("TA", h), IDF, False, h == 1)
+        def new_ends(h, last):
+            cp(A("TA", 128 * h + 15, 128 * h + 128, 16), A(RE, 8 * h, 8 * h + 8))
+            mm(P(7, 128 * h, 128 * h + 128), half("TA", h), IDF, False, last)
 
         if t == 0:
-            sz(act, 120, 256)
+            sz(act, 112, 256)
             last_places()
-            sz(cp, 0, 120)
+            sz(cp, 0, 112)
             for h in (1, 0):
                 exts("WB", 12288, h, 5, 128 * h, S_E)
-            xi(act, 128, 256)
-            xi(cp, 0, 96)
+            xi(act, 192, 256)
+            xi(cp, 0, 64)
             act(A("TA"), P(5))
-            new_ends()
-            xi(cp, 96, 128)
+            xi(act, 136, 192)
+            for h in range(2):
+                new_ends(h, h == 1)
+            xi(cp, 64, 104)
+            ts(cc(6), P(7, 0, 1), pc(3), None, OP.min)
             ts(P(6), P(7), pc(3), None, OP.min)
-            act(A("EB"), P(6))
-            tables()
-            for i in range(15):
-                order(act if i % 3 == 0 else cp, i)
-            cp(A(XO, 3840, 4096), A(LX))
+            xi(act, 104, 136)
+            tables(lambda: [order(cp, i) for i in range(5)])
+            for i in range(5, 15):
+                order(act if i % 4 == 0 else cp, i)
+            act(A(XO, 3840, 4096), A(LX))
         else:
-            xi(act, 112, 256)
+            xi(act, 108, 256)
             last_places()
-            xi(cp, 0, 112)
+            xi(cp, 16, 108)
             sz(act, 128, 256)
             exts("WB", 12288, 1, 6, 128, S_E)
+            keep = lambda o, a: op("g", lambda: g.affine_select(o[0], a[0], [[0, 256]], OP.is_ge, 0.0, 0, 0), a[1], o[1])
             for i in range(15):
-                order(cp, i)
+                order(keep if i in (3, 11) else cp, i)
                 if i in (3, 7, 11, 14):
                     dma(IO("y", slice(0, 128), slice(i // 4 * 1024, 256 * i + 256)), A(XO, i // 4 * 1024, 256 * i + 256))
             dma(IO("y", slice(0, 128), slice(3840, 4096)), A(LX))
-            sz(act, 64, 128)
-            sz(cp, 0, 64)
+            sz(act, 84, 128)
+            sz(cp, 0, 84)
             exts("WB", 12288, 0, 5, 0, S_E)
             act(half("TA", 1), P(6, 128, 256))
+            new_ends(1, False)
             cp(half("TA", 0), P(5, 0, 128))
-            new_ends()
+            new_ends(0, True)
             ts(A("EB"), P(7), pc(3), None, OP.min)
             dma(IO("ye"), A("EB"), "s")
 

from concourse.mybir import dt, AluOpType, AxisListType, ActivationFunctionType

OP = AluOpType
AF = ActivationFunctionType
F32, BF, I32, U16 = "float32", "bfloat16", "int32", "uint16"
NDMA = 110
ZC = 4128
NB_ = 13
SCRATCH = {
    "XW0": ("sbuf", [128, 3 * ZC], BF), "XW1": ("sbuf", [128, 3 * ZC], BF),
    "XB": ("sbuf", [128, 4096], BF), "W": ("sbuf", [128, 4096], BF), "KT": ("sbuf", [128, 4112], BF),
    "WB": ("sbuf", [128, 16384], BF), "WF": ("sbuf", [128, 16384], F32),
    "VT": ("sbuf", [128, 4096], BF), "ST": ("sbuf", [128, 4096], F32),
    "ZB": ("sbuf", [128, 264], BF), "CR": ("sbuf", [128, 64], BF), "CM": ("sbuf", [128, 12 * 128], BF),
    "IDF": ("sbuf", [128, 128], F32), "SHU": ("sbuf", [128, 128], F32), "TRI": ("sbuf", [128, 128], F32),
    "IHF": ("sbuf", [128, 128], F32), "NID": ("sbuf", [128, 128], F32), "DFS": ("sbuf", [128, 128], F32),
    "MSK": ("sbuf", [128, 16], F32), "DEC": ("sbuf", [128, 32], F32), "S15": ("sbuf", [128, 8], F32),
    "PI": ("sbuf", [128, 8], I32), "PC": ("sbuf", [128, 24], F32), "SEL": ("sbuf", [128, 88], BF),
    "ROW": ("sbuf", [2, 640], BF), "NG": ("sbuf", [128, 512], BF), "SW": ("sbuf", [128, 512], BF),
    "STEP": ("sbuf", [128, 128 * NB_], BF), "FS": ("sbuf", [128, 512], BF), "HD": ("sbuf", [128, 256], BF),
    "SC": ("sbuf", [128, 264], F32),
    "AT1": ("sbuf", [128, 256], F32), "Q2": ("sbuf", [128, 256], F32),
    "AM": ("sbuf", [128, 256], F32), "EB": ("sbuf", [128, 256], F32),
    "DHI": ("sbuf", [128, 256], BF), "DLO": ("sbuf", [128, 256], BF),
    "PHI": ("sbuf", [128, 256], BF), "PLO": ("sbuf", [128, 256], BF),
    "NB": ("sbuf", [128, 256], BF), "HM": ("sbuf", [128, 264], BF), "FL": ("sbuf", [128, 264], BF),
    "BLB": ("sbuf", [128, 256], U16), "ELB": ("sbuf", [128, 256], U16), "VL": ("sbuf", [128, 256], U16),
    "VB": ("sbuf", [128, 256], U16), "QL": ("sbuf", [128, 256], U16), "L15": ("sbuf", [128, 32], U16),
    "TA": ("sbuf", [128, 256], F32), "TB": ("sbuf", [128, 256], F32), "TC": ("sbuf", [128, 256], F32),
    "TD": ("sbuf", [128, 256], F32), "VI": ("sbuf", [128, 256], I32), "HI": ("sbuf", [128, 256], I32),
    "AQ": ("sbuf", [128, 256], BF), "NOH": ("sbuf", [128, 256], BF), "S12": ("sbuf", [128, 512], BF),
    "HB": ("sbuf", [128, 256], BF), "KP2": ("sbuf", [128, 256], BF), "KP4": ("sbuf", [128, 256], BF),
    "KI": ("sbuf", [128, 256], BF), "INS": ("sbuf", [128, 256], BF), "TOP": ("sbuf", [128, 256], BF),
    "K2": ("sbuf", [128, 260], F32), "I4": ("sbuf", [128, 260], F32), "CC": ("sbuf", [128, 16], F32),
    "RH": ("sbuf", [128, 48], F32), "FA": ("sbuf", [128, 512], BF), "FB": ("sbuf", [128, 512], BF),
    "M1": ("sbuf", [128, 256], BF), "M2": ("sbuf", [128, 256], BF), "C2": ("sbuf", [128, 256], BF),
    "CS": ("sbuf", [128, 256], F32), "TX": ("sbuf", [128, 256], BF), "TZ": ("sbuf", [128, 256], BF),
    "LX0": ("sbuf", [128, 256], BF), "LX1": ("sbuf", [128, 256], BF),
    "ES0": ("sbuf", [128, 16], F32), "ES1": ("sbuf", [128, 16], F32),
    "RE0": ("sbuf", [128, 16], F32), "RE1": ("sbuf", [128, 16], F32),
}
for _k in range(8):
    SCRATCH["P%d" % _k] = ("psum", [128, 512], F32)
SEMAPHORES = ["qv", "qs", "qt", "qg"] + ["d%d" % k for k in range(NDMA)]
SEMAPHORES += ["%s%d" % (a, k) for a in ("xs", "xr", "es", "er") for k in range(2)]

ALIAS = {"VF": (8192, 256), "Z2": (8720, 264), "D1": (8984, 264), "TE": (9248, 512), "LEN": (9760, 256)}
S_P, S_M, S_K, S_0, S_J, S_E, S_C = 0, 8, 16, 48, 56, 72, 80
CMS = (1.0, -64.0, -128.0, 32768.0, 32768.0, 128.0, 2.0, float(ZC), 4096.0, 256.0, 16.0, -1.0)
IB, N64, N128, BI, BSU, I128, I2, IZ, I4K, I256, I16, NI = range(12)
BIG, TOPB = 32768.0, 8192.0
KM = 4112
VS = (128, 128)
EN = 96
VA = 96
XS = 64


def rank_program(g, core, T, topo):
    rank = T.rank_of(core)
    if rank is None:
        return
    n = len(T.cores)
    nxt, prv = T.cores[(rank + 1) % n], T.cores[(rank - 1) % n]
    eng = {"v": g.vector, "s": g.scalar, "t": g.tensor, "g": g, "y": g.sync}
    hist, known, cnt, total = {}, {q: {} for q in eng}, {q: 0 for q in eng}, {}
    nd, serial = [0], [0]

    def over(a, b):
        if a[0] >= b[1] or b[0] >= a[1] or a[3] >= b[4] or b[3] >= a[4]:
            return False
        m = min(a[2], b[2])
        return a[0] % m == b[0] % m

    def inside(a, b):
        if not (b[0] <= a[0] and a[1] <= b[1] and b[3] <= a[3] and a[4] <= b[4] and b[5] == 1):
            return False
        return a[2] % b[2] == 0 and a[0] % b[2] == b[0] % b[2]

    def is_psum(name):
        return name[0] == "P" and name[1:].isdigit()

    def op(q, call, R, W, dma=False, remote=None):
        deps = []
        for w, lst in ((False, R), (True, W)):
            for name, reg in lst:
                ps = is_psum(name)
                for r in hist.get(name, []):
                    if ps and r["q"] != q:
                        deps.append(r)
                    elif over(r["reg"], reg) and (w or r["w"]) and not (ps and q == "t"):
                        deps.append(r)
        deps.sort(key=lambda r: -r["n"])
        kn = known[q]
        for r in deps:
            if kn.get(r["sem"], 0) >= r["val"]:
                continue
            eng[q].wait_ge(T.sem[r["sem"]], r["val"])
            for k, v in r["vc"].items():
                if kn.get(k, 0) < v:
                    kn[k] = v
            kn[r["sem"]] = r["val"]
        ins = call()
        serial[0] += 1
        if remote is not None:
            sem, val = remote
        elif dma:
            sem, val = "d%d" % nd[0], 16
            nd[0] += 1
            ins.then_inc(T.sem[sem], 16)
        else:
            cnt[q] += 1
            sem, val = "q" + q, cnt[q]
            ins.then_inc(T.sem[sem], 1)
        total[sem] = val
        vc = dict(kn)
        for w, lst in ((False, R), (True, W)):
            for name, reg in lst:
                h = hist.setdefault(name, [])
                if is_psum(name):
                    h[:] = [r for r in h if r["q"] == q and q != "t" and not (inside(r["reg"], reg) and (w or not r["w"]))]
                elif w:
                    h[:] = [r for r in h if not inside(r["reg"], reg)]
                elif not dma and remote is None:
                    h[:] = [r for r in h if r["w"] or r["dma"] or r["q"] != q or not inside(r["reg"], reg)]
                h.append({"reg": reg, "w": w, "q": q, "sem": sem, "val": val, "vc": vc, "n": serial[0],
                          "dma": dma or remote is not None})

    def A(name, c0=0, c1=None, cs=1, p0=0, p1=None, ps=1):
        if name in ALIAS:
            o, k = ALIAS[name]
            return A("WF", o + c0, o + (k if c1 is None else c1), cs, p0, p1, ps)
        shape = T[name].shape
        c1 = shape[1] if c1 is None else c1
        p1 = shape[0] if p1 is None else p1
        sc = slice(c0, c1) if cs == 1 else slice(c0, c1, cs)
        sp = slice(p0, p1) if ps == 1 else slice(p0, p1, ps)
        return T[name][sp, sc], [(name, (p0, p1, ps, c0, c1, cs))]

    def IND(name, c0, c1, lst, l0, l1):
        return (T[name][:, c0:c1].indirect(T[lst][:, l0:l1]),
                [(name, (0, 128, 1, c0, c1, 1)), (lst, (0, 128, 1, l0, l1, 1))])

    def outs(o):
        return o[1][:1], o[1][1:]

    def num(x):
        return x if isinstance(x, tuple) else (x, [])

    def tt(o, a, b, f):
        op("v", lambda: g.vector.tensor_tensor(o[0], a[0], b[0], f), a[1] + b[1], o[1])

    def ts(o, a, s1, s2, f1, f2=None):
        s1, s2 = num(s1), num(s2)
        r = a[1] + s1[1] + s2[1]
        if f2 is None:
            op("v", lambda: g.vector.tensor_scalar(o[0], a[0], s1[0], None, f1), r, o[1])
        else:
            op("v", lambda: g.vector.tensor_scalar(o[0], a[0], s1[0], s2[0], f1, f2), r, o[1])

    def cp(o, a):
        w, r = outs(o)
        op("v", lambda: g.vector.tensor_copy(o[0], a[0]), a[1] + r, w)

    def fill(o, val):
        op("v", lambda: g.vector.memset(o[0], val), [], o[1])

    def scan(o, a, b, f1, f2, first=0.0):
        first = num(first)
        op("v", lambda: g.vector.tensor_tensor_scan(o[0], a[0], b[0], first[0], f1, f2), a[1] + b[1] + first[1], o[1])

    def most(o, a, f=OP.max):
        op("v", lambda: g.vector.tensor_reduce(o[0], a[0], AxisListType.X, f), a[1], o[1])

    def act(o, a, f=AF.Copy, bias=None, scale=1.0):
        w, r = outs(o)
        if bias is None and scale == 1.0:
            op("s", lambda: g.scalar.activation(o[0], a[0], f), a[1] + r, w)
        elif bias is None:
            op("s", lambda: g.scalar.activation(o[0], a[0], f, scale=scale), a[1] + r, w)
        else:
            op("s", lambda: g.scalar.activation(o[0], a[0], f, bias=bias[0], scale=scale), a[1] + r + bias[1], w)

    def mm(o, l, r, start=True, stop=True):
        op("t", lambda: g.tensor.matmul(o[0], l[0], r[0], start, stop), l[1] + r[1], o[1])

    def mms(*terms):
        for k, (o, l, r) in enumerate(terms):
            mm(o, l, r, k == 0, k == len(terms) - 1)

    def dma(o, a, q="y"):
        op(q, lambda: eng[q].dma_start(o[0], a[0]), a[1], o[1], dma=True)

    def iota(o, pattern, base, mul, loose=True):
        if loose:
            op("g", lambda: g.iota(o[0], pattern, base, mul, allow_small_or_imprecise_dtypes=True), [], o[1])
        else:
            op("g", lambda: g.iota(o[0], pattern, base, mul), [], o[1])

    def IO(name, *idx):
        return (T[name][idx] if idx else T[name][:]), []

    sel = lambda c, k=8: A("SEL", c, c + k)
    cm = lambda k: A("CM", 128 * k, 128 * k + 128)
    zb = lambda k: A("ZB", 0, k)
    pi = lambda k: A("PI", k, k + 1)
    pc = lambda k: A("PC", k, k + 1)
    cc = lambda k: A("CC", k, k + 1)
    half = lambda nm, h, o=0: A(nm, o + 128 * h, o + 128 * h + 128)
    P = lambda b, c0=0, c1=256, cs=1, p0=0, p1=128: A("P%d" % b, c0, c1, cs, p0, p1)
    IDF = A("IDF")

    def rows(name, off, r, src, q="y"):
        dma(A(name, off, off + 4096, 1, r, 128, 16), src, q)

    dma(A("VI"), IO("ends"), "y")
    dma(A("HI"), IO("start", slice(0, 128), slice(0, 256)), "s")
    dma(A("XW0", 0, 4096), IO("x"), "y")

    def pick(o, pattern, f, v, base, mul):
        op("g", lambda: g.affine_select(o[0], o[0], pattern, f, v, base, mul), o[1], o[1])

    def selector(o, terms):
        for r, v in terms:
            pick(o, [[-16, 8]], OP.not_equal, float(v), -r, 1)

    def blocks(nm, k):
        pick(A(nm), [[-k, 128 // k], [0, k]], OP.is_ge, 0.0, 0, 1)
        pick(A(nm), [[k, 128 // k], [0, k]], OP.is_ge, 0.0, k - 1, -1)

    zero = lambda o, v=0: iota(o, [[0, o[1][0][1][4] - o[1][0][1][3]]], v, 0)
    iota(A("PI", 0, 1), [[0, 1]], 0, 1, False)
    iota(A("TA"), [[1, 256]], 1, 0)
    zero(A("SHU"))
    pick(A("SHU"), [[-1, 128]], OP.not_equal, 1.0, -1, 1)
    iota(A("TB"), [[0, 2], [1, 128]], 1, 0)
    iota(A("TC"), [[128, 2], [0, 128]], 0, 0)
    fill(A("VT"), 0.0)
    act(A("WB", 0, 4096), A("VT"))
    fill(A("KT"), 0.0)
    ts(pi(1), pi(0), 15, None, OP.bitwise_and)
    cp(pc(0), pi(1))
    ts(pc(1), pc(0), 256.0, None, OP.mult)
    ts(A("AT1"), A("TA"), pc(1), None, OP.add)
    ts(pc(5), pc(0), 15.0, 8192.0, OP.is_equal, OP.mult)
    for k, v in ((6, 1.0), (10, 4096.0), (11, 4.0), (12, -2.0), (13, -4 * BIG), (14, 160 - 63.5 / 128),
                 (15, -160.0 * 128), (16, 160 - 31.5 / 64), (17, 2 * TOPB - 3)):
        fill(pc(k), v)
    cp(A("PLO"), A("TB"))
    ts(A("PHI"), A("TC"), pc(1), None, OP.add)
    rows("KT", 1, 0, A("PLO"), "y")
    rows("KT", 1, 1, A("PHI"), "s")

    def constants():
        for nm in ("SEL", "IDF", "NID"):
            zero(A(nm))
        zero(sel(S_P), 4096)
        zero(sel(S_M), -4096)
        for c in (S_P, S_M):
            pick(sel(c), [[-16, 8]], OP.is_ge, 0.0, 0, 1)
            pick(sel(c), [[16, 8]], OP.is_ge, 0.0, 15, -1)
        pick(A("IDF"), [[-1, 128]], OP.not_equal, 1.0, 0, 1)
        pick(A("NID"), [[-1, 128]], OP.not_equal, -1.0, 0, 1)
        for k in (IB, NI):
            zero(cm(k))
            pick(cm(k), [[-1, 128]], OP.not_equal, CMS[k], 0, 1)
        for k, terms in enumerate((((1, 1), (3, 1)), ((0, 1), (4, 1), (2, -1)), ((3, 1), (4, 1)), ((2, 1),))):
            selector(sel(S_K + 8 * k), terms)
        for c in range(3):
            zero(A("XW0", c * ZC + 4096, c * ZC + ZC))
        zero(A("HM"))
        fill(A("SW"), 0.0)
        fill(A("ZB"), 0.0)
        act(A("WB", 4096, 6144), A("VT", 0, 2048), AF.Silu)
        fill(A("WB", 6144, 8192), 0.0)

    def late_constants():
        iota(A("MSK"), [[1, 16]], 0, 0)
        iota(A("CR"), [[1, 64]], 0, 0)
        iota(A("ROW", 0, 128), [[0, 128]], 1, 0)
        iota(A("ROW", 128, 384, 2), [[0, 128]], -159, 159)
        iota(A("ROW", 129, 384, 2), [[0, 128]], 10240, -10239)
        zero(A("STEP"), -1)
        iota(A("STEP", 0, 128 * NB_, 64), [[0, 2 * NB_]], -128, 0)
        zero(A("SC"))
        zero(A("ROW", 384, 640), -1)
        for nm, v in (("TRI", 1), ("DFS", 0), ("S15", 0), ("IHF", 0)):
            zero(A(nm), v)
        zero(A("XW1", 10240, 3 * ZC))
        for k, v in enumerate(CMS):
            if k not in (IB, NI):
                zero(cm(k))
                pick(cm(k), [[-1, 128]], OP.not_equal, v, -1 if k == BSU else 0, 1)
        pick(A("IHF"), [[-1, 128]], OP.not_equal, 0.5, 0, 1)
        pick(A("IHF"), [[0, 8], [-1, 16]], OP.not_equal, 0.0, 15, 0)
        selector(sel(S_0), [(0, 1)])
        selector(sel(S_J), [(0, 1), (1, 1), (12, -1), (13, -1)])
        selector(sel(S_J + 8), [(4, 16), (5, 16), (8, 1), (9, 1), (12, -17), (13, -17)])
        selector(sel(S_E), [(0, 0.5), (1, 0.5)])
        selector(sel(S_C), [(15, 1)])
        selector(A("S15"), [(15, 0.5)])
        pick(A("TRI"), [[1, 128]], OP.is_ge, 0.0, -1, -1)
        blocks("TRI", 16)
        for k, v in ((0, 1.0), (1, -2.0), (2, 1.0)):
            pick(A("DFS"), [[-1, 128]], OP.not_equal, v, -k, 1)
        blocks("DFS", 64)
        zero(A("NG", 0, 256), -1)
        zero(A("NG", 256, 512), -4)

    def late_constants_v():
        ts(pc(3), pc(0), 15.0, 256.0, OP.is_equal, OP.mult)
        ts(pc(3), pc(3), 3840.0, None, OP.add)
        ts(pc(4), pc(0), -1.0, 1.0, OP.mult, OP.add)
        ts(A("Q2"), A("AT1"), -1.0, 2.0, OP.add, OP.mult)
        ts(A("AM"), A("AT1"), 8191.0, None, OP.add)
        ts(A("DEC", 0, 16), A("MSK"), pc(4), 0.0, OP.add, OP.min)
        ts(A("DEC", 16, 32), A("DEC", 0, 16), 1024.0, None, OP.mult)
        ts(A("DEC", 0, 16), A("DEC", 0, 16), 256.0, None, OP.mult)
        ts(A("MSK"), A("MSK"), pc(0), None, OP.is_equal)

    def scatter_data():
        ts(A("KI"), zb(256), pc(0), 64.0, OP.add, OP.add)
        ts(A("K2", 4, 260), zb(256), pc(0), 64.0, OP.add, OP.add)
        fill(A("K2", 0, 1), 0.0)
        fill(A("I4", 0, 1), 0.0)
        zero(A("ST"))
        for nm, tiles in (("VT", (A("M1"), A("M2"), A("C2"))), ("ST", (A("CS"), A("TE", 0, 256), A("TE", 256, 512)))):
            for r, pattern, src in zip((0, 8, 12), ([[0, 16], [1, 16]], [[1, 16], [0, 16]], [[0, 256]]), tiles):
                iota(src, pattern, 64, 0)
                rows(nm, 0, r, src)
        rows("VT", 0, 4, A("KI"), "g")
        rows("ST", 0, 4, A("K2", 4, 260))

    def exts(buf, off, h, b, c0, s, k=8, start=True, stop=True, p0=0, p1=128):
        for i in range(16):
            mm(P(b, c0 + i, c0 + i + (k - 1) * 16 + 1, 16, p0, p1),
               A(buf, off + 2048 * h + i, off + 2048 * h + 16 * (p1 - p0), 16),
               sel(s, k), start, stop if stop is True else (stop == "last" and i == 15))

    def carry(outs_, cols, dec, meanwhile):
        k = len(cols)
        mm(P(4, 0, 16 * k), zb(128), zb(16 * k), True, False)
        for j in range(k):
            mm(P(4, 16 * j, 16 * j + 16), IDF, A("DEC", dec, dec + 16), False, False)
        for j, col in enumerate(cols):
            ts(A("RH", 16 * j, 16 * j + 16), A("MSK"), col, None, OP.mult)
        mm(P(4, 0, 16 * k), A("TRI"), A("RH", 0, 16 * k), False, True)
        meanwhile()
        for j, o in enumerate(outs_):
            most(o, P(4, 16 * j, 16 * j + 16))

    rid, pid, _se = topo.addr(nxt)
    mask = topo.mask(core, nxt)
    ne, nb = len(topo.engines(core, nxt)), len(topo.engines(prv, core))

    def send(src, dst, ss, rs):
        sa, da = A(src), T[dst][:]
        op("g", lambda: g.remote_dma(da, sa[0], T.sem[rs], T.sem[ss], pid, rid, mask), sa[1], [], remote=(ss, ne))
        total[rs] = nb
        hist[dst] = [{"reg": (0, 128, 1, 0, 256, 1), "w": True, "q": "remote", "sem": rs, "val": nb, "vc": {}, "n": 0,
                      "dma": True}]

    def tables(meanwhile):
        DL, D = P(3, 256, 512), P(5, 256, 512)
        mm(P(4, 0, 1), A("SHU"), cc(6))
        tt(DL, P(6), A("AT1"), OP.subtract)
        ts(P(6, 256, 257), P(4, 0, 1), pc(5), None, OP.add)
        tt(A("TD"), P(6, 1, 257), A("AT1"), OP.subtract)
        tt(P(5), DL, A("TD"), OP.is_gt)
        act(A("HD"), DL, AF.Relu, pc(6), -1.0)
        rows("KT", 1, 2, A("HD"), "s")
        tt(D, P(5), A("TD"), OP.mult)
        if meanwhile:
            act(A("DLO"), D, AF.Identity, pc(14), 1.0 / 128)
            act(A("DHI"), A("DLO"), AF.Identity, pc(15), 128.0)
        else:
            ts(A("DLO"), D, 1.0 / 128, 160 - 63.5 / 128, OP.mult, OP.add)
            ts(A("DHI"), A("DLO"), -160.0, 128.0, OP.add, OP.mult)
        rows("KT", 1, 3, A("DHI"), "s")
        if meanwhile:
            meanwhile()
        tt(A("DLO"), D, A("DHI"), OP.subtract)
        rows("KT", 1, 4, A("DLO"), "y")
        act(A("NB"), DL, AF.Copy, None, BIG)
        act(A("TE", 0, 256), DL, AF.Identity, pc(11), 4.0)
        act(A("EB"), P(6))

    def tables2():
        tt(A("TC"), P(5, 256, 512), A("AT1"), OP.add)
        ts(A("BLB"), A("TC"), 4095.0, None, OP.min)
        tt(A("LEN"), A("TE", 0, 256), A("NB"), OP.min)
        for k in range(4):
            dma(A("HM", 66 * k, 66 * k + 64), A("NB", 0, 256, 1, 32 * k, 32 * k + 32))

    def weapon_sums(h):
        part = lambda k: A("SW", 128 * k, 128 * k + 128, 1, VA, 128)
        cp(part(2 * h), P(h, 0, 128, 1, VA, 128))
        tt(part(2 * h + 1), P(h, 0, 128, 1, VA, 128), part(2 * h), OP.subtract)

    cp(cc(6), A("VI", 0, 1))
    cp(P(6), A("VI"))
    tables(None)
    for a, b in ((0, 16 * VA), (16 * VA, 2048 + 16 * XS), (2048 + 16 * XS, 4096)):
        dma(A("W", a, b), IO("w", slice(0, 128), slice(a, b)))
    constants()
    tables2()
    late_constants()

    for t in range(2):
        X, XO = "XW%d" % t, "XW%d" % (1 - t)

        def xg(lst, off, h, a, b):
            tt(A("WB", off + 2048 * h + 16 * a, off + 2048 * h + 16 * b), IND(X, 0, 4112, lst, 128 * h + a, 128 * h + b),
               A("W", 2048 * h + 16 * a, 2048 * h + 16 * b), OP.min)

        def xa(h, a, b):
            xg("VL", 8192, h, a, b)

        def asum(h):
            for k in range(2):
                mm(P(h, 0, 128), cm(IB), half("SW", 2 * h + k), k == 0, False)
            exts("WB", 8192, h, h, 0, S_P, 8, False, False, 0, VA)

        def xb(h):
            xg("VB", 12288, h, 0, 128)
            exts("WB", 12288, h, h, 0, S_M, 8, False, "last")

        def xr(h):
            act(A(XO, 512 * h, 512 * h + 512), IND(X, 0, 4112, "VL", 128 * h + VA, 128 * h + 128))

        def sub(h):
            mms((P(6 + h, 0, 512), cm(IB), A("W", 2048 * h + 16 * VA, 2048 * h + 2048)),
                (P(6 + h, 0, 512), cm(NI), A(XO, 512 * h, 512 * h + 512)))

        def rr(h):
            act(A(XO, 1024 + 2048 * h, 1536 + 2048 * h), P(6 + h, 0, 512), AF.Relu)

        def rsum(h):
            exts(XO, 1024, h, h, 0, S_M, 8, False, False, VA, 128)

        def kid(h):
            act(A("XB", 2048 * h, 2048 * h + 2048), IND("KT", 0, 4112, "VL", 128 * h, 128 * h + 128))

        def ksum(h):
            exts("XB", 0, h, 2 + h, 0, S_K, 32)

        def second(o, h, turn, stop):
            for k in range(2):
                f = half("FS", 2 * h + k)
                mm(o, *((f, cm(IB)) if turn else (cm(IB), f)), k == 0, stop and k == 1)

        def kids(h, s):
            act(A("FS", 256 * h, 256 * h + 256), P(2 + h))
            second(P(4 + h, 128, 256), h, True, True)
            if s == 1:
                act(half("NOH", h), P(2 + h, 384, 512))

        def relu(h):
            act(half("TA", h), P(h, 0, 128), AF.Relu, pc(10), -1.0)

        def vb(h, s):
            cp(half("VB", h), P(4 + h, 128, 256))
            second(P(4 + h, 0, 128), h, s < 3, False)

        def choose(h, s):
            tt(half("TB", h), P(2 + h, 256, 384), half("TA", h), OP.min)
            mm(P(4 + h, 0, 128), *((half("TB", h), A("NID")) if s < 3 else (A("NID"), half("TB", h))), False, True)

        vl = lambda h: ts(half("VL", h), P(4 + h, 0, 128), 1.0, None, OP.add)

        def digits(h):
            act(half("AQ", h), P(4 + h, 0, 128), AF.Identity, pc(16), 1.0 / 64)
            act(half("VF", h), P(4 + h, 0, 128))
            ev, od = P(6 + h, 0, 256, 2), P(6 + h, 1, 256, 2)
            mms((P(6 + h), A("ROW", 0, 128), A("ROW", 128, 384)), (od, cm(N128), half("NOH", h)),
                (ev, cm(IB), half("AQ", h)), (od, cm(N64), half("AQ", h)), (od, IDF, half("VF", h)))
            mm(P(h, 0, 256), zb(128), zb(256), True, False)

        def starts(h, q):
            ts(A("WB", 0, 8192, 64), A("S12", 256 * h + 32 * q, 256 * h + 32 * q + 128), 0.0, None, OP.max)

        slot = lambda h, q: 2048 * ((8 * h + q + 2) % 5)

        def ramps(h, q, a, b):
            for c in range(2 * a, 2 * b):
                k, o = 256 * h + 32 * q + c, slot(h, q) + 64 * c
                act(A(XO, o, o + 64), A("CR"), AF.Relu, A("S12", k, k + 1), -1.0)

        def products(h, q, a, b):
            bank = h - (h == 1 and q >= 6)
            for i in range(a, b):
                o = slot(h, q) + 128 * i
                mm(P(bank, 64 * (q // 2), 64 * (q // 2) + 64, 1, 64 * (q % 2), 64 * (q % 2) + 64),
                   A(XO, o, o + 64), A(XO, o + 64, o + 128), False, i == 15 and (q >= 6 or (h == 1 and q >= 4)))

        def group(h, q):
            o, w = slot(h, q), 2048 * (q % 4)
            scan(A(XO, o, o + 128 * NB_), A("STEP"), A("WB", w, w + 128 * NB_), OP.add, OP.max)
            ramps(h, q, NB_, 16)
            products(h, q, 0, 16)

        def sums(bank, ks):
            for k in ks:
                act(A("SC", 66 * k, 66 * k + 64), P(bank, 64 * k, 64 * k + 64))

        def differences(bank, a, b, first):
            mm(P(bank, a, b), A("DFS"), A("SC", a, b), first, not first)

        def counts(bank, a, b):
            tt(A("D1", a, b - 2), P(bank, a, b - 2), A("Z2", a + 1, b - 1), OP.subtract)
            tt(P(6, a, b - 2), P(bank, a + 2, b), A("D1", a, b - 2), OP.add)
            tt(A("FL", a, b - 2), P(6, a, b - 2), A("HM", a, b - 2), OP.is_gt)

        def marked(ks):
            for k in ks:
                dma(A(XO, 0, 4096, 1, 32 * k, 32 * k + 32, 16), A("FL", 66 * k, 66 * k + 64), "ys"[k % 2])

        for h in range(2):
            ts(half("VL", h), half("HI", h), 1.0, None, OP.add)
        def first_kids():
            act(A("XB", 0, 1024), IND("KT", 0, 4112, "VL", 0, 64))
            cp(A("XB", 1024, 2048), IND("KT", 0, 4112, "VL", 64, 128))
            ksum(0)

        if t == 0:
            scatter_data()
            late_constants_v()
            first_kids()
            xr(0)
            kids(0, 0)
            xa(0, 0, VA)
            exts("W", 16 * VA, 0, 0, 0, S_P, 8, True, True, VA, 128)
            sub(0)
            rr(0)
            weapon_sums(0)
        else:
            xr(0)
            sub(0)
            rr(0)
            xa(0, 0, VA)
            zero(A("WB", 0, 8192))
            first_kids()
            xa(1, 0, XS)
            kids(0, 0)
        zero(A("WF", 0, 8192))
        for k in range(8):
            h, s, s2 = k % 2, k // 2, (k + 1) // 2
            more = k < 7
            if more:
                xr(1 - h)
            vb(h, s)
            asum(h)
            if more:
                sub(1 - h)
                kid(1 - h)
            rsum(h)
            if (t, k) == (0, 0):
                exts("W", 16 * VA, 1, 1, 0, S_P, 8, True, True, VA, 128)
            if k == 7:
                ramps(0, 0, 0, 12)
                products(0, 0, 0, 8)
            xb(h)
            if (t, k) == (1, 0):
                tables2()
            if more:
                ksum(1 - h)
                relu(h)
                if k or t == 0:
                    xa(1 - h, 0, XS)
                rr(1 - h)
                choose(h, s)
                kids(1 - h, s2)
                xa(1 - h, XS, VA)
                if (t, k) == (0, 0):
                    weapon_sums(1)
            if s < 3:
                vl(h)
            if k == 6:
                digits(0)
                act(A("S12", 0, 256), P(6))
        relu(1)
        ramps(0, 0, 12, 16)
        products(0, 0, 8, 16)
        for h in range(2):
            for q in range(8):
                if q % 4 == 0:
                    starts(h, q)
                if h or q:
                    group(h, q)
                if (h, q) == (0, 2):
                    choose(1, 3)
                if (h, q) == (0, 4):
                    digits(1)
                if (h, q) == (0, 5):
                    act(A("S12", 256, 512), P(7))
                if (h, q) == (1, 0):
                    sums(0, range(4))
                if (h, q) == (1, 1):
                    differences(4, 0, 198, True)
                    differences(5, 198, 264, True)
                    mm(P(0, 192, 256), zb(128), zb(64), True, False)
                if (h, q) == (1, 6):
                    sums(1, range(3))
                    differences(4, 0, 198, False)
        if t == 0:
            dma(A("HI"), IO("start", slice(0, 128), slice(256, 512)), "y")
        fill(A("WB", 0, 8192, 64), 0.0)
        act(A("Z2", 0, 198), P(4, 0, 198), AF.Copy, None, 2.0)
        sums(0, [3])
        differences(5, 198, 264, False)
        counts(4, 0, 198)
        marked(range(3))
        act(A("Z2", 198, 264), P(5, 198, 264), AF.Copy, None, 2.0)
        counts(5, 198, 264)
        marked([3])
        dma(A("HB"), A(XO, 0, 4096, 1, 0, 128, 16))
        copy = lambda c, a, b: ts(A(X, c * ZC + a, c * ZC + b), A(X, a, b), -float(c), 0.0, OP.add, OP.max)
        copy(1, 0, 4096)
        act(A(X, 2 * ZC, 2 * ZC + 2048), A(X, 0, 2048), AF.Relu, pc(12))

        def shared(buf, off, win, h):
            for f, a in ((act, 128 * h), (cp, 128 * h + 64)):
                f(A(buf, off + 16 * a, off + 16 * a + 1024), win(a, a + 64))

        mm(P(2), zb(128), zb(256), True, False)
        mm(P(7), IDF, A("AM"), True, False)
        for h in (1, 0):
            shared("XB", 0, lambda a, b: IND(XO, 0, 4096, "BLB", a, b), h)
            exts("XB", 0, h, h, 0, S_0)
        act(half("M1", 1), P(1, 0, 128))
        ts(A("KP2"), A("HB"), -2.0, 2.0, OP.mult, OP.add)
        scan(A("K2", 1, 257), A("KP2"), zb(256), OP.add, OP.add)
        act(half("M1", 0), P(0, 0, 128))
        ts(A("RH", 32, 48), zb(16), A("K2", 256, 257), None, OP.subtract)
        mm(P(2, 0, 255), cm(BI), A("HB", 1, 256), False, False)
        mm(P(2, 255, 256), cm(BSU), A("HB", 0, 1), False, False)
        for h in (1, 0):
            mm(P(2, 128 * h, 128 * h + 128), half("M1", h), cm(BI), False, h == 0)
        mm(P(7), cm(I4K), A("HB"), False, True)
        mm(P(6), cm(BI), A("HB"), True, False)
        tt(A("TC"), P(2), A("LEN"), OP.min)
        ng4 = A("NG", 256, 512)
        scan(A("TA"), ng4, A("TC"), OP.add, OP.max)
        carry([P(3, 0, 1)], [A("TA", 255, 256)], 16, lambda: ts(A("KP4"), A("HB"), -4.0, 4.0, OP.mult, OP.add))
        mm(P(6), IDF, A("K2", 0, 256), False, False)
        scan(P(3, 1, 257), ng4, A("TC"), OP.add, OP.max, P(3, 0, 1))
        tt(A("KI"), P(3, 1, 257), A("KP4"), OP.min)
        act(P(5), P(3), AF.Relu, pc(13), BIG)
        act(A("INS"), P(3, 1, 257), AF.Sign)
        scan(A("I4", 1, 257), A("KI"), zb(256), OP.add, OP.add)
        mms((P(0, 0, 1), A("TRI"), A("K2", 256, 257)), (P(0, 0, 1), A("TRI"), A("I4", 256, 257)))
        mm(P(0, 2, 3), A("TRI"), A("I4", 256, 257))
        tt(A("TA"), P(5), A("I4", 0, 256), OP.subtract)
        scan(A("TB"), A("TA"), A("TA"), OP.min, OP.min, BIG)
        ts(A("RH", 0, 16), A("MSK"), A("TB", 255, 256), None, OP.mult)
        ts(A("RH", 16, 32), A("MSK"), P(0, 2, 3), -1.0, OP.mult, OP.mult)
        mms(*[(P(4, 0, 16), A("TRI"), A("RH", o, o + 16)) for o in (32, 0, 16)])
        tt(A("TOP"), P(5), A("TC"), OP.is_lt)
        mm(P(6), cm(IB), A("TOP"), False, True)
        mms((P(2), IDF, A("EB")), (P(2), cm(I4K), A("INS")))
        cp(cc(0), P(0, 0, 1))
        most(cc(3), P(4, 0, 16), OP.min)
        ts(A("TD"), A("TB"), cc(0), cc(3), OP.subtract, OP.min)
        tt(A("TA"), P(6), A("TD"), OP.subtract)
        tt(A("TA"), P(7), A("TA"), OP.min)
        cp(A("QL"), A("TA"))
        act(IND("WF", 0, 16384, "QL", VS[t], 256), A("ST", 16 * VS[t], 4096), AF.Silu)
        cp(IND("WB", 0, 16384, "QL", 0, VS[t]), A("VT", 0, 16 * VS[t]))
        dma(A("FB"), A("WF", 0, 8192, 1, 12, 128, 16), "g")
        dma(A("FA"), A("WB", 0, 8192, 1, 12, 128, 16), "y")
        src = A("WF", 0, 8192, 1, 0, 128, 4)
        dma(A("WB", 0, 8192, 1, 1, 128, 4), (src[0], src[1] + A("FA")[1]), "g")
        tt(P(5), A("K2", 1, 257), A("TD"), OP.subtract)
        act(A("DHI"), P(5))
        tt(P(3), A("K2", 1, 257), A("I4", 1, 257), OP.add)
        rows(XO, KM + 4096, 0, A("DHI"), "s")
        ts(P(3), P(3), cc(0), None, OP.add)
        act(A("PHI"), P(3))
        tt(A("DLO"), P(5), A("DHI"), OP.subtract)
        rows(XO, KM + 4096, 1, A("DLO"), "y")
        rows(XO, KM, 0, A("PHI"), "s")
        tt(A("PLO"), P(3), A("PHI"), OP.subtract)
        rows(XO, KM, 1, A("PLO"), "y")
        ts(A("ELB"), P(2), -1.0, None, OP.add)
        copy(2, 2048, 4096)
        ends = lambda f, a, b: f(A("XB", 16 * a, 16 * b), IND(XO, KM, KM + 8192, "ELB", a, b))

        one = A("ROW", 0, 128, 1, 0, 1)
        mm(P(7), one, A("ROW", 384, 640, 1, 0, 1), True, False)
        for nm in ("FA", "FB"):
            mm(P(7), cm(I128), A(nm, 1, 512, 2), False, nm == "FB")
            for o in (0, 1):
                mm(P(0), cm(I128), A(nm, o, 512, 2), (nm, o) == ("FA", 0), (nm, o) == ("FB", 1))
        ng1 = A("NG", 0, 256)
        scan(A("TE", 256, 512), ng1, P(7), OP.add, OP.max)
        scan(A("TE", 0, 256), ng1, P(0), OP.add, OP.max)
        carry([cc(4), cc(5)], [A("TE", 255, 256), A("TE", 511, 512)], 0, lambda: None)
        scan(P(1), ng1, P(0), OP.add, OP.max, cc(4))
        scan(A("TB"), ng1, P(7), OP.add, OP.max, cc(5))
        act(P(3), A("TB"), AF.Identity, pc(17), -2.0)
        ends(act, 0, EN)
        ts(A("M1"), P(1), TOPB, None, OP.is_lt)
        mm(P(2), cm(I2), A("M1"), True, False)
        tt(A("TA"), P(1), A("TB"), OP.subtract)
        tt(A("TC"), P(1), A("TA"), OP.add)
        ts(A("M2"), A("TC"), TOPB, None, OP.is_lt)
        mm(P(2), cm(I2), A("M2"), False, True)
        tt(A("CS"), P(2), A("TA"), OP.mult)
        tt(P(1), P(3), A("CS"), OP.min)
        tt(A("TC"), A("Q2"), P(1), OP.subtract)
        cp(A("QL"), A("TC"))
        shared("WB", 8192, lambda a, b: IND("WB", 0, 8192, "QL", a, b), 1)
        exts("WB", 8192, 1, 6, 0, S_J, 16)
        shared("WB", 8192, lambda a, b: IND("WB", 0, 8192, "QL", a, b), 0)
        mm(P(0, 0, 512), zb(128), A("NG", 0, 512), True, False)
        mm(P(0), cm(IZ), A("M1"), False, False)
        mm(P(0), cm(IZ), A("M2"), False, False)
        mm(P(4, 0, 32), zb(128), zb(32), True, False)
        for r in range(16):
            mms(*[(P(7, 256 + r, 384, 16, 0, 16), A(nm, r, 256, 16), sel(S_C)) for nm in ("M1", "M2")])
        exts("WB", 8192, 0, 5, 0, S_J, 16)
        act(A("FA", 256, 512), P(6))
        ends(act, EN, 192)
        ends(cp, 192, 224)
        weights = ((1, 0, IB), (1, 1, I16), (0, 0, I256), (0, 1, IB), (0, 2, IZ))
        for h in (1, 0):
            if h == 0:
                for r in range(16):
                    mm(P(7, r, 256, 16, 0, 16), A("WB", 8192 + 16 * r + 15, 12288, 256), sel(S_J, 16))
                cp(A("FA", 0, 256), P(5))
            for k, (l, d, wt) in enumerate(weights[:4]):
                mm(P(0, 256 * l + 128 * h, 256 * l + 128 * h + 128), A("FA", 256 * h + 128 * d, 256 * h + 128 * d + 128),
                   cm(wt), False, h == 0 and k == 3)
        ends(cp, 224, 256)
        lists = [(A("VB"), P(0, 256, 512)), (A("VL"), P(0))]
        cp(*lists[t])
        cp(A("FB", 0, 384, 1, 0, 16), P(7, 0, 384, 1, 0, 16))
        for k, (l, d, wt) in enumerate(weights):
            mm(P(4, 16 * l, 16 * l + 16), A("FB", 128 * d, 128 * d + 128, 1, 0, 16),
               A("CM", 128 * wt, 128 * wt + 16, 1, 0, 16), False, k == 4)
        cp(*lists[1 - t])
        LX, ES, RE = ["%s%d" % (nm, t) for nm in ("LX", "ES", "RE")]
        SZ = lambda lst, a, b: IND("XB", 0, 4096, lst, a, b)
        XI = lambda lst, a, b: IND(X, 0, 3 * ZC, lst, a, b)
        sz = lambda f, a, b: f(A("WB", 12288 + 16 * a, 12288 + 16 * b), SZ("VB", a, b))
        xi = lambda f, a, b: f(A(XO, KM + 16 * a, KM + 16 * b), XI("VL", a, b))
        order = lambda f, i: f(A(XO, 256 * i, 256 * i + 256), A(XO, KM + i, KM + 4096, 16))

        def last_places():
            cp(A("L15"), P(4, 0, 32))
            if t == 1:
                cp(A("TX"), XI("L15", 0, 16))
                send("TX", LX, "xs%d" % t, "xr%d" % t)
            cp(A("TZ"), SZ("L15", 16, 32))
            mms((P(4, 0, 16), zb(128), zb(16)),
                *[(P(4, 8 * h, 8 * h + 8), half("CS", h), A("S15")) for h in range(2)],
                *[(P(4, 8 * h, 8 * h + 8), half("TZ", h), sel(S_E)) for h in range(2)])
            if t == 0:
                cp(A("TX"), XI("L15", 0, 16))
            else:
                xi(cp, 0, 16)
            ts(A(ES), P(4, 0, 16), 4096.0, None, OP.min)
            send(ES, RE, "es%d" % t, "er%d" % t)
            if t == 0:
                send("TX", LX, "xs%d" % t, "xr%d" % t)
            mm(P(7), A("IHF"), A("CS"), True, False)

        def new_ends(h, last):
            cp(A("TA", 128 * h + 15, 128 * h + 128, 16), A(RE, 8 * h, 8 * h + 8))
            mm(P(7, 128 * h, 128 * h + 128), half("TA", h), IDF, False, last)

        if t == 0:
            sz(act, 112, 256)
            last_places()
            sz(cp, 0, 112)
            for h in (1, 0):
                exts("WB", 12288, h, 5, 128 * h, S_E)
            xi(act, 192, 256)
            xi(cp, 0, 64)
            act(A("TA"), P(5))
            xi(act, 136, 192)
            for h in range(2):
                new_ends(h, h == 1)
            xi(cp, 64, 104)
            ts(cc(6), P(7, 0, 1), pc(3), None, OP.min)
            ts(P(6), P(7), pc(3), None, OP.min)
            xi(act, 104, 136)
            tables(lambda: [order(cp, i) for i in range(5)])
            for i in range(5, 15):
                order(act if i % 4 == 0 else cp, i)
            act(A(XO, 3840, 4096), A(LX))
        else:
            xi(act, 108, 256)
            last_places()
            xi(cp, 16, 108)
            sz(act, 128, 256)
            exts("WB", 12288, 1, 6, 128, S_E)
            keep = lambda o, a: op("g", lambda: g.affine_select(o[0], a[0], [[0, 256]], OP.is_ge, 0.0, 0, 0), a[1], o[1])
            for i in range(15):
                order(keep if i in (3, 11) else cp, i)
                if i in (3, 7, 11, 14):
                    dma(IO("y", slice(0, 128), slice(i // 4 * 1024, 256 * i + 256)), A(XO, i // 4 * 1024, 256 * i + 256))
            dma(IO("y", slice(0, 128), slice(3840, 4096)), A(LX))
            sz(act, 84, 128)
            sz(cp, 0, 84)
            exts("WB", 12288, 0, 5, 0, S_E)
            act(half("TA", 1), P(6, 128, 256))
            new_ends(1, False)
            cp(half("TA", 0), P(5, 0, 128))
            new_ends(0, True)
            ts(A("EB"), P(7), pc(3), None, OP.min)
            dma(IO("ye"), A("EB"), "s")

    for s in sorted(total):
        if known["g"].get(s, 0) < total[s]:
            g.wait_ge(T.sem[s], total[s])
